import numpy as np, ml_dtypes
CORES = [23,119,17,113]
N = 4
import mx_ref
BF = ml_dtypes.bfloat16
def gentries(a):
    return np.ascontiguousarray(a.reshape(8, 16, -1).transpose(0, 2, 1)).reshape(8, -1)
def gtable(e):
    e = np.asarray(e); return np.ascontiguousarray(e.reshape(8, -1, 16).transpose(0, 2, 1)).reshape(128, -1).astype(np.int32)
def gcols(t, e):
    v = np.concatenate([t.reshape(8, 16, -1, 4), np.zeros((8, 16, 1, 4), BF)], axis=2)
    return np.ascontiguousarray(np.stack([v[g][:, e[g]] for g in range(8)])).reshape(128, -1)
def tile(rs):
    return np.stack(rs, axis=2).reshape(128, -1).astype(BF)
def pick(q, e):
    c = np.concatenate([q[0].reshape(128, -1, 4), np.zeros((128, 1, 4), np.uint8)], axis=1); s = np.concatenate([q[1], np.ones((16, 1), np.uint8)], axis=1)
    return (np.ascontiguousarray(c[:, e].reshape(128, -1)), np.ascontiguousarray(s[:, e]))
def join(*qs):
    return (np.concatenate([q[0] for q in qs], axis=1), np.concatenate([q[1] for q in qs], axis=1))
def put(q, e, v):
    c, s = q[0].reshape(128, -1, 4).copy(), q[1].copy(); c[:, e] = v[0].reshape(128, -1, 4); s[:, e] = v[1]
    return (c.reshape(128, -1), s)
def pk(c, s):
    return (np.ascontiguousarray(c), mx_ref.live(s))
def emit(q):
    return q[0], q[1]
def packed(v, rng):
    q = [mx_ref.quantize(np.ascontiguousarray(v[r])) for r in range(N)]
    return np.stack([a for a, b in q]), np.stack([mx_ref.plane(b, rng) for a, b in q])
def values_of_codes():
    e, c = np.zeros((128, 128, 4), np.float32), np.zeros((128, 2, 4), np.uint8)
    e[np.arange(128), np.arange(128), 0] = 1
    c[:127, :, 0] = np.arange(256).reshape(2, 128).T[:127]
    return mx_ref.matmul(mx_ref.quantize(e.reshape(128, 512).astype(BF)), (c.reshape(128, 8), np.full((16, 2), 127, np.uint8))).T.reshape(-1).astype(np.float64)
CODE_VALUE, SCALE_VALUE = values_of_codes(), 2.0 ** (np.arange(256) - 127.0)
def decode(q):
    return (CODE_VALUE[q[0]].reshape(16, 8, -1, 4) * SCALE_VALUE[q[1]][:, None, :, None] + 0.0).reshape(128, -1).astype(np.float32)
def f(rng, *shape):
    return mx_ref.flush((rng.standard_normal(shape, dtype=np.float32) * np.exp2(rng.integers(-2, 3, shape[:-1] + (1,)))).astype(BF))
def wide(rng, *shape, cols=0):
    v = rng.standard_normal(shape, dtype=np.float32) * np.exp2(rng.integers(-12, 13, shape)).astype(np.float32)
    if cols: v *= np.repeat(np.exp2(rng.integers(-cols, cols + 1, shape[:-2] + (1, shape[-1] // 4))) * (rng.random(shape[:-2] + (1, shape[-1] // 4)) > 0.0625), 4, axis=-1).astype(np.float32)
    return mx_ref.flush(v.astype(BF))
C, F = 448, 336
MASK = [1, 2, 3]
def numbers_of(rng):
    return {"x": np.array(f(rng, N, 128, 4 * C)), "u": np.array(f(rng, N, 128, 512)), "v": np.array(f(rng, N, 128, 512))}
def stored(k, n):
    return {"dl": np.stack([gtable(k[r]) for r in range(N)]), "nl": np.stack([gtable(n[r]) for r in range(N)])}
def lists(rng):
    e = np.tile(np.arange(C), (N, 8, 1))
    k, e = rng.permuted(e, axis=2), rng.permuted(e, axis=2)
    n = np.empty_like(e)
    np.put_along_axis(n, e, e.reshape(N, 8, -1, 2)[..., ::-1].reshape(N, 8, C), axis=2)
    return k, n
def layers(rng, still=[]):
    w = np.array(f(rng, N, 128, 2048)).reshape(N, 8, 16, 4, 8, 16, 4)
    for i in still:
        w[:, :, i] = 0
        w[:, :, :, :, :, i] = 0
    return w
def weights(rng, w):
    c, s = packed(np.ascontiguousarray(w).reshape(N, 128, 2048), rng)
    return {"wc": c, "ws": s}
def setup_inputs(rng):
    return {**numbers_of(rng), **stored(*lists(rng)), **weights(rng, layers(rng))}
def setup_inputs_ties(rng):
    d = numbers_of(rng)
    k, n = lists(rng)
    o, h = rng.permutation(N), rng.permutation(8)
    i = np.arange(N)
    e = (i ^ (i >> 1) ^ (i >> 2)) % 2
    s = rng.integers(0, 4, (N, 8, C))
    s[o[1]] += 1
    s[:, h[:3]] = 1
    for g in h[:2]:
        for r in np.flatnonzero(e):
            k[r, g] = n[r, g]
            s[r, g] = np.where(np.arange(C) < n[r, g], 2, 0)
    c = np.ones((N, 8), np.float32)
    c[o[0]] = 0
    c[o[1]] = -1
    c[:, h[:3]] = 1
    x = d["x"].reshape(N, 8, 16, C, 4)
    x[:, :, 0] = 0
    x[:, :, 0, :, 0] = s.astype(np.float32).astype(BF)
    a = np.exp2(rng.integers(-3, 4, (1, 8, 1)).astype(np.float32))
    x[:, :, 8:] = 0
    x[:, :, 8, :, 0] = (-1.125 * a).astype(BF)
    x[:, :, 10, :, 0] = (-0.0703125 * a).astype(BF)
    u = d["u"].reshape(N, 128, 128, 4)
    u[:, :, ::16] = 0
    w = layers(rng, [0])
    w[:, :, :, :, :, 8:] = 0
    for g in range(8):
        u[:, 16 * g, 16 * g, 0] = c[:, g].astype(BF)
        w[:, g, 8, 0, g, 8, 0] = -28.0
        for b in range(4): w[:, g, 10, b, g, 9, 0] = -2.0 ** (b - 5)
    return {"x": x.reshape(N, 128, 4 * C), "u": u.reshape(N, 128, 512), "v": d["v"], **stored(k, n), **weights(rng, w)}
def setup_inputs_near(rng):
    d = numbers_of(rng)
    k, n = lists(rng)
    x = d["x"].astype(np.float32).reshape(N, 8, 16, C, 4)
    x[:, :, 0] = 0
    x[:, :, 8:] = 0
    u = d["u"].reshape(N, 128, 128, 4)
    u[:, :, ::16] = 0
    w = layers(rng, [0, 8, 9, 10, 11, 12, 13, 14, 15])
    at = [0, C - 1, int(rng.integers(C)), int(rng.integers(C))]
    for i, g in enumerate(rng.permutation(8)):
        h, c = 16 * g, 1.0 if i < 2 else 2.0 ** -30
        s = rng.integers(0, 16, (N, C))
        digits = ((s[:, :, None] >> np.arange(4)) & 1) * np.exp2(np.arange(4) - 23.0)
        u[:, h, h, 0] = c
        if i < 4:
            x[:, g, 0, :, 0] = i % 2 * 3.0 - 1.5
            x[:, g, 8] = digits
            x[:, g, 11, :, 0] = 2.0 ** -10
            u[:, h + 11, h, 0] = c
        elif i < 6: x[:, g, 8] = digits * rng.choice([-1.0, 1.0], (N, C, 1))
        else:
            x[:, g, 10, :, 0] = rng.choice([-1.0, 1.0], (N, C)) * 2.0 ** -30
            x[:, g, 11, :, 0] = 2.0 ** -29
            w[:, g, 10, 0, g, 9, 0] = 2.0 ** -9
            w[:, g, 12, 0, g, 9, 0] = 1.0
            w[:, g, 10, 0, g, 13, 0] = -2.0 ** -9
            w[:, g, 12, 0, g, 13, 0] = 1.0
            w[:, g, 11, 0, g, 11, 0] = 16.0
            u[:, h + 9, h, 0] = 1.125 * c
            u[:, h + 13, h, 0] = c
        if i < 6: u[:, h + 8, h] = c
        if i % 2: x[:, g, 0, at[i // 2], 0] = 2.0 ** 29 * rng.choice([-1.0, 1.0], N)
    return {"x": x.reshape(N, 128, 4 * C).astype(BF), "u": u.reshape(N, 128, 512), "v": d["v"], **stored(k, n), **weights(rng, w)}
def setup_inputs_odd(rng):
    d = numbers_of(rng)
    x = (1.0 + (2 * rng.integers(0, 64, (N, 16, 8, C, 4)) + 1) * 2.0 ** -7) * np.exp2(-rng.integers(0, 7, (N, 16, 8, C, 4)).astype(np.float64)) * rng.choice([-1.0, 1.0], (N, 16, 8, C, 4))
    x[:, :, 0, :, 0] = 1.96875 * 2.0 ** 8 * rng.choice([-1.0, 1.0], (N, 16, C))
    x[:, ::2, 1, :, 0] = (8 + rng.integers(0, 2, (N, 8, C))) * 2.0 ** -8
    u = d["u"].reshape(N, 128, 128, 4)
    u[:, :, ::16] = 0
    for h in range(0, 128, 16): u[:, h + 1, h, 0] = 1.0
    return {"x": x.astype(np.float32).reshape(N, 128, 4 * C).astype(BF), "u": u.reshape(N, 128, 512), "v": d["v"], **stored(*lists(rng)), **weights(rng, layers(rng, [0, 8]))}
def setup_inputs_ends(rng):
    d = numbers_of(rng)
    k, n = lists(rng)
    j = np.arange(C)
    o = np.zeros(N, np.int64)
    for i, r in enumerate(rng.permutation([r for r in range(N) if not r & MASK[0]])):
        o[r], o[r ^ MASK[0]] = rng.permutation([1, 2] if i % 2 else [0, 3])
    e, h = rng.permutation(N) % 4, rng.permutation(N) % 4
    k[e == 0] = j
    k[e == 1] = j[::-1]
    k[e == 2] = (j + 1) % C
    n[h == 0] = j[::-1]
    n[h == 1] = j ^ 1
    n[h == 2] = (j + C // 2) % C
    s = rng.choice([-1.0, 1.0], (N, 8, 16, C, 4))
    s[o == 0] = -1
    s[o == 1] = rng.choice([-1.0, 1.0], (N, 1, 1, C, 1))[o == 1]
    x = s * (0.955 + 0.02 * rng.random((N, 8, 16, C, 4))) * 2.0 ** 30
    x[o == 3] = 2.0 ** -30
    g = int(rng.integers(8))
    x[:, g, :8] = 2.0 ** -30
    size = np.where(o == 3, 2.0 ** -30, 2.0 ** 30)
    a = np.stack([rng.permutation(8) % 2 * 2.0 - 1.0 for r in range(N)]) * size[:, None]
    u = d["u"].reshape(N, 128, 128, 4)
    u[:, :, ::16] = a.astype(np.float32).astype(BF)[:, None, :, None]
    v = rng.choice([-1.0, 1.0], (N, 128, 512)) * size[:, None, None]
    w = np.zeros((N, 128, 4, 128, 4), np.float32)
    i, l = np.arange(128), np.arange(16 * g, 16 * g + 8)
    for b in range(4):
        w[:, i, b, i, b] = np.where(o == 3, 32.0, -0.125)[:, None]
        w[:, l, b, l, b] = np.where(o == 3, 256.0, 0.0)[:, None]
    return {"x": x.astype(np.float32).reshape(N, 128, 4 * C).astype(BF), "u": u.reshape(N, 128, 512), "v": v.astype(np.float32).astype(BF), **stored(k, n), **weights(rng, w.astype(BF))}
def setup_inputs_spread(rng):
    d = setup_inputs(rng)
    d["x"] = wide(rng, N, 128, 4 * C, cols=6)
    return d
def check_inputs(d):
    b = []
    for k in ("x", "u", "v"):
        a = np.abs(d[k].astype(np.float32))
        if not (np.isfinite(a).all() and ((a == 0) | (a >= 2.0 ** -30) & (a <= 2.0 ** 30)).all()): b.append("a value of " + k)
    none, least, most = [emit(mx_ref.quantize(np.full((128, 16), k, np.float32).astype(BF)))[1][0, 0] for k in (0.0, 2.0 ** -8, 2.0 ** 8)]
    top = emit(mx_ref.quantize(np.ascontiguousarray(np.tile(np.repeat(1.0 + np.arange(128) * 2.0 ** -7, 4), (128, 1))).astype(np.float32).astype(BF)))[0] & 0x7F
    for r in range(N):
        k, n = gentries(d["dl"][r]), gentries(d["nl"][r])
        if not (np.sort(k, axis=1) == np.arange(C)).all(): b.append("dl: not every column once")
        if not ((n >= 0) & (n < C)).all(): b.append("an entry of nl")
        elif not ((at(n, n) == np.arange(C)) & (n != np.arange(C))).all(): b.append("nl: not in pairs")
        if ((d["wc"][r] == 0x7F) | (d["wc"][r] == 0xFF)).any(): b.append("wc: a code that is no number")
        s = mx_ref.live(d["ws"][r])
        if ((s != none) & ((s < least) | (s > most))).any(): b.append("ws: a scale out of range")
        a = np.max(d["wc"][r].reshape(16, 8, 512, 4) & 0x7F, axis=(1, 3))
        if ((s == none) & (a != 0)).any(): b.append("wc: a code other than zero under the scale of zeros")
        if ((s != none) & ((a < top.min()) | (a > top.max()))).any(): b.append("wc: a block whose largest code isn't one of quantize_mx")
    return b
def at(t, e):
    return np.take_along_axis(t, e, axis=1)
def layer(w, q):
    return tile([mx_ref.matmul(pick(w, np.arange(128 * b, 128 * b + 128)), q) * np.float32(0.03125) for b in range(4)])
def reference(x, u, v, dl, nl, wc, ws):
    qu = [mx_ref.quantize(u[r]) for r in range(N)]
    lay = [pk(wc[r], ws[r]) for r in range(N)]
    d, n = [gentries(dl[r]) for r in range(N)], [gentries(nl[r]) for r in range(N)]
    now = [x[r] for r in range(N)]
    for m in MASK:
        s = [mx_ref.matmul(qu[r], mx_ref.quantize(now[r]))[::16] + np.float32(0.0) for r in range(N)]
        new, h, made = [], [], []
        for r in range(N):
            p = r ^ m
            a, b, k = np.tile(np.arange(C), (8, 1)), n[r], np.zeros((8, C), np.int64)
            for step in range(6):
                own = at(s[r], a) > at(s[p], b)
                a, b, k = np.where(own, at(d[r], a), a), np.where(own, b, at(d[p], b)), k + own
            z = ((gcols(now[r], a).astype(np.float32) + gcols(now[r], b).astype(np.float32)) * np.float32(0.5)).astype(BF)
            h.append(layer(lay[r], mx_ref.quantize(z)))
            new.append(np.where((k + at(k, n[r])) % 2 == 1, at(d[r], n[r]), d[r]))
        for r in range(N):
            p = r ^ m
            far = decode(mx_ref.quantize(np.ascontiguousarray(h[p][:, :4 * F]))).astype(BF)
            both = np.concatenate([far, h[r][:, 4 * F:]], axis=1)
            place = at(np.argsort(d[p], axis=1), new[r])
            made.append((now[r].astype(np.float32) + gcols(both, place).astype(np.float32)).astype(BF))
        now, d = made, new
    y, dn = np.zeros((N, 128, C), np.float32), np.zeros((N, 8, C), np.float32)
    oc, osc = np.zeros((N, 128, 4 * C), np.uint8), np.zeros((N, 16, C), np.uint8)
    for r in range(N):
        q = mx_ref.quantize(now[r])
        y[r] = mx_ref.matmul(mx_ref.quantize(v[r]), q)
        dn[r] = d[r]
        oc[r], osc[r] = emit(q)
    return {"y": y, "dn": dn, "oc": oc, "osc": osc}

@@ -1,0 +1,392 @@
+from concourse.mybir import dt, AluOpType, ActivationFunctionType
+
+C, F, ROUNDS = 448, 336, 3
+K = C // 16
+MASKS = [1, 2, 3]
+CH = [(0, 192), (192, 336)]
+CHZ = [(0, 192), (192, 352), (352, 448)]
+OWN = (320, 448)
+NB = 1 << 9
+NK = 1 << 19
+SLOTS = ["iotaT", "mask", "inv", "dT", "nT", "i512", "nd", "P", "hp", "pk", "pk2", "V1", "U", "V1b", "Ub", "df", "dfo", "eo",
+         "glo", "par", "wd", "wn"]
+ISLOTS = ["W", "i1", "i2", "is", "odd", "ip", "ib", "dli", "nli"]
+OPT = {"scat": 2, "z3": 1, "can": 6, "ssend": 1, "exp": 3, "pl": 0}
+
+SCRATCH = {
+    "sm": ("sbuf", [128, K * len(SLOTS)], "float32"),
+    "si": ("sbuf", [128, K * len(ISLOTS)], "int32"),
+    "xp": ("sbuf", [128, 4 * C], "bfloat16"), "tmp": ("sbuf", [128, 4 * C], "bfloat16"),
+    "z": ("sbuf", [128, 4 * C], "bfloat16"), "hh": ("sbuf", [128, 4 * F], "bfloat16"),
+    "jp": ("sbuf", [128, 4 * C], "bfloat16"),
+    "ub": ("sbuf", [128, 512], "bfloat16"), "vb": ("sbuf", [128, 512], "bfloat16"),
+    "one": ("sbuf", [128, 512], "bfloat16"),
+    "qu": ("sbuf", [128, 128], "float8_e4m3fn_x4"), "su": ("sbuf", [128, 128], "uint8"),
+    "qv": ("sbuf", [128, 128], "float8_e4m3fn_x4"), "sv_": ("sbuf", [128, 128], "uint8"),
+    "qx": ("sbuf", [128, C], "float8_e4m3fn_x4"), "sx": ("sbuf", [128, C], "uint8"),
+    "qz": ("sbuf", [128, C], "float8_e4m3fn_x4"), "sz": ("sbuf", [128, C], "uint8"),
+    "qo": ("sbuf", [128, 128], "float8_e4m3fn_x4"), "so": ("sbuf", [128, 128], "uint8"),
+    "qw": ("sbuf", [128, 512], "float8_e4m3fn_x4"), "sw": ("sbuf", [128, 512], "uint8"),
+    "qe": ("sbuf", [128, 512], "float8_e4m3fn_x4"), "se_": ("sbuf", [128, 512], "uint8"),
+    "bm": ("sbuf", [128, 6 * K], "float32"), "pp": ("sbuf", [128, 6 * K], "float32"),
+    "hw": ("sbuf", [128, 6 * K], "float32"), "hpw": ("sbuf", [128, 6 * K], "float32"), "x84": ("sbuf", [128, 3 * K], "float32"),
+    "ysb": ("sbuf", [128, C], "float32"),
+    "ph": ("psum", [128, 2048], "float32"), "pd": ("psum", [128, 2048], "float32"),
+    "pq": ("sbuf", [128, 1], "float32"),
+}
+for _n in ("iotaS", "einv", "m16", "rst", "c16", "gm", "sc", "ta0", "ca", "can", "tac", "ts", "tbb", "tcb", "tfb", "spk", "te", "tm", "mi"):
+    SCRATCH[_n] = ("sbuf", [128, C], "float32")
+for _n in ("s480", "t480", "r480", "f480"): SCRATCH[_n] = ("sbuf", [128, C + 32], "float32")
+for _n in ("dW", "nW", "eW", "pW", "aW", "bW", "lW"): SCRATCH[_n] = ("sbuf", [128, K], "uint16")
+for _i in range(4):
+    SCRATCH["x%d" % _i] = ("sbuf", [128, 4 * C], "bfloat16")
+    SCRATCH["et%d" % _i] = ("sbuf", [128, 512], "bfloat16")
+for _i in range(6):
+    SCRATCH["tb%d" % _i] = ("sbuf", [128, C], "float32")
+    SCRATCH["sa%d" % _i] = ("sbuf", [128, C], "float32")
+for _i in range(7): SCRATCH["sb%d" % _i] = ("sbuf", [128, C], "float32")
+for _r in range(ROUNDS):
+    SCRATCH["tsend%d" % _r] = ("sbuf", [128, K], "float32")
+    SCRATCH["tland%d" % _r] = ("sbuf", [128, K], "float32")
+    SCRATCH["lsend%d" % _r] = ("sbuf", [128, 2 * K], "float32")
+    SCRATCH["lland%d" % _r] = ("sbuf", [128, 2 * K], "float32")
+    SCRATCH["qh%d" % _r] = ("sbuf", [128, F], "float8_e4m3fn_x4")
+    SCRATCH["sh%d" % _r] = ("sbuf", [128, F], "uint8")
+    SCRATCH["ql%d" % _r] = ("sbuf", [128, F], "float8_e4m3fn_x4")
+    SCRATCH["sl%d" % _r] = ("sbuf", [128, F], "uint8")
+
+SEMAPHORES = ["qv", "qs", "qt", "qg", "da"] + ["ld%d" % i for i in range(9)] + ["st%d" % i for i in range(7)]
+for _r in range(ROUNDS):
+    for _n in ("t", "l", "c0", "s0", "c1", "s1"): SEMAPHORES += ["a%s%d" % (_n, _r), "o%s%d" % (_n, _r)]
+
+
+def rank_program(g, core, T, topo):
+    rank = T.rank_of(core)
+    if rank is None:
+        return
+    A = AluOpType
+    CP = ActivationFunctionType.Copy
+    eng = {"v": g.vector, "s": g.scalar, "t": g.tensor, "g": g, "y": g.sync}
+    own = {"v": "qv", "s": "qs", "t": "qt", "g": "qg"}
+    count, known, lastw, readers, snap = {}, {q: {} for q in eng}, {}, {}, {}
+
+    def wait(q, ev):
+        s, n = ev
+        if known[q].get(s, 0) >= n: return
+        eng[q].wait_ge(T.sem[s], n)
+        known[q][s] = n
+        for a, b in snap.get(ev, {}).items():
+            if known[q].get(a, 0) < b: known[q][a] = b
+
+    def need(q, r, w):
+        deps = []
+        for k in r: deps += lastw.get(k, [])
+        for k in w: deps += lastw.get(k, []) + readers.get(k, [])
+        best = {}
+        for s, n in deps: best[s] = max(n, best.get(s, 0))
+        for s in sorted(best): wait(q, (s, best[s]))
+
+    def done(q, ev, r, w):
+        snap[ev] = dict(known[q])
+        for k in r: readers.setdefault(k, []).append(ev)
+        for k in w: lastw[k], readers[k] = [ev], []
+
+    def op(q, call, r, w):
+        w = w + [k for k in r if k[0] == "P"]
+        r = [k for k in r if k[0] != "P"]
+        need(q, r, w)
+        s = own[q]
+        count[s] = count.get(s, 0) + 1
+        call().then_inc(T.sem[s], 1)
+        done(q, (s, count[s]), r, w)
+
+    def dma(q, sem, out, in_, r, w):
+        need(q, r, w)
+        eng[q].dma_start(out, in_).then_inc(T.sem[sem], 16)
+        count[sem] = count.get(sem, 0) + 16
+        done(q, (sem, count[sem]), r, w)
+
+    def send(dst, name, out, in_, r):
+        need("g", r, [])
+        m = topo.mask(core, dst)
+        rid, pid = topo.addr(dst)[:2]
+        g.remote_dma(out, in_, T.sem["a" + name], T.sem["o" + name], pid, rid, m)
+        count["o" + name] = len(topo.engines(core, dst))
+        done("g", ("o" + name, count["o" + name]), r, [])
+
+    def arrives(src, name, w):
+        count["a" + name] = len(topo.engines(src, core))
+        for k in w: lastw[k] = [("a" + name, count["a" + name])]
+
+    def sm(n):
+        i = SLOTS.index(n)
+        return T.sm[:, K * i:K * i + K]
+
+    def si(n):
+        i = ISLOTS.index(n)
+        return T.si[:, K * i:K * i + K]
+
+    def sl(b, i, n=1): return T[b][:, K * i:K * i + K * n]
+
+    def col(b, q):
+        return T[b][:, q:C:16]
+
+    def shifted(b, q):
+        return T[b][:, 16 + q:C + q + 1:16]
+
+    def tt(out, a, b, o, r, w): op("v", lambda: g.vector.tensor_tensor(out, a, b, o), r, w)
+    def ts1(out, a, s, o, r, w): op("v", lambda: g.vector.tensor_scalar(out, a, s, None, o), r, w)
+    def ts2(out, a, s, o, s2, o2, r, w): op("v", lambda: g.vector.tensor_scalar(out, a, s, s2, o, o2), r, w)
+    def cp(out, a, r, w): op("v", lambda: g.vector.tensor_copy(out, a), r, w)
+    def tr(out, a, r, w): op("v", lambda: g.vector.transpose(out, a), r, w)
+    def act(out, a, r, w, scale=1.0):
+        if scale == 1.0: op("s", lambda: g.scalar.activation(out, a, CP), r, w)
+        else: op("s", lambda: g.scalar.activation(out, a, CP, scale=scale), r, w)
+    def quant(q, s, t, r, w): op("v", lambda: g.vector.quantize_mx(q, s, t), r, w)
+    def mm(out, a, sa, b, sb, r, w): op("t", lambda: g.tensor.matmul_mx(out, a, sa, b, sb, True, True), r, w)
+    def fill(ap, v, w): op("v", lambda: g.vector.memset(ap, v), [], w)
+    def iota(out, pat, base, cm, w, f=True):
+        if f: op("g", lambda: g.iota(out, pat, base, cm, allow_small_or_imprecise_dtypes=True), [], w)
+        else: op("g", lambda: g.iota(out, pat, base, cm), [], w)
+
+    def zero(ap, w): iota(ap, [[0, ap.shape[1]]], 0, 0, w)
+
+    peer = [T.cores[rank ^ m] for m in MASKS]
+    for r in range(ROUNDS):
+        arrives(peer[r], "t%d" % r, ["tland%d" % r])
+        arrives(peer[r], "l%d" % r, ["lland%d" % r])
+        for k in range(2):
+            arrives(peer[r], "c%d%d" % (k, r), ["ql%d.%d" % (r, k)])
+            arrives(peer[r], "s%d%d" % (k, r), ["sl%d.%d" % (r, k)])
+
+    dma("s", "ld0", si("dli"), T.dl[:, :], [], ["dli"])
+    dma("y", "ld2", T.x0[:, 0:2 * C], T.x[:, 0:2 * C], [], ["x0"])
+    dma("s", "ld1", si("nli"), T.nl[:, :], [], ["nli"])
+    dma("y", "ld3", T.x0[:, 2 * C:4 * C], T.x[:, 2 * C:4 * C], [], ["x0b"])
+    dma("y", "ld4", T.ub[:, :], T.u[:, :], [], ["ub"])
+    dma("y", "ld5", T.qw[:, :].bitcast(dt.uint8), T.wc[:, :], [], ["qw"])
+    dma("y", "ld6", T.sw[:, :], T.ws[:, :], [], ["sw"])
+    dma("y", "ld7", T.vb[:, :], T.v[:, :], [], ["vb"])
+    lastw["x0"] = [("ld2", 16), ("ld3", 16)]
+
+    iota(si("ip"), [[0, K]], 0, 1, ["ip"], False)
+    iota(sm("glo"), [[0, K // 2], [1, 2]], 0, 0, ["glo"])
+    iota(si("ib"), [[32, K // 2], [0, 2]], 0, 0, ["ib"], False)
+    zero(T.ta0[:, :], ["ta0"])
+    zero(T.tbb[:, :], ["tbb"])
+    for b in ("tfb", "r480"): fill(T[b][:, :], 0.0, [b])
+    ts2(si("i1"), si("ip"), 4, A.arith_shift_right, 1, A.bitwise_and, ["ip"], ["i1"])
+    cp(sm("par"), si("i1"), ["i1"], ["par"])
+    tt(sm("mask"), sm("par"), sm("glo"), A.is_equal, ["par", "glo"], ["mask"])
+    tt(sm("inv"), sm("par"), sm("glo"), A.not_equal, ["par", "glo"], ["inv"])
+    ts1(si("i2"), si("ip"), 31, A.bitwise_and, ["ip"], ["i2"])
+    tt(sm("iotaT"), si("i2"), si("ib"), A.add, ["i2", "ib"], ["iotaT"])
+
+    def swap(t, s, u, vals, outs):
+        for q, (v, k) in enumerate(vals): cp(col(t, q), v, k, [t])
+        tr(T[s][:, 16:16 + C], T[t][:, :], [t], [s])
+        tr(T[u][:, :], T[s][:, :], [s], [u])
+        for q, ((v, k), (o, ok)) in enumerate(zip(vals, outs)):
+            tt(sm("V1b"), v, sm("mask"), A.mult, k + ["mask"], ["V1b"])
+            tt(sm("Ub"), shifted(u, q), sm("inv"), A.mult, [u, "inv"], ["Ub"])
+            tt(o, sm("V1b"), sm("Ub"), A.add, ["V1b", "Ub"], ok)
+
+    cp(T.dW[:, :], si("dli"), ["dli"], ["dW"])
+    cp(T.lsend0[:, K:2 * K], si("dli"), ["dli"], ["ls0w"])
+    cp(T.nW[:, :], si("nli"), ["nli"], ["nW"])
+    cp(sm("wn"), si("nli"), ["nli"], ["wn"])
+    swap("tfb", "r480", "f480", [(T.lsend0[:, K:2 * K], ["ls0w"]), (sm("wn"), ["wn"])], [(sm("dT"), ["dT"]), (sm("nT"), ["nT"])])
+    cp(T.lsend0[:, 0:K], sm("dT"), ["dT"], ["ls0t"])
+    send(peer[0], "l0", T.lland0[:, :], T.lsend0[:, :], ["ls0w", "ls0t"])
+    quant(T.qu[:, :], T.su[:, :], T.ub[:, :], ["ub"], ["qu"])
+    zero(T.ca[:, :], ["ca%d" % i for i in range(7)])
+    zero(T.tcb[:, :], ["tcb"])
+    cp(col("ta0", 4), sm("iotaT"), ["iotaT"], ["ta0"])
+    fill(T.tm[:, :], 1e29, ["tm"])
+
+    def late_constants():
+        zero(T.s480[:, :], ["s480"])
+        iota(T.iotaS[:, :], [[1, C]], 0, 0, ["iotaS"])
+        iota(T.c16[:, :], [[0, K], [1, 16]], 0, 0, ["c16"])
+        fill(T.one[:, :], 1.0, ["one"])
+        for b in range(4):
+            op("g", lambda: g.affine_select(T["et%d" % b][:, :], T.one[:, :], [[-1, 512]], A.is_equal, 0.0, b, 4), ["one"], ["et%d" % b])
+        ts1(sm("i512"), sm("iotaT"), float(NB), A.mult, ["iotaT"], ["i512"])
+        ts1(si("i1"), si("ip"), 15, A.bitwise_and, ["ip"], ["i1"])
+        cp(T.pq[:, :], T.si[:, K * ISLOTS.index("i1"):K * ISLOTS.index("i1") + 1], ["i1"], ["pq"])
+        ts1(T.m16[:, :], T.c16[:, :], T.pq[:, :], A.is_equal, ["c16", "pq"], ["m16"])
+        ts1(T.rst[:, :], T.c16[:, :], 0.0, A.not_equal, ["c16"], ["rst"])
+
+    def pick16(win, off, wkeys):
+        tt(T.gm[:, :], win.indirect(off), T.m16[:, :], A.mult, wkeys + ["m16"], ["gm"])
+
+    def fold16(out, okey):
+        op("v", lambda: g.vector.tensor_tensor_scan(T.sc[:, :], T.rst[:, :], T.gm[:, :], 0.0, A.mult, A.add), ["rst", "gm"], ["sc"])
+        cp(out, T.sc[:, 15:C:16], ["sc"], [okey])
+
+    def partner_list(r):
+        cp(T.eW[:, :], T["lland%d" % r][:, K:2 * K], ["lland%d" % r], ["eW"])
+        tt(sm("eo"), T["lland%d" % r][:, 0:K], sm("iotaT"), A.subtract, ["lland%d" % r, "iotaT"], ["eo"])
+        ts2(col("tbb", 8), sm("eo"), float(NB), A.mult, float(NK), A.add, ["eo"], ["tbb"])
+
+    def invert(): op("v", lambda: g.vector.tensor_copy(T.einv[:, :].indirect(T.eW[:, :]), T.iotaS[:, :]), ["eW", "iotaS"], ["einv"])
+
+    for r in range(ROUNDS):
+        p = peer[r]
+        X, XN = "x%d" % r, "x%d" % (r + 1)
+        ll, lk = T["lland%d" % r], "lland%d" % r
+        quant(T.qx[:, :], T.sx[:, :], T[X][:, :], [X], ["qx"])
+        mm(T.pd[:, 0:C], T.qu[:, :], T.su[:, :], T.qx[:, :], T.sx[:, :], ["qu", "qx"], ["Pd0"])
+        tt(col("ta0", 8), sm("iotaT"), sm("dT"), A.subtract, ["iotaT", "dT"], ["ta0"])
+        tt(sm("nd"), sm("nT"), sm("dT"), A.subtract, ["nT", "dT"], ["nd"])
+        if r: partner_list(r)
+        if OPT["scat"] == 4: invert()
+        for t in range(4): act(T.xp[:, C * t:C * t + C], T[X][:, t:4 * C:4], [X], ["xp%d" % t], 0.5)
+        tr(T.ts[:, :], T.pd[:, 0:C], ["Pd0"], ["ts"])
+        if OPT["ssend"]: act(T["tsend%d" % r][:, :], col("ts", 0), ["ts"], ["tsend%d" % r])
+        else: cp(T["tsend%d" % r][:, :], col("ts", 0), ["ts"], ["tsend%d" % r])
+        send(p, "t%d" % r, T["tland%d" % r][:, :], T["tsend%d" % r][:, :], ["tsend%d" % r])
+        cp(col("ta0", 0), col("ts", 0), ["ts"], ["ta0"])
+        cp(col("tm", 0), col("ts", 0), ["ts"], ["tm"])
+        tr(T.sa0[:, :], T.ta0[:, :], ["ta0"], ["sa0"])
+        tr(T.mi[:, :], T.tm[:, :], ["tm"], ["mi"])
+
+        def rows(i): dma("y", "da", T.ca[i:128:8, :], T["sa%d" % i][0:128:8, :], ["sa%d" % i], ["ca%d" % i])
+        rows(0)
+        for i in range(1, 6):
+            if i == OPT["exp"]:
+                if r == 0: partner_list(0)
+                cp(col("tbb", 0), T["tland%d" % r][:, :], ["tland%d" % r], ["tbb"])
+                tr(T.sb0[:, :], T.tbb[:, :], ["tbb"], ["sb0"])
+            tt(T["sa%d" % i][:, :], T["sa%d" % (i - 1)][:, :].indirect(T.dW[:, :]), T.mi[:, :], A.min, ["sa%d" % (i - 1), "dW", "mi"], ["sa%d" % i])
+            rows(i)
+        dma("y", "da", T.ca[6:128:16, :], T.sa5[4:128:16, :], ["sa5"], ["ca6"])
+        cp(sl("bm", 0), T["tland%d" % r][:, :], ["tland%d" % r], ["bm0"])
+        if OPT["scat"] == 1: invert()
+        for j in range(1, 6): act(T["sb%d" % j][:, :], T["sb%d" % (j - 1)][:, :].indirect(T.eW[:, :]), ["sb%d" % (j - 1), "eW"], ["sb%d" % j])
+        act(T.can[:, :], T.ca[:, :].indirect(T.nW[:, :]), ["nW"] + ["ca%d" % i for i in range(7)], ["can"])
+
+        def tb_(j): tr(T["tb%d" % j][:, :], T["sb%d" % j][:, :], ["sb%d" % j], ["tb%d" % j])
+        def bm_(j): tt(sl("bm", j), sl("bm", j - 1), col("tb%d" % j, 0), A.min, ["bm%d" % (j - 1), "tb%d" % j], ["bm%d" % j])
+        def pp_(j):
+            b = "tb%d" % j if j else "tbb"
+            tt(sl("pp", j), col(b, 8), col("tac", 13 - j), A.add, [b, "tac"], ["pp%d" % j])
+        def h_(j): tt(sl("hw", j), col("tac", 5 - j), sl("bm", j), A.is_le, ["tac", "bm%d" % j], ["hw%d" % j])
+        if r == 0: late_constants()
+        for j in range(1, OPT["can"]): tb_(j)
+        for j in range(1, OPT["can"]): bm_(j)
+        if OPT["scat"] == 0: invert()
+        tr(T.tac[:, :], T.can[:, :], ["can"], ["tac"])
+        tt(sm("pk"), sm("i512"), col("tac", 6), A.add, ["i512", "tac"], ["pk"])
+        for j in range(0, OPT["can"]):
+            pp_(j)
+            h_(j)
+        tt(sm("pk2"), sm("pk"), col("tac", 13), A.subtract, ["pk", "tac"], ["pk2"])
+        for j in range(OPT["can"], 6):
+            tb_(j)
+            bm_(j)
+            pp_(j)
+            h_(j)
+        tt(T.hpw[:, :], T.hw[:, :], T.pp[:, :], A.mult, ["%s%d" % (b, j) for b in ("hw", "pp") for j in range(6)], ["hpw"])
+        tt(T.x84[:, :], sl("hpw", 0, 3), sl("hpw", 3, 3), A.add, ["hpw"], ["x84"])
+        tt(sm("P"), sl("x84", 0), sl("x84", 1), A.add, ["x84"], ["P"])
+        tt(sm("hp"), sl("x84", 2), sm("pk2"), A.add, ["x84", "pk2"], ["hp"])
+        tt(col("tcb", 0), sm("P"), sm("hp"), A.add, ["P", "hp"], ["tcb"])
+        tr(T.spk[:, :], T.tcb[:, :], ["tcb"], ["spk"])
+        act(T.s480[:, 16:16 + C], T.spk[:, :].indirect(T.nW[:, :]), ["spk", "nW"], ["s480"])
+        if OPT["scat"] == 2: invert()
+        tr(T.te[:, :], T.s480[:, 16:16 + C], ["s480"], ["te"])
+        tr(T.t480[:, :], T.s480[:, :], ["s480"], ["t480"])
+        tt(sm("V1"), col("te", 0), sm("mask"), A.mult, ["te", "mask"], ["V1"])
+        tt(sm("U"), shifted("t480", 0), sm("inv"), A.mult, ["t480", "inv"], ["U"])
+        tt(si("W"), sm("V1"), sm("U"), A.add, ["V1", "U"], ["W"])
+        ts1(si("i1"), si("W"), NB - 1, A.bitwise_and, ["W"], ["i1"])
+        cp(T.aW[:, :], si("i1"), ["i1"], ["aW"])
+        ts2(si("i2"), si("W"), 9, A.arith_shift_right, NB - 1, A.bitwise_and, ["W"], ["i2"])
+        cp(T.bW[:, :], si("i2"), ["i2"], ["bW"])
+
+        def gather_a(k, t):
+            lo, hi = CHZ[k]
+            act(T.tmp[:, C * t + lo:C * t + hi], T.xp[:, C * t:C * t + C].indirect(T.aW[:, lo // 16:hi // 16]), ["xp%d" % t, "aW"], ["tmp%d%d" % (k, t)])
+
+        def add_b(k, t):
+            lo, hi = CHZ[k]
+            tt(T.z[:, 4 * lo + t:4 * hi:4], T.xp[:, C * t:C * t + C].indirect(T.bW[:, lo // 16:hi // 16]), T.tmp[:, C * t + lo:C * t + hi], A.add,
+               ["xp%d" % t, "bW", "tmp%d%d" % (k, t)], ["z%d%d" % (k, t)])
+
+        def layer(lo, hi, bank, q, s, c0, zk, qk):
+            quant(T[q][:, lo - c0:hi - c0], T[s][:, lo - c0:hi - c0], T.z[:, 4 * lo:4 * hi], ["z%d%d" % (k, t) for k in zk for t in range(4)], [qk])
+            for i in range(4):
+                mm(T[bank][:, 512 * i:512 * i + hi - lo], T.qw[:, 128 * i:128 * i + 128], T.sw[:, 128 * i:128 * i + 128], T[q][:, lo - c0:hi - c0], T[s][:, lo - c0:hi - c0],
+                   ["qw", "sw", qk], ["P" + bank[1] + str(i)])
+
+        def pack(k):
+            lo, hi = CH[k]
+            quant(T["qh%d" % r][:, lo:hi], T["sh%d" % r][:, lo:hi], T.hh[:, 4 * lo:4 * hi], ["hh%d%d" % (k, i) for i in range(4)], ["qh%d%d" % (r, k)])
+            send(p, "c%d%d" % (k, r), T["ql%d" % r][:, lo:hi].bitcast(dt.uint8), T["qh%d" % r][:, lo:hi].bitcast(dt.uint8), ["qh%d%d" % (r, k)])
+            send(p, "s%d%d" % (k, r), T["sl%d" % r][:, lo:hi], T["sh%d" % r][:, lo:hi], ["qh%d%d" % (r, k)])
+
+        def evac(k, i, q):
+            lo, hi = CH[k]
+            src, dst, pk_ = T[("ph", "pd")[k]][:, 512 * i:512 * i + hi - lo], T.hh[:, 4 * lo + i:4 * hi:4], "P" + "hd"[k] + str(i)
+            if q == "s": act(dst, src, [pk_], ["hh%d%d" % (k, i)], 0.03125)
+            else: ts1(dst, src, 0.03125, A.mult, [pk_], ["hh%d%d" % (k, i)])
+
+        for k in range(2):
+            for t in range(4): gather_a(k, t)
+        for t in range(4): add_b(0, t)
+        layer(0, 192, "ph", "qz", "sz", 0, [0], "qz0")
+        for t in range(4): add_b(1, t)
+        layer(192, 336, "pd", "qz", "sz", 0, [1], "qz1")
+        for i in range(4): evac(0, i, "s")
+        pack(0)
+        for i in range(4): evac(1, i, "vs"[i % 2])
+        for t in range(4): gather_a(2, t)
+        pack(1)
+
+        def own_part():
+            for t in range(4): add_b(2, t)
+            layer(OWN[0], OWN[1], "ph", "qo", "so", OWN[0], [1, 2], "qo")
+            for i in range(4): act(T.jp[:, C * i + F:C * i + C], T.ph[:, 512 * i + F - OWN[0]:512 * i + C - OWN[0]], ["Ph%d" % i], ["jp%dh" % i], 0.03125)
+        if OPT["z3"] == 1: own_part()
+        tt(si("is"), col("tcb", 0), col("te", 0), A.add, ["tcb", "te"], ["is"])
+        tt(sm("df"), sm("nd"), col("tac", 8), A.subtract, ["nd", "tac"], ["df"])
+        ts2(si("odd"), si("is"), 19, A.arith_shift_right, 1, A.bitwise_and, ["is"], ["odd"])
+        tt(sm("dfo"), sm("df"), si("odd"), A.mult, ["df", "odd"], ["dfo"])
+        tt(sm("dT"), sm("dT"), sm("dfo"), A.add, ["dT", "dfo"], ["dT"])
+        last = r == ROUNDS - 1
+        fw, fk = (sm("wd"), "wd") if last else (T["lsend%d" % (r + 1)][:, K:2 * K], "ls%dw" % (r + 1))
+        if not last: cp(T["lsend%d" % (r + 1)][:, 0:K], sm("dT"), ["dT"], ["ls%dt" % (r + 1)])
+        swap("tfb", "r480", "f480", [(sm("dT"), ["dT"])], [(fw, [fk])])
+        cp(T.dW[:, :], fw, [fk], ["dW"])
+        if last:
+            dma("y", "st0", T.dn[:, :], T.r480[0:128:16, 16:16 + C], ["r480"], [])
+        else:
+            send(peer[r + 1], "l%d" % (r + 1), T["lland%d" % (r + 1)][:, :], T["lsend%d" % (r + 1)][:, :], ["ls%dw" % (r + 1), "ls%dt" % (r + 1)])
+        if OPT["scat"] == 3: invert()
+        if OPT["z3"] == 0: own_part()
+        pick16(T.einv[:, :], T.dW[:, :], ["einv", "dW"])
+        fold16(T.lW[:, :], "lW")
+        if r == 0:
+            for b in range(4): quant(T.qe[:, 128 * b:128 * b + 128], T.se_[:, 128 * b:128 * b + 128], T["et%d" % b][:, :], ["et%d" % b], ["qe%d" % b])
+        if last: quant(T.qv[:, :], T.sv_[:, :], T.vb[:, :], ["vb"], ["qv"])
+        for k, (lo, hi) in enumerate(CH):
+            n = hi - lo
+            for b in range(4):
+                mm(T[("ph", "pd")[k]][:, 512 * b:512 * b + n], T.qe[:, 128 * b:128 * b + 128], T.se_[:, 128 * b:128 * b + 128], T["ql%d" % r][:, lo:hi], T["sl%d" % r][:, lo:hi],
+                   ["qe%d" % b, "ql%d.%d" % (r, k), "sl%d.%d" % (r, k)], ["P" + "hd"[k] + str(b)])
+            for b in range(4):
+                src, dst, pk_ = T[("ph", "pd")[k]][:, 512 * b:512 * b + n], T.jp[:, C * b + lo:C * b + hi], "P" + "hd"[k] + str(b)
+                if k == 0 or b % 2: act(dst, src, [pk_], ["jp%d%d" % (b, k)])
+                else: cp(dst, src, [pk_], ["jp%d%d" % (b, k)])
+        for t in range(4):
+            tt(T[XN][:, t:4 * C:4], T.jp[:, C * t:C * t + C].indirect(T.lW[:, :]), T[X][:, t:4 * C:4], A.add,
+               ["jp%d0" % t, "jp%d1" % t, "jp%dh" % t, "lW", X], [XN])
+
+    quant(T.qx[:, :], T.sx[:, :], T.x3[:, :], ["x3"], ["qx"])
+    dma("y", "st1", T.oc[:, :], T.qx[:, :].bitcast(dt.uint8), ["qx"], [])
+    mm(T.pd[:, 0:C], T.qv[:, :], T.sv_[:, :], T.qx[:, :], T.sx[:, :], ["qv", "qx"], ["Pd0"])
+    for k in range(4): dma("y", "st%d" % (2 + k), T.osc[4 * k:4 * k + 4, :], T.sx[32 * k:32 * k + 4, :], ["qx"], [])
+    act(T.ysb[:, :], T.pd[:, 0:C], ["Pd0"], ["ysb"])
+    dma("s", "st6", T.y[:, :], T.ysb[:, :], ["ysb"], [])
+    for s in sorted(count): wait("g", (s, count[s]))

@@ -3,61 +3,70 @@ from concourse.mybir import dt, AluOpType, ActivationFunctionType
 C, F, ROUNDS = 448, 336, 3
 K = C // 16
 MASKS = [1, 2, 3]
+HALF = [(0, C // 2), (C // 2, C)]
 CH = [(0, 192), (192, 336)]
 CHZ = [(0, 192), (192, 352), (352, 448)]
 OWN = (320, 448)
-NB = 1 << 9
-NK = 1 << 19
-SLOTS = ["iotaT", "mask", "inv", "dT", "nT", "i512", "nd", "P", "hp", "pk", "pk2", "V1", "U", "V1b", "Ub", "df", "dfo", "eo",
-         "glo", "par", "wd", "wn"]
-ISLOTS = ["W", "i1", "i2", "is", "odd", "ip", "ib", "dli", "nli"]
-OPT = {"scat": 2, "z3": 1, "can": 6, "ssend": 1, "exp": 3, "pl": 0}
+NZ = 1024.0
+BIG, E0, E1 = 2.0 ** 90, 2.0 ** 80, 2.0 ** 60
+SLOTS = ["iotaT", "iotaE", "mask", "inv", "par", "glo", "A3", "A4", "A5", "B3", "B4", "B5", "d3", "e3", "np", "pbn", "t1", "t2", "t3", "t4", "xw"]
+ISLOTS = ["i1", "i2", "i3", "is", "odd", "ip", "ib", "dli", "nli", "bi"]
+COLS = ["pq", "sW", "bW", "sS", "bS", "sL", "bL", "b1", "s3", "sQ", "bQ", "s0", "b0", "c1", "c2", "c3", "c4"]
+OPT = {"fpos": 1, "ew": 2}
 
 SCRATCH = {
     "sm": ("sbuf", [128, K * len(SLOTS)], "float32"),
     "si": ("sbuf", [128, K * len(ISLOTS)], "int32"),
+    "cl": ("sbuf", [128, len(COLS)], "float32"), "ind": ("sbuf", [128, 16], "float32"), "c16": ("sbuf", [128, 16], "float32"),
     "xp": ("sbuf", [128, 4 * C], "bfloat16"), "tmp": ("sbuf", [128, 4 * C], "bfloat16"),
     "z": ("sbuf", [128, 4 * C], "bfloat16"), "hh": ("sbuf", [128, 4 * F], "bfloat16"),
     "jp": ("sbuf", [128, 4 * C], "bfloat16"),
     "ub": ("sbuf", [128, 512], "bfloat16"), "vb": ("sbuf", [128, 512], "bfloat16"),
-    "one": ("sbuf", [128, 512], "bfloat16"),
+    "one": ("sbuf", [128, 512], "bfloat16"), "et": ("sbuf", [128, 2048], "bfloat16"),
     "qu": ("sbuf", [128, 128], "float8_e4m3fn_x4"), "su": ("sbuf", [128, 128], "uint8"),
+    "qu2": ("sbuf", [128, 128], "float8_e4m3fn_x4"), "su2": ("sbuf", [128, 128], "uint8"),
     "qv": ("sbuf", [128, 128], "float8_e4m3fn_x4"), "sv_": ("sbuf", [128, 128], "uint8"),
     "qx": ("sbuf", [128, C], "float8_e4m3fn_x4"), "sx": ("sbuf", [128, C], "uint8"),
     "qz": ("sbuf", [128, C], "float8_e4m3fn_x4"), "sz": ("sbuf", [128, C], "uint8"),
     "qo": ("sbuf", [128, 128], "float8_e4m3fn_x4"), "so": ("sbuf", [128, 128], "uint8"),
     "qw": ("sbuf", [128, 512], "float8_e4m3fn_x4"), "sw": ("sbuf", [128, 512], "uint8"),
     "qe": ("sbuf", [128, 512], "float8_e4m3fn_x4"), "se_": ("sbuf", [128, 512], "uint8"),
-    "bm": ("sbuf", [128, 6 * K], "float32"), "pp": ("sbuf", [128, 6 * K], "float32"),
-    "hw": ("sbuf", [128, 6 * K], "float32"), "hpw": ("sbuf", [128, 6 * K], "float32"), "x84": ("sbuf", [128, 3 * K], "float32"),
+    "fl": ("sbuf", [128, 8 * K], "float32"), "da": ("sbuf", [128, 8 * K], "float32"),
+    "ra": ("sbuf", [128, 8 * K], "float32"), "rb": ("sbuf", [128, 8 * K], "float32"),
+    "m56": ("sbuf", [128, 2 * K], "float32"), "i56": ("sbuf", [128, 2 * K], "float32"),
+    "v56": ("sbuf", [128, 2 * K], "float32"), "u56": ("sbuf", [128, 2 * K], "float32"), "w56": ("sbuf", [128, 2 * K], "int32"),
+    "lb": ("sbuf", [128, 3 * K], "float32"), "df": ("sbuf", [128, 3 * K], "float32"), "pr": ("sbuf", [128, 3 * K], "float32"),
+    "qi": ("sbuf", [128, C], "int32"),
     "ysb": ("sbuf", [128, C], "float32"),
     "ph": ("psum", [128, 2048], "float32"), "pd": ("psum", [128, 2048], "float32"),
-    "pq": ("sbuf", [128, 1], "float32"),
 }
-for _n in ("iotaS", "einv", "m16", "rst", "c16", "gm", "sc", "ta0", "ca", "can", "tac", "ts", "tbb", "tcb", "tfb", "spk", "te", "tm", "mi"):
+for _n in ("mw", "mi", "ms", "o1", "o2", "to2", "g3o", "tg3o", "tbb", "sb", "g0", "g3", "tg0", "tg3", "tcb", "kn", "lrow", "l2", "d3p",
+           "q", "fi", "ep", "e1", "e2", "te", "e3p", "ei", "m1", "mn", "mp", "iotaS"):
     SCRATCH[_n] = ("sbuf", [128, C], "float32")
-for _n in ("s480", "t480", "r480", "f480"): SCRATCH[_n] = ("sbuf", [128, C + 32], "float32")
-for _n in ("dW", "nW", "eW", "pW", "aW", "bW", "lW"): SCRATCH[_n] = ("sbuf", [128, K], "uint16")
+for _n in ("s480", "t480"): SCRATCH[_n] = ("sbuf", [128, C + 32], "float32")
+for _n in ("nW", "npW", "cpW", "d3W", "e3W", "aW", "bW"): SCRATCH[_n] = ("sbuf", [128, K], "uint16")
+SCRATCH["eW"] = ("sbuf", [128, 2 * K], "uint16")
+SCRATCH["uW"] = ("sbuf", [128, 8], "uint16")
 for _i in range(4):
     SCRATCH["x%d" % _i] = ("sbuf", [128, 4 * C], "bfloat16")
-    SCRATCH["et%d" % _i] = ("sbuf", [128, 512], "bfloat16")
-for _i in range(6):
-    SCRATCH["tb%d" % _i] = ("sbuf", [128, C], "float32")
-    SCRATCH["sa%d" % _i] = ("sbuf", [128, C], "float32")
-for _i in range(7): SCRATCH["sb%d" % _i] = ("sbuf", [128, C], "float32")
+    SCRATCH["ln%d" % _i] = ("sbuf", [128, 3 * K], "float32")
+    SCRATCH["uw%d" % _i] = ("sbuf", [128, 3 * K], "uint16")
 for _r in range(ROUNDS):
-    SCRATCH["tsend%d" % _r] = ("sbuf", [128, K], "float32")
-    SCRATCH["tland%d" % _r] = ("sbuf", [128, K], "float32")
-    SCRATCH["lsend%d" % _r] = ("sbuf", [128, 2 * K], "float32")
+    SCRATCH["tsend%d" % _r] = ("sbuf", [128, 3 * K], "float32")
+    SCRATCH["tland%d" % _r] = ("sbuf", [128, 3 * K], "float32")
     SCRATCH["lland%d" % _r] = ("sbuf", [128, 2 * K], "float32")
     SCRATCH["qh%d" % _r] = ("sbuf", [128, F], "float8_e4m3fn_x4")
     SCRATCH["sh%d" % _r] = ("sbuf", [128, F], "uint8")
     SCRATCH["ql%d" % _r] = ("sbuf", [128, F], "float8_e4m3fn_x4")
     SCRATCH["sl%d" % _r] = ("sbuf", [128, F], "uint8")
+    if _r:
+        SCRATCH["isend%d" % _r] = ("sbuf", [128, K], "float32")
+        SCRATCH["iland%d" % _r] = ("sbuf", [128, K], "float32")
 
-SEMAPHORES = ["qv", "qs", "qt", "qg", "da"] + ["ld%d" % i for i in range(9)] + ["st%d" % i for i in range(7)]
+SEMAPHORES = ["qv", "qs", "qt", "qg"] + ["ld%d" % i for i in range(10)] + ["st%d" % i for i in range(9)]
+SEMAPHORES += ["md3", "me2", "me3", "mei", "mmn", "mmp", "mkn", "mq9", "mq1", "mis", "mep", "mnp", "mx9"]
 for _r in range(ROUNDS):
-    for _n in ("t", "l", "c0", "s0", "c1", "s1"): SEMAPHORES += ["a%s%d" % (_n, _r), "o%s%d" % (_n, _r)]
+    for _n in ("t", "l", "c0", "s0", "c1", "s1") + (("i",) if _r else ()): SEMAPHORES += ["a%s%d" % (_n, _r), "o%s%d" % (_n, _r)]
 
 
 def rank_program(g, core, T, topo):
@@ -65,7 +74,7 @@ def rank_program(g, core, T, topo):
     if rank is None:
         return
     A = AluOpType
-    CP = ActivationFunctionType.Copy
+    CP, ID = ActivationFunctionType.Copy, ActivationFunctionType.Identity
     eng = {"v": g.vector, "s": g.scalar, "t": g.tensor, "g": g, "y": g.sync}
     own = {"v": "qv", "s": "qs", "t": "qt", "g": "qg"}
     count, known, lastw, readers, snap = {}, {q: {} for q in eng}, {}, {}, {}
@@ -122,26 +131,34 @@ def rank_program(g, core, T, topo):
         i = SLOTS.index(n)
         return T.sm[:, K * i:K * i + K]
 
-    def si(n):
+    def si(n, w=K):
         i = ISLOTS.index(n)
-        return T.si[:, K * i:K * i + K]
+        return T.si[:, K * i:K * i + w]
+
+    def cl(n):
+        i = COLS.index(n)
+        return T.cl[:, i:i + 1]
 
     def sl(b, i, n=1): return T[b][:, K * i:K * i + K * n]
-
-    def col(b, q):
-        return T[b][:, q:C:16]
-
-    def shifted(b, q):
-        return T[b][:, 16 + q:C + q + 1:16]
+    def col(b, q): return T[b][:, q:C:16]
+    def row(b, q): return T[b][q:128:16, :]
+    def slot(b, h, s): return T[b][:, 4 * K * h + s:4 * K * (h + 1):4]
+    def whole(b): return T[b][:, :]
 
     def tt(out, a, b, o, r, w): op("v", lambda: g.vector.tensor_tensor(out, a, b, o), r, w)
     def ts1(out, a, s, o, r, w): op("v", lambda: g.vector.tensor_scalar(out, a, s, None, o), r, w)
     def ts2(out, a, s, o, s2, o2, r, w): op("v", lambda: g.vector.tensor_scalar(out, a, s, s2, o, o2), r, w)
     def cp(out, a, r, w): op("v", lambda: g.vector.tensor_copy(out, a), r, w)
     def tr(out, a, r, w): op("v", lambda: g.vector.transpose(out, a), r, w)
-    def act(out, a, r, w, scale=1.0):
-        if scale == 1.0: op("s", lambda: g.scalar.activation(out, a, CP), r, w)
+    def scan(out, a, b, r, w, first=0.0): op("v", lambda: g.vector.tensor_tensor_scan(out, a, b, first, A.mult, A.add), r, w)
+    def act(out, a, r, w, scale=1.0, bias=None):
+        if bias is not None: op("s", lambda: g.scalar.activation(out, a, ID, bias=bias, scale=scale), r, w)
+        elif scale == 1.0: op("s", lambda: g.scalar.activation(out, a, CP), r, w)
         else: op("s", lambda: g.scalar.activation(out, a, CP, scale=scale), r, w)
+    ROWS = {"q": ["", "1", "9"], "ep": ["", "9"], "ei": ["", "1", "9"], "e1": ["", "1"]}
+    def keys(b): return [b + k for k in ROWS.get(b, [""])]
+    def gat(out, win, off, r, **kw):
+        act(whole(out), whole(win).indirect(off), keys(win) + r, keys(out), **kw)
     def quant(q, s, t, r, w): op("v", lambda: g.vector.quantize_mx(q, s, t), r, w)
     def mm(out, a, sa, b, sb, r, w): op("t", lambda: g.tensor.matmul_mx(out, a, sa, b, sb, True, True), r, w)
     def fill(ap, v, w): op("v", lambda: g.vector.memset(ap, v), [], w)
@@ -149,161 +166,212 @@ def rank_program(g, core, T, topo):
         if f: op("g", lambda: g.iota(out, pat, base, cm, allow_small_or_imprecise_dtypes=True), [], w)
         else: op("g", lambda: g.iota(out, pat, base, cm), [], w)
 
-    def zero(ap, w): iota(ap, [[0, ap.shape[1]]], 0, 0, w)
-
     peer = [T.cores[rank ^ m] for m in MASKS]
     for r in range(ROUNDS):
         arrives(peer[r], "t%d" % r, ["tland%d" % r])
         arrives(peer[r], "l%d" % r, ["lland%d" % r])
+        if r: arrives(peer[r], "i%d" % r, ["iland%d" % r])
         for k in range(2):
             arrives(peer[r], "c%d%d" % (k, r), ["ql%d.%d" % (r, k)])
             arrives(peer[r], "s%d%d" % (k, r), ["sl%d.%d" % (r, k)])
 
     dma("s", "ld0", si("dli"), T.dl[:, :], [], ["dli"])
-    dma("y", "ld2", T.x0[:, 0:2 * C], T.x[:, 0:2 * C], [], ["x0"])
-    dma("s", "ld1", si("nli"), T.nl[:, :], [], ["nli"])
-    dma("y", "ld3", T.x0[:, 2 * C:4 * C], T.x[:, 2 * C:4 * C], [], ["x0b"])
     dma("y", "ld4", T.ub[:, :], T.u[:, :], [], ["ub"])
+    dma("s", "ld1", si("nli"), T.nl[:, :], [], ["nli"])
+    for h, (lo, hi) in enumerate(HALF): dma("y", "ld%d" % (2 + h), T.x0[:, 4 * lo:4 * hi], T.x[:, 4 * lo:4 * hi], [], ["x0.%d" % h])
+    iota(whole("qi"), [[1, 16], [16, K]], 0, 0, ["qi1", "qi9"], False)
+    iota(si("ip"), [[0, K]], 0, 1, ["ip"], False)
+    iota(whole("c16"), [[1, 16]], 0, 0, ["c16"])
+    iota(si("ib"), [[16, K]], 0, 0, ["ib"], False)
+    iota(sm("glo"), [[0, K // 2], [1, 2]], 0, 0, ["glo"])
+    dma("s", "ld8", row("qi", 9), T.dl[:, :], [], ["qi9"])
+    dma("s", "ld9", row("qi", 1), T.nl[:, :], [], ["qi1"])
+    fill(whole("mw"), 1.0, ["mw0", "mw1"])
+    scan(whole("iotaS"), whole("mw"), whole("mw"), ["mw0", "mw1"], ["iotaS"], -1.0)
+    ts1(si("i1"), si("ip"), 15, A.bitwise_and, ["ip"], ["i1"])
+    cp(cl("pq"), si("i1", 1), ["i1"], ["pq"])
+    ts1(whole("ind"), whole("c16"), cl("pq"), A.is_equal, ["c16", "pq"], ["ind"])
+    tt(sm("xw"), si("i1"), si("ib"), A.add, ["i1", "ib"], ["xw"])
+    cp(whole("uW"), si("ib", 8), ["ib"], ["uW"])
+
+    def ind(q): return T.ind[:, q:q + 1]
+    def lin(n, src, skey, a, b): act(cl(n), src, [skey], [n], scale=a, bias=b)
+    tt(cl("c1"), ind(5), ind(9), A.add, ["ind"], ["c1"])
+    tt(cl("c2"), ind(4), ind(8), A.add, ["ind"], ["c2"])
+    ts1(si("i2"), si("dli"), 4, A.arith_shift_right, ["dli"], ["i2"])
+    ts1(sm("t2"), si("dli"), float(K), A.mult, ["dli"], ["t2"])
+    cp(sl("ln0", 0), si("dli"), ["dli"], ["ln0"])
+    ts1(sm("t1"), si("i2"), float(1 - C), A.mult, ["i2"], ["t1"])
+    tt(sl("ln0", 1), sm("t1"), sm("t2"), A.add, ["t1", "t2", "ln0"], ["ln0"])
+    send(peer[0], "l0", whole("lland0"), sl("ln0", 0, 2), ["ln0"])
+    cp(sl("uw0", 0, 2), sl("ln0", 0, 2), ["ln0"], ["uw0"])
+    lin("sQ", cl("c1"), "c1", E1, 0.0)
+    lin("bQ", cl("c1"), "c1", E0 - BIG, BIG)
+    lin("s0", ind(1), "ind", E1, 0.0)
+    lin("c3", cl("c2"), "c2", -2 * BIG, BIG)
+    lin("c4", ind(1), "ind", E0 - BIG, 0.0)
+    lin("bW", ind(8), "ind", -BIG, BIG)
+    tt(cl("sS"), cl("c2"), ind(0), A.add, ["c2", "ind"], ["sS"])
+    tt(cl("b0"), cl("c3"), cl("c4"), A.add, ["c3", "c4"], ["b0"])
+    lin("bS", cl("sS"), "sS", -BIG, BIG)
+    act(whole("mp"), whole("iotaS"), ["iotaS", "s0", "b0"], ["mp"], scale=cl("s0"), bias=cl("b0"))
+    ts2(si("i3"), sm("xw"), -0.5 * (K - 1), A.add, 1.0 / K, A.mult, ["xw"], ["i3"])
+    ts1(sm("t4"), sm("xw"), 16.0, A.mult, ["xw"], ["t4"])
+    ts1(sm("t3"), si("i3"), float(1 - C), A.mult, ["i3"], ["t3"])
+    tt(sm("t3"), sm("t3"), sm("t4"), A.add, ["t3", "t4"], ["t3"])
+    cp(whole("cpW"), sm("t3"), ["t3"], ["cpW"])
+    quant(T.qu[:, :], T.su[:, :], T.ub[:, :], ["ub"], ["qu"])
+    cp(whole("qu2").bitcast(dt.uint32), whole("qu").bitcast(dt.uint32).indirect(whole("uW")), ["qu", "uW"], ["qu2"])
+    op("s", lambda: g.scalar.activation(whole("su2"), whole("su").indirect(whole("uW")), CP), ["qu", "uW"], ["su2"])
+    ts2(whole("m1"), whole("qi"), cl("sQ"), A.mult, cl("bQ"), A.add, ["qi1", "qi9", "sQ", "bQ"], ["m1"])
+    tt(whole("lrow"), whole("m1").indirect(sl("uw0", 1)), whole("mp"), A.min, ["m1", "uw0", "mp"], ["lrow"])
+    cp(whole("ep"), whole("qi"), ["qi1", "qi9"], keys("ep"))
+
+    def cube(r):
+        gat("l2", "lrow", sl("uw%d" % r, 0), ["uw%d" % r])
+        gat("d3p", "l2", whole("cpW"), ["cpW"], scale=1.0 / E1, bias=-E0 / E1)
+        dma("y", "md3", sm("d3"), row("d3p", 9), ["d3p"], ["d3"])
+
+    def scores(r, h):
+        lo, hi = HALF[h]
+        quant(T.qx[:, lo:hi], T.sx[:, lo:hi], T["x%d" % r][:, 4 * lo:4 * hi], ["x%d.%d" % (r, h)], ["qx%d" % h])
+        a, sa, ka = ("qu2", "su2", ["qu2", "su2"]) if r < ROUNDS else ("qv", "sv_", ["qv"])
+        for b in range(2 if r < ROUNDS else 1):
+            k = 2 * h + b
+            mm(T.pd[:, 512 * k:512 * k + hi - lo], whole(a), whole(sa), T.qx[:, lo:hi], T.sx[:, lo:hi], ka + ["qx%d" % h], ["Pd%d" % k])
+
+    def late_constants():
+        ts2(si("i1"), si("ip"), 4, A.arith_shift_right, 1, A.bitwise_and, ["ip"], ["i1"])
+        ts1(si("i2"), si("ip"), 31, A.bitwise_and, ["ip"], ["i2"])
+        ts1(sm("t1"), sm("glo"), -16.0, A.mult, ["glo"], ["t1"])
+        tt(sm("mask"), si("i1"), sm("glo"), A.is_equal, ["i1", "glo"], ["mask"])
+        tt(sm("t2"), si("i2"), si("ib"), A.add, ["i2", "ib"], ["t2"])
+        tt(sm("inv"), si("i1"), sm("glo"), A.not_equal, ["i1", "glo"], ["inv"])
+        tt(sm("iotaT"), sm("t1"), sm("t2"), A.add, ["t1", "t2"], ["iotaT"])
+        for b, s in (("m56", "mask"), ("i56", "inv")):
+            act(T[b][:, 0:2 * K:2], sm(s), [s], [b + "a"], scale=1.0 / E1)
+            act(T[b][:, 1:2 * K:2], sm(s), [s], [b])
+        act(sm("iotaE"), sm("iotaT"), ["iotaT"], ["iotaE"], scale=E1, bias=E0)
+        lin("s3", ind(13), "ind", -1.0, 1.0)
+        tt(cl("sL"), cl("sQ"), cl("s0"), A.add, ["sQ", "s0"], ["sL"])
+        tt(cl("bL"), cl("b0"), cl("bQ"), A.min, ["b0", "bQ"], ["bL"])
+
+    def zero(ap, w): iota(ap, [[0, ap.shape[1]]], 0, 0, w)
+
+    def invert(off, okey):
+        op("v", lambda: g.vector.tensor_copy(whole("fi").indirect(off), whole("iotaS")), [okey, "iotaS"], ["fi"])
+
+    def e_row(r): dma("y", "mep", row("ep", 9), sl("lland%d" % r, 0), ["lland%d" % r], ["ep9"])
+    def e_list(r): cp(whole("eW"), whole("lland%d" % r), ["lland%d" % r], ["eW"])
+    def e_first(): gat("e1", "ep", sl("eW", 1), ["eW", "b1"], bias=cl("b1"))
+    def e_rest():
+        act(whole("e2"), whole("e1").indirect(sl("eW", 0)), ["e1", "e11", "eW"], ["e2"], bias=NZ)
+        gat("e3p", "e2", whole("npW"), ["npW"], bias=-3 * NZ)
+        dma("y", "me2", row("e1", 1), row("e2", 9), ["e2"], ["e11"])
+        dma("y", "me3", sm("e3"), row("e3p", 9), ["e3p"], ["e3"])
+
+    def mates(r):
+        gat("m1", "ei", sl("uw%d" % r, 1), ["uw%d" % r])
+        gat("mn", "m1", whole("npW"), ["npW"])
+        for i, q in enumerate((5, 9, 1)): dma("y", "mmn", sl("lb", i), row("mn", q), ["mn"], ["lb%d" % i])
+        gat("mp", "m1", whole("cpW"), ["cpW"])
+        dma("y", "mmp", sl("ln%d" % r, 2), row("mp", 1), ["mp"], ["ln%dm" % r])
+
+    cube(0)
+    scores(0, 0)
+    cp(whole("mn"), whole("qi").indirect(whole("cpW")), ["qi1", "qi9", "cpW"], ["mn"])
+    dma("y", "mnp", sm("np"), row("mn", 1), ["mn"], ["np"])
+    act(whole("ei"), whole("ep"), keys("ep"), keys("ei"))
+    act(cl("c3"), ind(9), ["ind", "c1"], ["c3"], scale=1.0, bias=cl("c1"))
+    lin("b1", cl("c3"), "c3", NZ, 0.0)
+    e_row(0)
+    dma("y", "mx9", row("ei", 9), row("iotaS", 9), ["iotaS"], ["ei9"])
     dma("y", "ld5", T.qw[:, :].bitcast(dt.uint8), T.wc[:, :], [], ["qw"])
     dma("y", "ld6", T.sw[:, :], T.ws[:, :], [], ["sw"])
     dma("y", "ld7", T.vb[:, :], T.v[:, :], [], ["vb"])
-    lastw["x0"] = [("ld2", 16), ("ld3", 16)]
-
-    iota(si("ip"), [[0, K]], 0, 1, ["ip"], False)
-    iota(sm("glo"), [[0, K // 2], [1, 2]], 0, 0, ["glo"])
-    iota(si("ib"), [[32, K // 2], [0, 2]], 0, 0, ["ib"], False)
-    zero(T.ta0[:, :], ["ta0"])
-    zero(T.tbb[:, :], ["tbb"])
-    for b in ("tfb", "r480"): fill(T[b][:, :], 0.0, [b])
-    ts2(si("i1"), si("ip"), 4, A.arith_shift_right, 1, A.bitwise_and, ["ip"], ["i1"])
-    cp(sm("par"), si("i1"), ["i1"], ["par"])
-    tt(sm("mask"), sm("par"), sm("glo"), A.is_equal, ["par", "glo"], ["mask"])
-    tt(sm("inv"), sm("par"), sm("glo"), A.not_equal, ["par", "glo"], ["inv"])
-    ts1(si("i2"), si("ip"), 31, A.bitwise_and, ["ip"], ["i2"])
-    tt(sm("iotaT"), si("i2"), si("ib"), A.add, ["i2", "ib"], ["iotaT"])
-
-    def swap(t, s, u, vals, outs):
-        for q, (v, k) in enumerate(vals): cp(col(t, q), v, k, [t])
-        tr(T[s][:, 16:16 + C], T[t][:, :], [t], [s])
-        tr(T[u][:, :], T[s][:, :], [s], [u])
-        for q, ((v, k), (o, ok)) in enumerate(zip(vals, outs)):
-            tt(sm("V1b"), v, sm("mask"), A.mult, k + ["mask"], ["V1b"])
-            tt(sm("Ub"), shifted(u, q), sm("inv"), A.mult, [u, "inv"], ["Ub"])
-            tt(o, sm("V1b"), sm("Ub"), A.add, ["V1b", "Ub"], ok)
-
-    cp(T.dW[:, :], si("dli"), ["dli"], ["dW"])
-    cp(T.lsend0[:, K:2 * K], si("dli"), ["dli"], ["ls0w"])
-    cp(T.nW[:, :], si("nli"), ["nli"], ["nW"])
-    cp(sm("wn"), si("nli"), ["nli"], ["wn"])
-    swap("tfb", "r480", "f480", [(T.lsend0[:, K:2 * K], ["ls0w"]), (sm("wn"), ["wn"])], [(sm("dT"), ["dT"]), (sm("nT"), ["nT"])])
-    cp(T.lsend0[:, 0:K], sm("dT"), ["dT"], ["ls0t"])
-    send(peer[0], "l0", T.lland0[:, :], T.lsend0[:, :], ["ls0w", "ls0t"])
-    quant(T.qu[:, :], T.su[:, :], T.ub[:, :], ["ub"], ["qu"])
-    zero(T.ca[:, :], ["ca%d" % i for i in range(7)])
-    zero(T.tcb[:, :], ["tcb"])
-    cp(col("ta0", 4), sm("iotaT"), ["iotaT"], ["ta0"])
-    fill(T.tm[:, :], 1e29, ["tm"])
-
-    def late_constants():
-        zero(T.s480[:, :], ["s480"])
-        iota(T.iotaS[:, :], [[1, C]], 0, 0, ["iotaS"])
-        iota(T.c16[:, :], [[0, K], [1, 16]], 0, 0, ["c16"])
-        fill(T.one[:, :], 1.0, ["one"])
-        for b in range(4):
-            op("g", lambda: g.affine_select(T["et%d" % b][:, :], T.one[:, :], [[-1, 512]], A.is_equal, 0.0, b, 4), ["one"], ["et%d" % b])
-        ts1(sm("i512"), sm("iotaT"), float(NB), A.mult, ["iotaT"], ["i512"])
-        ts1(si("i1"), si("ip"), 15, A.bitwise_and, ["ip"], ["i1"])
-        cp(T.pq[:, :], T.si[:, K * ISLOTS.index("i1"):K * ISLOTS.index("i1") + 1], ["i1"], ["pq"])
-        ts1(T.m16[:, :], T.c16[:, :], T.pq[:, :], A.is_equal, ["c16", "pq"], ["m16"])
-        ts1(T.rst[:, :], T.c16[:, :], 0.0, A.not_equal, ["c16"], ["rst"])
-
-    def pick16(win, off, wkeys):
-        tt(T.gm[:, :], win.indirect(off), T.m16[:, :], A.mult, wkeys + ["m16"], ["gm"])
-
-    def fold16(out, okey):
-        op("v", lambda: g.vector.tensor_tensor_scan(T.sc[:, :], T.rst[:, :], T.gm[:, :], 0.0, A.mult, A.add), ["rst", "gm"], ["sc"])
-        cp(out, T.sc[:, 15:C:16], ["sc"], [okey])
-
-    def partner_list(r):
-        cp(T.eW[:, :], T["lland%d" % r][:, K:2 * K], ["lland%d" % r], ["eW"])
-        tt(sm("eo"), T["lland%d" % r][:, 0:K], sm("iotaT"), A.subtract, ["lland%d" % r, "iotaT"], ["eo"])
-        ts2(col("tbb", 8), sm("eo"), float(NB), A.mult, float(NK), A.add, ["eo"], ["tbb"])
-
-    def invert(): op("v", lambda: g.vector.tensor_copy(T.einv[:, :].indirect(T.eW[:, :]), T.iotaS[:, :]), ["eW", "iotaS"], ["einv"])
+    scores(0, 1)
+    for b in ("tbb", "tcb"): zero(whole(b), [b + k for k in ("", "s", "d")])
 
     for r in range(ROUNDS):
         p = peer[r]
+        last = r == ROUNDS - 1
         X, XN = "x%d" % r, "x%d" % (r + 1)
-        ll, lk = T["lland%d" % r], "lland%d" % r
-        quant(T.qx[:, :], T.sx[:, :], T[X][:, :], [X], ["qx"])
-        mm(T.pd[:, 0:C], T.qu[:, :], T.su[:, :], T.qx[:, :], T.sx[:, :], ["qu", "qx"], ["Pd0"])
-        tt(col("ta0", 8), sm("iotaT"), sm("dT"), A.subtract, ["iotaT", "dT"], ["ta0"])
-        tt(sm("nd"), sm("nT"), sm("dT"), A.subtract, ["nT", "dT"], ["nd"])
-        if r: partner_list(r)
-        if OPT["scat"] == 4: invert()
-        for t in range(4): act(T.xp[:, C * t:C * t + C], T[X][:, t:4 * C:4], [X], ["xp%d" % t], 0.5)
-        tr(T.ts[:, :], T.pd[:, 0:C], ["Pd0"], ["ts"])
-        if OPT["ssend"]: act(T["tsend%d" % r][:, :], col("ts", 0), ["ts"], ["tsend%d" % r])
-        else: cp(T["tsend%d" % r][:, :], col("ts", 0), ["ts"], ["tsend%d" % r])
-        send(p, "t%d" % r, T["tland%d" % r][:, :], T["tsend%d" % r][:, :], ["tsend%d" % r])
-        cp(col("ta0", 0), col("ts", 0), ["ts"], ["ta0"])
-        cp(col("tm", 0), col("ts", 0), ["ts"], ["tm"])
-        tr(T.sa0[:, :], T.ta0[:, :], ["ta0"], ["sa0"])
-        tr(T.mi[:, :], T.tm[:, :], ["tm"], ["mi"])
+        uw, uwn, ln, lnn = "uw%d" % r, "uw%d" % (r + 1), "ln%d" % r, "ln%d" % (r + 1)
+        dW = sl(uw, 0)
+        for h, (lo, hi) in enumerate(HALF):
+            tt(T.mi[:, lo:hi], T.pd[:, 1024 * h:1024 * h + hi - lo], T.lrow[:, lo:hi], A.max, ["Pd%d" % (2 * h), "lrow"], ["mi%d" % h])
+        for b, s, sk, o in (("mw", ind(8), "ind", "bW"), ("ms", cl("sS"), "sS", "bS")):
+            for h, (lo, hi) in enumerate(HALF):
+                act(T[b][:, lo:hi], T.pd[:, 1024 * h + 512:1024 * h + 512 + hi - lo], ["Pd%d" % (2 * h + 1), sk, o], [b + str(h)], scale=s, bias=cl(o))
+        tt(whole("o1"), whole("mw").indirect(dW), whole("mi"), A.min, ["mw0", "mw1", uw, "mi0", "mi1"], ["o1"])
+        if r == 0:
+            e_list(0)
+            e_first()
+            cp(whole("npW"), sm("np"), ["np"], ["npW"])
+        tt(whole("o2"), whole("o1").indirect(dW), whole("ms"), A.min, ["o1", uw, "ms0", "ms1"], ["o2"])
+        tr(whole("to2"), whole("o2"), ["o2"], ["to2"])
+        for i in range(3): cp(sl("tsend%d" % r, i), col("to2", 4 * i), ["to2"], ["tsend%d.%d" % (r, i)])
+        send(p, "t%d" % r, whole("tland%d" % r), whole("tsend%d" % r), ["tsend%d.%d" % (r, i) for i in range(3)])
+        cp(whole("d3W"), sm("d3"), ["d3"], ["d3W"])
 
-        def rows(i): dma("y", "da", T.ca[i:128:8, :], T["sa%d" % i][0:128:8, :], ["sa%d" % i], ["ca%d" % i])
-        rows(0)
-        for i in range(1, 6):
-            if i == OPT["exp"]:
-                if r == 0: partner_list(0)
-                cp(col("tbb", 0), T["tland%d" % r][:, :], ["tland%d" % r], ["tbb"])
-                tr(T.sb0[:, :], T.tbb[:, :], ["tbb"], ["sb0"])
-            tt(T["sa%d" % i][:, :], T["sa%d" % (i - 1)][:, :].indirect(T.dW[:, :]), T.mi[:, :], A.min, ["sa%d" % (i - 1), "dW", "mi"], ["sa%d" % i])
-            rows(i)
-        dma("y", "da", T.ca[6:128:16, :], T.sa5[4:128:16, :], ["sa5"], ["ca6"])
-        cp(sl("bm", 0), T["tland%d" % r][:, :], ["tland%d" % r], ["bm0"])
-        if OPT["scat"] == 1: invert()
-        for j in range(1, 6): act(T["sb%d" % j][:, :], T["sb%d" % (j - 1)][:, :].indirect(T.eW[:, :]), ["sb%d" % (j - 1), "eW"], ["sb%d" % j])
-        act(T.can[:, :], T.ca[:, :].indirect(T.nW[:, :]), ["nW"] + ["ca%d" % i for i in range(7)], ["can"])
-
-        def tb_(j): tr(T["tb%d" % j][:, :], T["sb%d" % j][:, :], ["sb%d" % j], ["tb%d" % j])
-        def bm_(j): tt(sl("bm", j), sl("bm", j - 1), col("tb%d" % j, 0), A.min, ["bm%d" % (j - 1), "tb%d" % j], ["bm%d" % j])
-        def pp_(j):
-            b = "tb%d" % j if j else "tbb"
-            tt(sl("pp", j), col(b, 8), col("tac", 13 - j), A.add, [b, "tac"], ["pp%d" % j])
-        def h_(j): tt(sl("hw", j), col("tac", 5 - j), sl("bm", j), A.is_le, ["tac", "bm%d" % j], ["hw%d" % j])
-        if r == 0: late_constants()
-        for j in range(1, OPT["can"]): tb_(j)
-        for j in range(1, OPT["can"]): bm_(j)
-        if OPT["scat"] == 0: invert()
-        tr(T.tac[:, :], T.can[:, :], ["can"], ["tac"])
-        tt(sm("pk"), sm("i512"), col("tac", 6), A.add, ["i512", "tac"], ["pk"])
-        for j in range(0, OPT["can"]):
-            pp_(j)
-            h_(j)
-        tt(sm("pk2"), sm("pk"), col("tac", 13), A.subtract, ["pk", "tac"], ["pk2"])
-        for j in range(OPT["can"], 6):
-            tb_(j)
-            bm_(j)
-            pp_(j)
-            h_(j)
-        tt(T.hpw[:, :], T.hw[:, :], T.pp[:, :], A.mult, ["%s%d" % (b, j) for b in ("hw", "pp") for j in range(6)], ["hpw"])
-        tt(T.x84[:, :], sl("hpw", 0, 3), sl("hpw", 3, 3), A.add, ["hpw"], ["x84"])
-        tt(sm("P"), sl("x84", 0), sl("x84", 1), A.add, ["x84"], ["P"])
-        tt(sm("hp"), sl("x84", 2), sm("pk2"), A.add, ["x84", "pk2"], ["hp"])
-        tt(col("tcb", 0), sm("P"), sm("hp"), A.add, ["P", "hp"], ["tcb"])
-        tr(T.spk[:, :], T.tcb[:, :], ["tcb"], ["spk"])
-        act(T.s480[:, 16:16 + C], T.spk[:, :].indirect(T.nW[:, :]), ["spk", "nW"], ["s480"])
-        if OPT["scat"] == 2: invert()
-        tr(T.te[:, :], T.s480[:, 16:16 + C], ["s480"], ["te"])
-        tr(T.t480[:, :], T.s480[:, :], ["s480"], ["t480"])
-        tt(sm("V1"), col("te", 0), sm("mask"), A.mult, ["te", "mask"], ["V1"])
-        tt(sm("U"), shifted("t480", 0), sm("inv"), A.mult, ["t480", "inv"], ["U"])
-        tt(si("W"), sm("V1"), sm("U"), A.add, ["V1", "U"], ["W"])
-        ts1(si("i1"), si("W"), NB - 1, A.bitwise_and, ["W"], ["i1"])
-        cp(T.aW[:, :], si("i1"), ["i1"], ["aW"])
-        ts2(si("i2"), si("W"), 9, A.arith_shift_right, NB - 1, A.bitwise_and, ["W"], ["i2"])
-        cp(T.bW[:, :], si("i2"), ["i2"], ["bW"])
+        def planes():
+            for t in range(4): act(T.xp[:, C * t:C * t + C], T[X][:, t:4 * C:4], [X + ".0", X + ".1"], ["xp%d" % t], 0.5)
+        if r == 0:
+            cp(whole("nW"), si("nli"), ["nli"], ["nW"])
+            e_rest()
+            gat("g3o", "o2", whole("d3W"), ["d3W"])
+            late_constants()
+            invert(sl("eW", 1), "eW")
+            dma("y", "mei", row("ei", 1), row("fi", 1), ["fi"], ["ei1"])
+            planes()
+            cp(col("tbb", 13), sm("iotaT"), ["iotaT"], ["tbb"])
+            zero(whole("fl"), ["fl0", "fl1"])
+            zero(whole("da"), ["da"])
+            zero(T.s480[:, 0:16], ["s480"])
+            zero(T.s480[:, 16 + C:32 + C], ["s480"])
+            fill(T.one[:, :], 1.0, ["one"])
+            for b in range(4):
+                op("g", lambda: g.affine_select(T.et[:, 512 * b:512 * b + 512], T.one[:, :], [[-1, 512]], A.is_equal, 0.0, b, 4), ["one"], ["et%d" % b])
+        else:
+            e_rest()
+            gat("g3o", "o2", whole("d3W"), ["d3W"])
+            planes()
+        tr(whole("tg3o"), whole("g3o"), ["g3o"], ["tg3o"])
+        for i in range(3): tt(sm("A%d" % (3 + i)), col("to2", 8), col("tg3o", 4 * i), A.min, ["to2", "tg3o"], ["A%d" % (3 + i)])
+        pw = [(sm("iotaE"), "iotaE")] + [(col(b, q), b) for b in ("to2", "tg3o") for q in (1, 5, 9)]
+        for i in range(6): tt(slot("da", i // 3, i % 3), pw[i][0], pw[i + 1][0], A.subtract, [pw[i][1], pw[i + 1][1], "da"], ["da%d" % i])
+        ts1(slot("da", 1, 3), pw[6][0], E0, A.subtract, ["tg3o", "da"], ["da6"])
+        tr(whole("te"), whole("e1"), keys("e1"), ["te"])
+        tt(col("tbb", 1), col("te", 1), col("te", 9), A.subtract, ["te", "tbbd"], ["tbbd0"])
+        tt(col("tbb", 5), col("te", 9), col("te", 5), A.subtract, ["te", "tbbd"], ["tbbd1"])
+        tt(col("tbb", 9), col("te", 5), sm("iotaT"), A.subtract, ["te", "iotaT", "tbbd"], ["tbbd2"])
+        cp(whole("e3W"), sm("e3"), ["e3"], ["e3W"])
+        if r: dma("y", "mei", row("ei", 1), whole("iland%d" % r), ["iland%d" % r], ["ei1"])
+        for i in range(3): cp(col("tbb", 4 * i), sl("tland%d" % r, i), ["tland%d" % r, "tbbs"], ["tbbs%d" % i])
+        tr(whole("sb"), whole("tbb"), ["tbb"] + ["tbb%s%d" % (k, i) for k in "sd" for i in range(3)], ["sb"])
+        gat("g3", "sb", whole("e3W"), ["e3W", "s3"], scale=cl("s3"), bias=0.0)
+        cp(whole("g0"), whole("sb").indirect(whole("nW")), ["sb", "nW"], ["g0"])
+        mates(r)
+        tr(whole("tg0"), whole("g0"), ["g0"], ["tg0"])
+        for j in range(3): tt(slot("fl", 1, 3 - j), sm("A%d" % (5 - j)), col("tg0", 4 * j), A.is_le, ["A%d" % (5 - j), "tg0", "fl1"], ["h%d" % j])
+        tr(whole("tg3"), whole("g3"), ["g3"], ["tg3"])
+        scan(sl("rb", 4, 4), sl("fl", 4, 4), T.tg0[:, 1:C:4], ["h0", "h1", "h2", "tg0"], ["rb1"])
+        for j in range(3): tt(sm("B%d" % (3 + j)), col("tg0", 8), col("tg3", 4 * j), A.min, ["tg0", "tg3"], ["B%d" % (3 + j)])
+        for j in range(3): tt(slot("fl", 0, 3 - j), col("to2", 8 - 4 * j), sm("B%d" % (3 + j)), A.is_le, ["to2", "B%d" % (3 + j), "fl0"], ["h%d" % (3 + j)])
+        scan(sl("rb", 0, 4), sl("fl", 0, 4), T.tg3[:, 1:C:4], ["h3", "h4", "h5", "tg3"], ["rb0"])
+        scan(whole("ra"), whole("fl"), whole("da"), ["h%d" % j for j in range(6)] + ["da%d" % i for i in range(7)], ["ra"])
+        tt(col("tcb", 8), slot("rb", 0, 3), slot("rb", 1, 3), A.add, ["rb0", "rb1", "tcb"], ["tcbs"])
+        tt(col("tcb", 0), slot("ra", 0, 3), slot("ra", 1, 3), A.add, ["ra", "tcb"], ["tcbd"])
+        tr(T.s480[:, 16:16 + C], whole("tcb"), ["tcbs", "tcbd"], ["s480"])
+        act(whole("kn"), T.s480[:, 16:16 + C].indirect(whole("npW")), ["s480", "npW"], ["kn"])
+        dma("y", "mkn", sm("pbn"), row("kn", 8), ["kn"], ["pbn"])
+        tr(whole("t480"), whole("s480"), ["s480"], ["t480"])
+        tt(whole("v56"), T.tcb[:, 0:C:8], whole("m56"), A.mult, ["tcbs", "tcbd", "m56", "m56a"], ["v56"])
+        tt(whole("u56"), T.t480[:, 16:16 + C:8], whole("i56"), A.mult, ["t480", "i56", "i56a"], ["u56"])
+        tt(whole("w56"), whole("v56"), whole("u56"), A.add, ["v56", "u56"], ["w56"])
+        cp(whole("aW"), T.w56[:, 0:2 * K:2], ["w56"], ["aW"])
+        ts1(si("bi"), T.w56[:, 1:2 * K:2], int(NZ) - 1, A.bitwise_and, ["w56"], ["bi"])
+        cp(whole("bW"), si("bi"), ["bi"], ["bW"])
 
         def gather_a(k, t):
             lo, hi = CHZ[k]
@@ -332,6 +400,15 @@ def rank_program(g, core, T, topo):
             if q == "s": act(dst, src, [pk_], ["hh%d%d" % (k, i)], 0.03125)
             else: ts1(dst, src, 0.03125, A.mult, [pk_], ["hh%d%d" % (k, i)])
 
+        def edit():
+            tt(si("is"), T.w56[:, 1:2 * K:2], sm("pbn"), A.add, ["w56", "pbn"], ["is"])
+            tt(whole("df"), whole("lb"), whole(ln), A.subtract, ["lb0", "lb1", "lb2", ln, ln + "m"], ["df"])
+            ts2(si("odd"), si("is"), 10, A.arith_shift_right, 1, A.bitwise_and, ["is"], ["odd"])
+            for i in range(3): tt(sl("pr", i), sl("df", i), si("odd"), A.mult, ["df", "odd"], ["pr%d" % i])
+            tt(whole(lnn), whole(ln), whole("pr"), A.add, [ln, ln + "m", "pr0", "pr1", "pr2"], [lnn, lnn + "m"])
+            cp(whole(uwn), whole(lnn), [lnn, lnn + "m"], [uwn])
+            if not last: dma("y", "mq9", row("q", 9), sl(lnn, 0), [lnn], ["q9"])
+
         for k in range(2):
             for t in range(4): gather_a(k, t)
         for t in range(4): add_b(0, t)
@@ -340,53 +417,53 @@ def rank_program(g, core, T, topo):
         layer(192, 336, "pd", "qz", "sz", 0, [1], "qz1")
         for i in range(4): evac(0, i, "s")
         pack(0)
+        if OPT["fpos"] == 0: edit()
         for i in range(4): evac(1, i, "vs"[i % 2])
         for t in range(4): gather_a(2, t)
         pack(1)
-
-        def own_part():
-            for t in range(4): add_b(2, t)
-            layer(OWN[0], OWN[1], "ph", "qo", "so", OWN[0], [1, 2], "qo")
-            for i in range(4): act(T.jp[:, C * i + F:C * i + C], T.ph[:, 512 * i + F - OWN[0]:512 * i + C - OWN[0]], ["Ph%d" % i], ["jp%dh" % i], 0.03125)
-        if OPT["z3"] == 1: own_part()
-        tt(si("is"), col("tcb", 0), col("te", 0), A.add, ["tcb", "te"], ["is"])
-        tt(sm("df"), sm("nd"), col("tac", 8), A.subtract, ["nd", "tac"], ["df"])
-        ts2(si("odd"), si("is"), 19, A.arith_shift_right, 1, A.bitwise_and, ["is"], ["odd"])
-        tt(sm("dfo"), sm("df"), si("odd"), A.mult, ["df", "odd"], ["dfo"])
-        tt(sm("dT"), sm("dT"), sm("dfo"), A.add, ["dT", "dfo"], ["dT"])
-        last = r == ROUNDS - 1
-        fw, fk = (sm("wd"), "wd") if last else (T["lsend%d" % (r + 1)][:, K:2 * K], "ls%dw" % (r + 1))
-        if not last: cp(T["lsend%d" % (r + 1)][:, 0:K], sm("dT"), ["dT"], ["ls%dt" % (r + 1)])
-        swap("tfb", "r480", "f480", [(sm("dT"), ["dT"])], [(fw, [fk])])
-        cp(T.dW[:, :], fw, [fk], ["dW"])
+        if r == 0: act(whole("q"), whole("ei"), keys("ei"), keys("q"))
+        if OPT["fpos"] == 1: edit()
+        if not last: send(peer[r + 1], "l%d" % (r + 1), whole("lland%d" % (r + 1)), sl(lnn, 0, 2), [lnn])
+        for t in range(4): add_b(2, t)
+        layer(OWN[0], OWN[1], "ph", "qo", "so", OWN[0], [1, 2], "qo")
+        for i in range(4): act(T.jp[:, C * i + F:C * i + C], T.ph[:, 512 * i + F - OWN[0]:512 * i + C - OWN[0]], ["Ph%d" % i], ["jp%dh" % i], 0.03125)
+        if r == 0: quant(whole("qe"), whole("se_"), whole("et"), ["et%d" % b for b in range(4)], ["qe"])
         if last:
-            dma("y", "st0", T.dn[:, :], T.r480[0:128:16, 16:16 + C], ["r480"], [])
+            quant(T.qv[:, :], T.sv_[:, :], T.vb[:, :], ["vb"], ["qv"])
         else:
-            send(peer[r + 1], "l%d" % (r + 1), T["lland%d" % (r + 1)][:, :], T["lsend%d" % (r + 1)][:, :], ["ls%dw" % (r + 1), "ls%dt" % (r + 1)])
-        if OPT["scat"] == 3: invert()
-        if OPT["z3"] == 0: own_part()
-        pick16(T.einv[:, :], T.dW[:, :], ["einv", "dW"])
-        fold16(T.lW[:, :], "lW")
-        if r == 0:
-            for b in range(4): quant(T.qe[:, 128 * b:128 * b + 128], T.se_[:, 128 * b:128 * b + 128], T["et%d" % b][:, :], ["et%d" % b], ["qe%d" % b])
-        if last: quant(T.qv[:, :], T.sv_[:, :], T.vb[:, :], ["vb"], ["qv"])
+            invert(sl(uwn, 1), uwn)
+            dma("y", "mq1", row("q", 1), row("fi", 1), ["fi"], ["q1"])
+            dma("y", "mis", whole("isend%d" % (r + 1)), row("fi", 0), ["fi"], ["isend"])
+            send(peer[r + 1], "i%d" % (r + 1), whole("iland%d" % (r + 1)), whole("isend%d" % (r + 1)), ["isend"])
+            e_row(r + 1)
         for k, (lo, hi) in enumerate(CH):
             n = hi - lo
             for b in range(4):
                 mm(T[("ph", "pd")[k]][:, 512 * b:512 * b + n], T.qe[:, 128 * b:128 * b + 128], T.se_[:, 128 * b:128 * b + 128], T["ql%d" % r][:, lo:hi], T["sl%d" % r][:, lo:hi],
-                   ["qe%d" % b, "ql%d.%d" % (r, k), "sl%d.%d" % (r, k)], ["P" + "hd"[k] + str(b)])
+                   ["qe", "ql%d.%d" % (r, k), "sl%d.%d" % (r, k)], ["P" + "hd"[k] + str(b)])
             for b in range(4):
                 src, dst, pk_ = T[("ph", "pd")[k]][:, 512 * b:512 * b + n], T.jp[:, C * b + lo:C * b + hi], "P" + "hd"[k] + str(b)
                 if k == 0 or b % 2: act(dst, src, [pk_], ["jp%d%d" % (b, k)])
                 else: cp(dst, src, [pk_], ["jp%d%d" % (b, k)])
-        for t in range(4):
-            tt(T[XN][:, t:4 * C:4], T.jp[:, C * t:C * t + C].indirect(T.lW[:, :]), T[X][:, t:4 * C:4], A.add,
-               ["jp%d0" % t, "jp%d1" % t, "jp%dh" % t, "lW", X], [XN])
+        if last:
+            gat("lrow", "q", sl(uwn, 1), [uwn])
+            dma("y", "st0", T.dn[:, :], row("lrow", 5), ["lrow"], [])
+        else:
+            gat("lrow", "q", sl(uwn, 1), [uwn, "sL", "bL"], scale=cl("sL"), bias=cl("bL"))
+            cube(r + 1)
+        for h, (lo, hi) in enumerate(HALF):
+            if h == 1 and not last:
+                e_list(r + 1)
+                e_first()
+            for t in range(4):
+                tt(T[XN][:, 4 * lo + t:4 * hi:4], T.jp[:, C * t:C * t + C].indirect(T[uwn][:, 2 * K + lo // 16:2 * K + hi // 16]), T[X][:, 4 * lo + t:4 * hi:4], A.add,
+                   ["jp%d0" % t, "jp%d1" % t, "jp%dh" % t, uwn, X + ".%d" % h], [XN + "t%d%d" % (h, t)])
+            lastw[XN + ".%d" % h] = [("qv", count["qv"])]
+            scores(r + 1, h)
+            if last:
+                dma("y", "st%d" % (1 + h), T.oc[:, 4 * lo:4 * hi], T.qx[:, lo:hi].bitcast(dt.uint8), ["qx%d" % h], [])
+                act(T.ysb[:, lo:hi], T.pd[:, 1024 * h:1024 * h + hi - lo], ["Pd%d" % (2 * h)], ["ysb%d" % h])
+                dma("s", "st%d" % (3 + h), T.y[:, lo:hi], T.ysb[:, lo:hi], ["ysb%d" % h], [])
 
-    quant(T.qx[:, :], T.sx[:, :], T.x3[:, :], ["x3"], ["qx"])
-    dma("y", "st1", T.oc[:, :], T.qx[:, :].bitcast(dt.uint8), ["qx"], [])
-    mm(T.pd[:, 0:C], T.qv[:, :], T.sv_[:, :], T.qx[:, :], T.sx[:, :], ["qv", "qx"], ["Pd0"])
-    for k in range(4): dma("y", "st%d" % (2 + k), T.osc[4 * k:4 * k + 4, :], T.sx[32 * k:32 * k + 4, :], ["qx"], [])
-    act(T.ysb[:, :], T.pd[:, 0:C], ["Pd0"], ["ysb"])
-    dma("s", "st6", T.y[:, :], T.ysb[:, :], ["ysb"], [])
+    for k in range(4): dma("y", "st%d" % (5 + k), T.osc[4 * k:4 * k + 4, :], T.sx[32 * k:32 * k + 4, :], ["qx0", "qx1"], [])
     for s in sorted(count): wait("g", (s, count[s]))

@@ -3,16 +3,15 @@ from concourse.mybir import dt, AluOpType, ActivationFunctionType
 C, F, ROUNDS = 448, 336, 3
 K = C // 16
 MASKS = [1, 2, 3]
-HALF = [(0, C // 2), (C // 2, C)]
+RUNS = [(0, 320), (320, C)]
 CH = [(0, 192), (192, 336)]
 CHZ = [(0, 192), (192, 352), (352, 448)]
 OWN = (320, 448)
 NZ = 1024.0
 BIG, E0, E1 = 2.0 ** 90, 2.0 ** 80, 2.0 ** 60
-SLOTS = ["iotaT", "iotaE", "mask", "inv", "par", "glo", "A3", "A4", "A5", "B3", "B4", "B5", "d3", "e3", "np", "pbn", "t1", "t2", "t3", "t4", "xw"]
+SLOTS = ["iotaT", "iotaE", "mask", "inv", "glo", "A3", "A4", "A5", "B3", "B4", "B5", "d3", "e3", "np", "pbn", "t1", "t2", "t3", "t4", "xw"]
 ISLOTS = ["i1", "i2", "i3", "is", "odd", "ip", "ib", "dli", "nli", "bi"]
-COLS = ["pq", "sW", "bW", "sS", "bS", "sL", "bL", "b1", "s3", "sQ", "bQ", "s0", "b0", "c1", "c2", "c3", "c4"]
-OPT = {"fpos": 1, "ew": 2}
+COLS = ["pq", "bW", "sS", "bS", "sL", "bL", "b1", "s3", "sQ", "bQ", "s0", "b0", "c1", "c2", "c3", "c4"]
 
 SCRATCH = {
     "sm": ("sbuf", [128, K * len(SLOTS)], "float32"),
@@ -41,7 +40,7 @@ SCRATCH = {
     "ph": ("psum", [128, 2048], "float32"), "pd": ("psum", [128, 2048], "float32"),
 }
 for _n in ("mw", "mi", "ms", "o1", "o2", "to2", "g3o", "tg3o", "tbb", "sb", "g0", "g3", "tg0", "tg3", "tcb", "kn", "lrow", "l2", "d3p",
-           "q", "fi", "ep", "e1", "e2", "te", "e3p", "ei", "m1", "mn", "mp", "iotaS"):
+           "q", "fi", "ep", "e1", "e2", "te", "e3p", "ei", "m1", "mn", "mp", "iotaS", "ide"):
     SCRATCH[_n] = ("sbuf", [128, C], "float32")
 for _n in ("s480", "t480"): SCRATCH[_n] = ("sbuf", [128, C + 32], "float32")
 for _n in ("nW", "npW", "cpW", "d3W", "e3W", "aW", "bW"): SCRATCH[_n] = ("sbuf", [128, K], "uint16")
@@ -144,6 +143,7 @@ def rank_program(g, core, T, topo):
     def row(b, q): return T[b][q:128:16, :]
     def slot(b, h, s): return T[b][:, 4 * K * h + s:4 * K * (h + 1):4]
     def whole(b): return T[b][:, :]
+    def ind(q): return T.ind[:, q:q + 1]
 
     def tt(out, a, b, o, r, w): op("v", lambda: g.vector.tensor_tensor(out, a, b, o), r, w)
     def ts1(out, a, s, o, r, w): op("v", lambda: g.vector.tensor_scalar(out, a, s, None, o), r, w)
@@ -155,7 +155,8 @@ def rank_program(g, core, T, topo):
         if bias is not None: op("s", lambda: g.scalar.activation(out, a, ID, bias=bias, scale=scale), r, w)
         elif scale == 1.0: op("s", lambda: g.scalar.activation(out, a, CP), r, w)
         else: op("s", lambda: g.scalar.activation(out, a, CP, scale=scale), r, w)
-    ROWS = {"q": ["", "1", "9"], "ep": ["", "9"], "ei": ["", "1", "9"], "e1": ["", "1"]}
+    def lin(n, src, skey, a, b): act(cl(n), src, [skey], [n], scale=a, bias=b)
+    ROWS = {"q": ["", "9"], "lrow": ["", "1"], "ep": ["", "9"], "ei": ["", "1", "9"], "e1": ["", "1"]}
     def keys(b): return [b + k for k in ROWS.get(b, [""])]
     def gat(out, win, off, r, **kw):
         act(whole(out), whole(win).indirect(off), keys(win) + r, keys(out), **kw)
@@ -165,6 +166,8 @@ def rank_program(g, core, T, topo):
     def iota(out, pat, base, cm, w, f=True):
         if f: op("g", lambda: g.iota(out, pat, base, cm, allow_small_or_imprecise_dtypes=True), [], w)
         else: op("g", lambda: g.iota(out, pat, base, cm), [], w)
+    def zero(ap, w): iota(ap, [[0, ap.shape[1]]], 0, 0, w)
+    PLACES = [[1, 16], [16, K]]
 
     peer = [T.cores[rank ^ m] for m in MASKS]
     for r in range(ROUNDS):
@@ -175,88 +178,20 @@ def rank_program(g, core, T, topo):
             arrives(peer[r], "c%d%d" % (k, r), ["ql%d.%d" % (r, k)])
             arrives(peer[r], "s%d%d" % (k, r), ["sl%d.%d" % (r, k)])
 
-    dma("s", "ld0", si("dli"), T.dl[:, :], [], ["dli"])
-    dma("y", "ld4", T.ub[:, :], T.u[:, :], [], ["ub"])
-    dma("s", "ld1", si("nli"), T.nl[:, :], [], ["nli"])
-    for h, (lo, hi) in enumerate(HALF): dma("y", "ld%d" % (2 + h), T.x0[:, 4 * lo:4 * hi], T.x[:, 4 * lo:4 * hi], [], ["x0.%d" % h])
-    iota(whole("qi"), [[1, 16], [16, K]], 0, 0, ["qi1", "qi9"], False)
-    iota(si("ip"), [[0, K]], 0, 1, ["ip"], False)
-    iota(whole("c16"), [[1, 16]], 0, 0, ["c16"])
-    iota(si("ib"), [[16, K]], 0, 0, ["ib"], False)
-    iota(sm("glo"), [[0, K // 2], [1, 2]], 0, 0, ["glo"])
-    dma("s", "ld8", row("qi", 9), T.dl[:, :], [], ["qi9"])
-    dma("s", "ld9", row("qi", 1), T.nl[:, :], [], ["qi1"])
-    fill(whole("mw"), 1.0, ["mw0", "mw1"])
-    scan(whole("iotaS"), whole("mw"), whole("mw"), ["mw0", "mw1"], ["iotaS"], -1.0)
-    ts1(si("i1"), si("ip"), 15, A.bitwise_and, ["ip"], ["i1"])
-    cp(cl("pq"), si("i1", 1), ["i1"], ["pq"])
-    ts1(whole("ind"), whole("c16"), cl("pq"), A.is_equal, ["c16", "pq"], ["ind"])
-    tt(sm("xw"), si("i1"), si("ib"), A.add, ["i1", "ib"], ["xw"])
-    cp(whole("uW"), si("ib", 8), ["ib"], ["uW"])
-
-    def ind(q): return T.ind[:, q:q + 1]
-    def lin(n, src, skey, a, b): act(cl(n), src, [skey], [n], scale=a, bias=b)
-    tt(cl("c1"), ind(5), ind(9), A.add, ["ind"], ["c1"])
-    tt(cl("c2"), ind(4), ind(8), A.add, ["ind"], ["c2"])
-    ts1(si("i2"), si("dli"), 4, A.arith_shift_right, ["dli"], ["i2"])
-    ts1(sm("t2"), si("dli"), float(K), A.mult, ["dli"], ["t2"])
-    cp(sl("ln0", 0), si("dli"), ["dli"], ["ln0"])
-    ts1(sm("t1"), si("i2"), float(1 - C), A.mult, ["i2"], ["t1"])
-    tt(sl("ln0", 1), sm("t1"), sm("t2"), A.add, ["t1", "t2", "ln0"], ["ln0"])
-    send(peer[0], "l0", whole("lland0"), sl("ln0", 0, 2), ["ln0"])
-    cp(sl("uw0", 0, 2), sl("ln0", 0, 2), ["ln0"], ["uw0"])
-    lin("sQ", cl("c1"), "c1", E1, 0.0)
-    lin("bQ", cl("c1"), "c1", E0 - BIG, BIG)
-    lin("s0", ind(1), "ind", E1, 0.0)
-    lin("c3", cl("c2"), "c2", -2 * BIG, BIG)
-    lin("c4", ind(1), "ind", E0 - BIG, 0.0)
-    lin("bW", ind(8), "ind", -BIG, BIG)
-    tt(cl("sS"), cl("c2"), ind(0), A.add, ["c2", "ind"], ["sS"])
-    tt(cl("b0"), cl("c3"), cl("c4"), A.add, ["c3", "c4"], ["b0"])
-    lin("bS", cl("sS"), "sS", -BIG, BIG)
-    act(whole("mp"), whole("iotaS"), ["iotaS", "s0", "b0"], ["mp"], scale=cl("s0"), bias=cl("b0"))
-    ts2(si("i3"), sm("xw"), -0.5 * (K - 1), A.add, 1.0 / K, A.mult, ["xw"], ["i3"])
-    ts1(sm("t4"), sm("xw"), 16.0, A.mult, ["xw"], ["t4"])
-    ts1(sm("t3"), si("i3"), float(1 - C), A.mult, ["i3"], ["t3"])
-    tt(sm("t3"), sm("t3"), sm("t4"), A.add, ["t3", "t4"], ["t3"])
-    cp(whole("cpW"), sm("t3"), ["t3"], ["cpW"])
-    quant(T.qu[:, :], T.su[:, :], T.ub[:, :], ["ub"], ["qu"])
-    cp(whole("qu2").bitcast(dt.uint32), whole("qu").bitcast(dt.uint32).indirect(whole("uW")), ["qu", "uW"], ["qu2"])
-    op("s", lambda: g.scalar.activation(whole("su2"), whole("su").indirect(whole("uW")), CP), ["qu", "uW"], ["su2"])
-    ts2(whole("m1"), whole("qi"), cl("sQ"), A.mult, cl("bQ"), A.add, ["qi1", "qi9", "sQ", "bQ"], ["m1"])
-    tt(whole("lrow"), whole("m1").indirect(sl("uw0", 1)), whole("mp"), A.min, ["m1", "uw0", "mp"], ["lrow"])
-    cp(whole("ep"), whole("qi"), ["qi1", "qi9"], keys("ep"))
-
-    def cube(r):
-        gat("l2", "lrow", sl("uw%d" % r, 0), ["uw%d" % r])
-        gat("d3p", "l2", whole("cpW"), ["cpW"], scale=1.0 / E1, bias=-E0 / E1)
-        dma("y", "md3", sm("d3"), row("d3p", 9), ["d3p"], ["d3"])
-
     def scores(r, h):
-        lo, hi = HALF[h]
+        lo, hi = RUNS[h]
         quant(T.qx[:, lo:hi], T.sx[:, lo:hi], T["x%d" % r][:, 4 * lo:4 * hi], ["x%d.%d" % (r, h)], ["qx%d" % h])
         a, sa, ka = ("qu2", "su2", ["qu2", "su2"]) if r < ROUNDS else ("qv", "sv_", ["qv"])
         for b in range(2 if r < ROUNDS else 1):
             k = 2 * h + b
             mm(T.pd[:, 512 * k:512 * k + hi - lo], whole(a), whole(sa), T.qx[:, lo:hi], T.sx[:, lo:hi], ka + ["qx%d" % h], ["Pd%d" % k])
 
-    def late_constants():
-        ts2(si("i1"), si("ip"), 4, A.arith_shift_right, 1, A.bitwise_and, ["ip"], ["i1"])
-        ts1(si("i2"), si("ip"), 31, A.bitwise_and, ["ip"], ["i2"])
-        ts1(sm("t1"), sm("glo"), -16.0, A.mult, ["glo"], ["t1"])
-        tt(sm("mask"), si("i1"), sm("glo"), A.is_equal, ["i1", "glo"], ["mask"])
-        tt(sm("t2"), si("i2"), si("ib"), A.add, ["i2", "ib"], ["t2"])
-        tt(sm("inv"), si("i1"), sm("glo"), A.not_equal, ["i1", "glo"], ["inv"])
-        tt(sm("iotaT"), sm("t1"), sm("t2"), A.add, ["t1", "t2"], ["iotaT"])
-        for b, s in (("m56", "mask"), ("i56", "inv")):
-            act(T[b][:, 0:2 * K:2], sm(s), [s], [b + "a"], scale=1.0 / E1)
-            act(T[b][:, 1:2 * K:2], sm(s), [s], [b])
-        act(sm("iotaE"), sm("iotaT"), ["iotaT"], ["iotaE"], scale=E1, bias=E0)
-        lin("s3", ind(13), "ind", -1.0, 1.0)
-        tt(cl("sL"), cl("sQ"), cl("s0"), A.add, ["sQ", "s0"], ["sL"])
-        tt(cl("bL"), cl("b0"), cl("bQ"), A.min, ["b0", "bQ"], ["bL"])
-
-    def zero(ap, w): iota(ap, [[0, ap.shape[1]]], 0, 0, w)
+    def cube(r):
+        gat("lrow", "q", sl("uw%d" % r, 1), ["uw%d" % r, "sL", "bL"], scale=cl("sL"), bias=cl("bL"))
+        gat("l2", "lrow", sl("uw%d" % r, 0), ["uw%d" % r])
+        dma("y", "mq1", row("lrow", 1), row("ide", 1), ["ide"], ["lrow1"])
+        gat("d3p", "l2", whole("cpW"), ["cpW"], scale=1.0 / E1, bias=-E0 / E1)
+        dma("y", "md3", sm("d3"), row("d3p", 9), ["d3p"], ["d3"])
 
     def invert(off, okey):
         op("v", lambda: g.vector.tensor_copy(whole("fi").indirect(off), whole("iotaS")), [okey, "iotaS"], ["fi"])
@@ -265,10 +200,13 @@ def rank_program(g, core, T, topo):
     def e_list(r): cp(whole("eW"), whole("lland%d" % r), ["lland%d" % r], ["eW"])
     def e_first(): gat("e1", "ep", sl("eW", 1), ["eW", "b1"], bias=cl("b1"))
     def e_rest():
-        act(whole("e2"), whole("e1").indirect(sl("eW", 0)), ["e1", "e11", "eW"], ["e2"], bias=NZ)
+        gat("e2", "e1", sl("eW", 0), ["eW"], bias=NZ)
         gat("e3p", "e2", whole("npW"), ["npW"], bias=-3 * NZ)
         dma("y", "me2", row("e1", 1), row("e2", 9), ["e2"], ["e11"])
         dma("y", "me3", sm("e3"), row("e3p", 9), ["e3p"], ["e3"])
+
+    def planes(r, ts):
+        for t in ts: act(T.xp[:, C * t:C * t + C], T["x%d" % r][:, t:4 * C:4], ["x%d.0" % r, "x%d.1" % r], ["xp%d" % t], 0.5)
 
     def mates(r):
         gat("m1", "ei", sl("uw%d" % r, 1), ["uw%d" % r])
@@ -277,19 +215,84 @@ def rank_program(g, core, T, topo):
         gat("mp", "m1", whole("cpW"), ["cpW"])
         dma("y", "mmp", sl("ln%d" % r, 2), row("mp", 1), ["mp"], ["ln%dm" % r])
 
-    cube(0)
-    scores(0, 0)
-    cp(whole("mn"), whole("qi").indirect(whole("cpW")), ["qi1", "qi9", "cpW"], ["mn"])
-    dma("y", "mnp", sm("np"), row("mn", 1), ["mn"], ["np"])
-    act(whole("ei"), whole("ep"), keys("ep"), keys("ei"))
+    def load_x(h): dma("y", "ld%d" % (2 + h), T.x0[:, 4 * RUNS[h][0]:4 * RUNS[h][1]], T.x[:, 4 * RUNS[h][0]:4 * RUNS[h][1]], [], ["x0.%d" % h])
+    dma("s", "ld0", si("dli"), T.dl[:, :], [], ["dli"])
+    dma("y", "ld4", T.ub[:, :], T.u[:, :], [], ["ub"])
+    dma("s", "ld1", si("nli"), T.nl[:, :], [], ["nli"])
+    load_x(1)
+    iota(si("ip"), [[0, K]], 0, 1, ["ip"], False)
+    iota(whole("c16"), [[1, 16]], 0, 0, ["c16"])
+    iota(si("ib"), [[16, K]], 0, 0, ["ib"], False)
+    iota(sm("glo"), [[0, K // 2], [1, 2]], 0, 0, ["glo"])
+    iota(whole("qi"), PLACES, 0, 0, ["qi3", "qi9"], False)
+    dma("y", "ld8", row("qi", 9), T.dl[:, :], [], ["qi9"])
+    dma("y", "ld9", row("qi", 3), T.nl[:, :], [], ["qi3"])
+    load_x(0)
+    fill(whole("mw"), 1.0, ["mw0", "mw1"])
+    scan(whole("iotaS"), whole("mw"), whole("mw"), ["mw0", "mw1"], ["iotaS"], -1.0)
+    ts1(si("i1"), si("ip"), 15, A.bitwise_and, ["ip"], ["i1"])
+    cp(cl("pq"), si("i1", 1), ["i1"], ["pq"])
+    ts1(whole("ind"), whole("c16"), cl("pq"), A.is_equal, ["c16", "pq"], ["ind"])
+    tt(sm("xw"), si("i1"), si("ib"), A.add, ["i1", "ib"], ["xw"])
+    cp(whole("uW"), si("ib", 8), ["ib"], ["uW"])
+    tt(cl("c1"), ind(5), ind(9), A.add, ["ind"], ["c1"])
+    tt(cl("c2"), ind(4), ind(8), A.add, ["ind"], ["c2"])
+    ts2(si("i3"), sm("xw"), -0.5 * (K - 1), A.add, 1.0 / K, A.mult, ["xw"], ["i3"])
+    ts1(sm("t4"), sm("xw"), 16.0, A.mult, ["xw"], ["t4"])
+    ts1(sm("t3"), si("i3"), float(1 - C), A.mult, ["i3"], ["t3"])
+    tt(sm("t3"), sm("t3"), sm("t4"), A.add, ["t3", "t4"], ["t3"])
+    cp(whole("cpW"), sm("t3"), ["t3"], ["cpW"])
+    ts1(si("i2"), si("dli"), 4, A.arith_shift_right, ["dli"], ["i2"])
+    ts1(sm("t2"), si("dli"), float(K), A.mult, ["dli"], ["t2"])
+    cp(sl("ln0", 0), si("dli"), ["dli"], ["ln0"])
+    ts1(sm("t1"), si("i2"), float(1 - C), A.mult, ["i2"], ["t1"])
+    tt(sl("ln0", 1), sm("t1"), sm("t2"), A.add, ["t1", "t2", "ln0"], ["ln0"])
+    send(peer[0], "l0", whole("lland0"), sl("ln0", 0, 2), ["ln0"])
+    cp(sl("uw0", 0, 2), sl("ln0", 0, 2), ["ln0"], ["uw0"])
+    act(cl("sL"), ind(3), ["ind", "c1"], ["sL"], scale=1.0, bias=cl("c1"))
+    lin("sQ", cl("sL"), "sL", E1, 0.0)
+    lin("bQ", cl("sL"), "sL", E0 - BIG, BIG)
+    lin("s0", ind(1), "ind", E1, 0.0)
+    lin("c3", cl("c2"), "c2", -2 * BIG, BIG)
+    lin("c4", ind(1), "ind", E0 - BIG, 0.0)
+    lin("bW", ind(8), "ind", -BIG, BIG)
+    tt(cl("sS"), cl("c2"), ind(0), A.add, ["c2", "ind"], ["sS"])
+    tt(cl("b0"), cl("c3"), cl("c4"), A.add, ["c3", "c4"], ["b0"])
+    lin("bS", cl("sS"), "sS", -BIG, BIG)
+    act(whole("ide"), whole("iotaS"), ["iotaS", "s0", "b0"], ["ide"], scale=cl("s0"), bias=cl("b0"))
+    ts2(si("i1"), si("ip"), 4, A.arith_shift_right, 1, A.bitwise_and, ["ip"], ["i1"])
+    ts1(si("i2"), si("ip"), 31, A.bitwise_and, ["ip"], ["i2"])
+    ts1(sm("t1"), sm("glo"), -16.0, A.mult, ["glo"], ["t1"])
+    tt(sm("mask"), si("i1"), sm("glo"), A.is_equal, ["i1", "glo"], ["mask"])
+    tt(sm("t2"), si("i2"), si("ib"), A.add, ["i2", "ib"], ["t2"])
+    tt(sm("inv"), si("i1"), sm("glo"), A.not_equal, ["i1", "glo"], ["inv"])
+    tt(sm("iotaT"), sm("t1"), sm("t2"), A.add, ["t1", "t2"], ["iotaT"])
+    for b, s in (("m56", "mask"), ("i56", "inv")):
+        act(T[b][:, 0:2 * K:2], sm(s), [s], [b + "a"], scale=1.0 / E1)
+        act(T[b][:, 1:2 * K:2], sm(s), [s], [b])
+    act(sm("iotaE"), sm("iotaT"), ["iotaT"], ["iotaE"], scale=E1, bias=E0)
+    lin("s3", ind(13), "ind", -1.0, 1.0)
+    tt(cl("sL"), cl("sQ"), cl("s0"), A.add, ["sQ", "s0"], ["sL"])
+    tt(cl("bL"), cl("b0"), cl("bQ"), A.min, ["b0", "bQ"], ["bL"])
+    quant(T.qu[:, :], T.su[:, :], T.ub[:, :], ["ub"], ["qu"])
+    cp(whole("qu2").bitcast(dt.uint32), whole("qu").bitcast(dt.uint32).indirect(whole("uW")), ["qu", "uW"], ["qu2"])
+    act(whole("su2"), whole("su").indirect(whole("uW")), ["qu", "uW"], ["su2"])
+    scores(0, 1)
     act(cl("c3"), ind(9), ["ind", "c1"], ["c3"], scale=1.0, bias=cl("c1"))
     lin("b1", cl("c3"), "c3", NZ, 0.0)
+    ts2(whole("m1"), whole("qi"), cl("sQ"), A.mult, cl("bQ"), A.add, ["qi3", "qi9", "sQ", "bQ"], ["m1"])
+    scores(0, 0)
+    tt(whole("lrow"), whole("m1").indirect(sl("uw0", 1)), whole("ide"), A.min, ["m1", "uw0", "ide"], keys("lrow"))
+    iota(whole("ep"), PLACES, 0, 0, keys("ep"))
+    gat("mn", "m1", whole("cpW"), ["cpW"], scale=1.0 / E1, bias=-E0 / E1)
+    dma("y", "mnp", sm("np"), row("mn", 3), ["mn"], ["np"])
     e_row(0)
-    dma("y", "mx9", row("ei", 9), row("iotaS", 9), ["iotaS"], ["ei9"])
     dma("y", "ld5", T.qw[:, :].bitcast(dt.uint8), T.wc[:, :], [], ["qw"])
     dma("y", "ld6", T.sw[:, :], T.ws[:, :], [], ["sw"])
     dma("y", "ld7", T.vb[:, :], T.v[:, :], [], ["vb"])
-    scores(0, 1)
+    planes(0, range(2))
+    iota(whole("ei"), PLACES, 0, 0, keys("ei"))
+    dma("y", "mx9", row("ei", 9), row("iotaS", 9), ["iotaS"], ["ei9"])
     for b in ("tbb", "tcb"): zero(whole(b), [b + k for k in ("", "s", "d")])
 
     for r in range(ROUNDS):
@@ -298,70 +301,77 @@ def rank_program(g, core, T, topo):
         X, XN = "x%d" % r, "x%d" % (r + 1)
         uw, uwn, ln, lnn = "uw%d" % r, "uw%d" % (r + 1), "ln%d" % r, "ln%d" % (r + 1)
         dW = sl(uw, 0)
-        for h, (lo, hi) in enumerate(HALF):
-            tt(T.mi[:, lo:hi], T.pd[:, 1024 * h:1024 * h + hi - lo], T.lrow[:, lo:hi], A.max, ["Pd%d" % (2 * h), "lrow"], ["mi%d" % h])
+        for h, (lo, hi) in enumerate(RUNS):
+            tt(T.mi[:, lo:hi], T.pd[:, 1024 * h:1024 * h + hi - lo], T.lrow[:, lo:hi], A.max, ["Pd%d" % (2 * h)] + keys("lrow"), ["mi%d" % h])
         for b, s, sk, o in (("mw", ind(8), "ind", "bW"), ("ms", cl("sS"), "sS", "bS")):
-            for h, (lo, hi) in enumerate(HALF):
+            for h, (lo, hi) in enumerate(RUNS):
                 act(T[b][:, lo:hi], T.pd[:, 1024 * h + 512:1024 * h + 512 + hi - lo], ["Pd%d" % (2 * h + 1), sk, o], [b + str(h)], scale=s, bias=cl(o))
         tt(whole("o1"), whole("mw").indirect(dW), whole("mi"), A.min, ["mw0", "mw1", uw, "mi0", "mi1"], ["o1"])
         if r == 0:
+            planes(0, range(2, 4))
             e_list(0)
             e_first()
             cp(whole("npW"), sm("np"), ["np"], ["npW"])
+        else:
+            cp(whole("d3W"), sm("d3"), ["d3"], ["d3W"])
         tt(whole("o2"), whole("o1").indirect(dW), whole("ms"), A.min, ["o1", uw, "ms0", "ms1"], ["o2"])
         tr(whole("to2"), whole("o2"), ["o2"], ["to2"])
         for i in range(3): cp(sl("tsend%d" % r, i), col("to2", 4 * i), ["to2"], ["tsend%d.%d" % (r, i)])
         send(p, "t%d" % r, whole("tland%d" % r), whole("tsend%d" % r), ["tsend%d.%d" % (r, i) for i in range(3)])
-        cp(whole("d3W"), sm("d3"), ["d3"], ["d3W"])
-
-        def planes():
-            for t in range(4): act(T.xp[:, C * t:C * t + C], T[X][:, t:4 * C:4], [X + ".0", X + ".1"], ["xp%d" % t], 0.5)
+        e_rest()
         if r == 0:
             cp(whole("nW"), si("nli"), ["nli"], ["nW"])
-            e_rest()
-            gat("g3o", "o2", whole("d3W"), ["d3W"])
-            late_constants()
+            for a, b in (("l2", "o2"), ("d3p", "l2"), ("g3o", "d3p")): gat(a, b, dW, [uw])
             invert(sl("eW", 1), "eW")
             dma("y", "mei", row("ei", 1), row("fi", 1), ["fi"], ["ei1"])
-            planes()
             cp(col("tbb", 13), sm("iotaT"), ["iotaT"], ["tbb"])
             zero(whole("fl"), ["fl0", "fl1"])
             zero(whole("da"), ["da"])
             zero(T.s480[:, 0:16], ["s480"])
             zero(T.s480[:, 16 + C:32 + C], ["s480"])
-            fill(T.one[:, :], 1.0, ["one"])
+            iota(T.one[:, :], [[0, 512]], 1, 0, ["one"])
+            iota(whole("q"), PLACES, 0, 0, keys("q"))
             for b in range(4):
                 op("g", lambda: g.affine_select(T.et[:, 512 * b:512 * b + 512], T.one[:, :], [[-1, 512]], A.is_equal, 0.0, b, 4), ["one"], ["et%d" % b])
         else:
-            e_rest()
             gat("g3o", "o2", whole("d3W"), ["d3W"])
-            planes()
-        tr(whole("tg3o"), whole("g3o"), ["g3o"], ["tg3o"])
-        for i in range(3): tt(sm("A%d" % (3 + i)), col("to2", 8), col("tg3o", 4 * i), A.min, ["to2", "tg3o"], ["A%d" % (3 + i)])
+            planes(r, range(4))
         pw = [(sm("iotaE"), "iotaE")] + [(col(b, q), b) for b in ("to2", "tg3o") for q in (1, 5, 9)]
-        for i in range(6): tt(slot("da", i // 3, i % 3), pw[i][0], pw[i + 1][0], A.subtract, [pw[i][1], pw[i + 1][1], "da"], ["da%d" % i])
-        ts1(slot("da", 1, 3), pw[6][0], E0, A.subtract, ["tg3o", "da"], ["da6"])
+
+        def steps_a(js):
+            for i in js: tt(slot("da", i // 3, i % 3), pw[i][0], pw[i + 1][0], A.subtract, [pw[i][1], pw[i + 1][1], "da"], ["da%d" % i])
+
+        def own_rest():
+            tr(whole("tg3o"), whole("g3o"), ["g3o"], ["tg3o"])
+            for i in range(3): tt(sm("A%d" % (3 + i)), col("to2", 8), col("tg3o", 4 * i), A.min, ["to2", "tg3o"], ["A%d" % (3 + i)])
+            steps_a(range(3, 6))
+            act(slot("da", 1, 3), pw[6][0], ["tg3o", "da"], ["da6"], bias=-E0)
+        steps_a(range(3))
         tr(whole("te"), whole("e1"), keys("e1"), ["te"])
         tt(col("tbb", 1), col("te", 1), col("te", 9), A.subtract, ["te", "tbbd"], ["tbbd0"])
         tt(col("tbb", 5), col("te", 9), col("te", 5), A.subtract, ["te", "tbbd"], ["tbbd1"])
         tt(col("tbb", 9), col("te", 5), sm("iotaT"), A.subtract, ["te", "iotaT", "tbbd"], ["tbbd2"])
+        if r: own_rest()
         cp(whole("e3W"), sm("e3"), ["e3"], ["e3W"])
         if r: dma("y", "mei", row("ei", 1), whole("iland%d" % r), ["iland%d" % r], ["ei1"])
         for i in range(3): cp(col("tbb", 4 * i), sl("tland%d" % r, i), ["tland%d" % r, "tbbs"], ["tbbs%d" % i])
         tr(whole("sb"), whole("tbb"), ["tbb"] + ["tbb%s%d" % (k, i) for k in "sd" for i in range(3)], ["sb"])
+        cp(T.g0[:, 0:C // 2], whole("sb").indirect(T.nW[:, 0:K // 2]), ["sb", "nW"], ["g0"])
+        act(T.g0[:, C // 2:C], whole("sb").indirect(T.nW[:, K // 2:K]), ["sb", "nW"], ["g0b"])
         gat("g3", "sb", whole("e3W"), ["e3W", "s3"], scale=cl("s3"), bias=0.0)
-        cp(whole("g0"), whole("sb").indirect(whole("nW")), ["sb", "nW"], ["g0"])
+        if r == 0: own_rest()
         mates(r)
-        tr(whole("tg0"), whole("g0"), ["g0"], ["tg0"])
+        tr(whole("tg0"), whole("g0"), ["g0", "g0b"], ["tg0"])
         for j in range(3): tt(slot("fl", 1, 3 - j), sm("A%d" % (5 - j)), col("tg0", 4 * j), A.is_le, ["A%d" % (5 - j), "tg0", "fl1"], ["h%d" % j])
-        tr(whole("tg3"), whole("g3"), ["g3"], ["tg3"])
         scan(sl("rb", 4, 4), sl("fl", 4, 4), T.tg0[:, 1:C:4], ["h0", "h1", "h2", "tg0"], ["rb1"])
+        scan(sl("ra", 4, 4), sl("fl", 4, 4), sl("da", 4, 4), ["h0", "h1", "h2", "da3", "da4", "da5", "da6"], ["ra1"])
+        tr(whole("tg3"), whole("g3"), ["g3"], ["tg3"])
         for j in range(3): tt(sm("B%d" % (3 + j)), col("tg0", 8), col("tg3", 4 * j), A.min, ["tg0", "tg3"], ["B%d" % (3 + j)])
         for j in range(3): tt(slot("fl", 0, 3 - j), col("to2", 8 - 4 * j), sm("B%d" % (3 + j)), A.is_le, ["to2", "B%d" % (3 + j), "fl0"], ["h%d" % (3 + j)])
         scan(sl("rb", 0, 4), sl("fl", 0, 4), T.tg3[:, 1:C:4], ["h3", "h4", "h5", "tg3"], ["rb0"])
-        scan(whole("ra"), whole("fl"), whole("da"), ["h%d" % j for j in range(6)] + ["da%d" % i for i in range(7)], ["ra"])
+        scan(sl("ra", 0, 4), sl("fl", 0, 4), sl("da", 0, 4), ["h3", "h4", "h5", "da0", "da1", "da2"], ["ra0"])
         tt(col("tcb", 8), slot("rb", 0, 3), slot("rb", 1, 3), A.add, ["rb0", "rb1", "tcb"], ["tcbs"])
-        tt(col("tcb", 0), slot("ra", 0, 3), slot("ra", 1, 3), A.add, ["ra", "tcb"], ["tcbd"])
+        tt(col("tcb", 0), slot("ra", 0, 3), slot("ra", 1, 3), A.add, ["ra0", "ra1", "tcb"], ["tcbd"])
         tr(T.s480[:, 16:16 + C], whole("tcb"), ["tcbs", "tcbd"], ["s480"])
         act(whole("kn"), T.s480[:, 16:16 + C].indirect(whole("npW")), ["s480", "npW"], ["kn"])
         dma("y", "mkn", sm("pbn"), row("kn", 8), ["kn"], ["pbn"])
@@ -388,17 +398,15 @@ def rank_program(g, core, T, topo):
                 mm(T[bank][:, 512 * i:512 * i + hi - lo], T.qw[:, 128 * i:128 * i + 128], T.sw[:, 128 * i:128 * i + 128], T[q][:, lo - c0:hi - c0], T[s][:, lo - c0:hi - c0],
                    ["qw", "sw", qk], ["P" + bank[1] + str(i)])
 
+        def evac(k):
+            lo, hi = CH[k]
+            for i in range(4): act(T.hh[:, 4 * lo + i:4 * hi:4], T[("ph", "pd")[k]][:, 512 * i:512 * i + hi - lo], ["P" + "hd"[k] + str(i)], ["hh%d%d" % (k, i)], 0.03125)
+
         def pack(k):
             lo, hi = CH[k]
             quant(T["qh%d" % r][:, lo:hi], T["sh%d" % r][:, lo:hi], T.hh[:, 4 * lo:4 * hi], ["hh%d%d" % (k, i) for i in range(4)], ["qh%d%d" % (r, k)])
             send(p, "c%d%d" % (k, r), T["ql%d" % r][:, lo:hi].bitcast(dt.uint8), T["qh%d" % r][:, lo:hi].bitcast(dt.uint8), ["qh%d%d" % (r, k)])
             send(p, "s%d%d" % (k, r), T["sl%d" % r][:, lo:hi], T["sh%d" % r][:, lo:hi], ["qh%d%d" % (r, k)])
-
-        def evac(k, i, q):
-            lo, hi = CH[k]
-            src, dst, pk_ = T[("ph", "pd")[k]][:, 512 * i:512 * i + hi - lo], T.hh[:, 4 * lo + i:4 * hi:4], "P" + "hd"[k] + str(i)
-            if q == "s": act(dst, src, [pk_], ["hh%d%d" % (k, i)], 0.03125)
-            else: ts1(dst, src, 0.03125, A.mult, [pk_], ["hh%d%d" % (k, i)])
 
         def edit():
             tt(si("is"), T.w56[:, 1:2 * K:2], sm("pbn"), A.add, ["w56", "pbn"], ["is"])
@@ -412,46 +420,40 @@ def rank_program(g, core, T, topo):
         for k in range(2):
             for t in range(4): gather_a(k, t)
         for t in range(4): add_b(0, t)
-        layer(0, 192, "ph", "qz", "sz", 0, [0], "qz0")
+        layer(*CH[0], "ph", "qz", "sz", 0, [0], "qz0")
         for t in range(4): add_b(1, t)
-        layer(192, 336, "pd", "qz", "sz", 0, [1], "qz1")
-        for i in range(4): evac(0, i, "s")
+        layer(*CH[1], "pd", "qz", "sz", 0, [1], "qz1")
+        evac(0)
         pack(0)
-        if OPT["fpos"] == 0: edit()
-        for i in range(4): evac(1, i, "vs"[i % 2])
+        edit()
+        evac(1)
         for t in range(4): gather_a(2, t)
         pack(1)
-        if r == 0: act(whole("q"), whole("ei"), keys("ei"), keys("q"))
-        if OPT["fpos"] == 1: edit()
-        if not last: send(peer[r + 1], "l%d" % (r + 1), whole("lland%d" % (r + 1)), sl(lnn, 0, 2), [lnn])
         for t in range(4): add_b(2, t)
         layer(OWN[0], OWN[1], "ph", "qo", "so", OWN[0], [1, 2], "qo")
+        if not last: send(peer[r + 1], "l%d" % (r + 1), whole("lland%d" % (r + 1)), sl(lnn, 0, 2), [lnn])
         for i in range(4): act(T.jp[:, C * i + F:C * i + C], T.ph[:, 512 * i + F - OWN[0]:512 * i + C - OWN[0]], ["Ph%d" % i], ["jp%dh" % i], 0.03125)
         if r == 0: quant(whole("qe"), whole("se_"), whole("et"), ["et%d" % b for b in range(4)], ["qe"])
         if last:
             quant(T.qv[:, :], T.sv_[:, :], T.vb[:, :], ["vb"], ["qv"])
         else:
             invert(sl(uwn, 1), uwn)
-            dma("y", "mq1", row("q", 1), row("fi", 1), ["fi"], ["q1"])
             dma("y", "mis", whole("isend%d" % (r + 1)), row("fi", 0), ["fi"], ["isend"])
             send(peer[r + 1], "i%d" % (r + 1), whole("iland%d" % (r + 1)), whole("isend%d" % (r + 1)), ["isend"])
             e_row(r + 1)
         for k, (lo, hi) in enumerate(CH):
-            n = hi - lo
+            bank = ("pd", "ph")[k]
             for b in range(4):
-                mm(T[("ph", "pd")[k]][:, 512 * b:512 * b + n], T.qe[:, 128 * b:128 * b + 128], T.se_[:, 128 * b:128 * b + 128], T["ql%d" % r][:, lo:hi], T["sl%d" % r][:, lo:hi],
-                   ["qe", "ql%d.%d" % (r, k), "sl%d.%d" % (r, k)], ["P" + "hd"[k] + str(b)])
+                mm(T[bank][:, 512 * b:512 * b + hi - lo], T.qe[:, 128 * b:128 * b + 128], T.se_[:, 128 * b:128 * b + 128], T["ql%d" % r][:, lo:hi], T["sl%d" % r][:, lo:hi],
+                   ["qe", "ql%d.%d" % (r, k), "sl%d.%d" % (r, k)], ["P" + bank[1] + str(b)])
             for b in range(4):
-                src, dst, pk_ = T[("ph", "pd")[k]][:, 512 * b:512 * b + n], T.jp[:, C * b + lo:C * b + hi], "P" + "hd"[k] + str(b)
-                if k == 0 or b % 2: act(dst, src, [pk_], ["jp%d%d" % (b, k)])
-                else: cp(dst, src, [pk_], ["jp%d%d" % (b, k)])
+                act(T.jp[:, C * b + lo:C * b + hi], T[bank][:, 512 * b:512 * b + hi - lo], ["P" + bank[1] + str(b)], ["jp%d%d" % (b, k)])
         if last:
             gat("lrow", "q", sl(uwn, 1), [uwn])
-            dma("y", "st0", T.dn[:, :], row("lrow", 5), ["lrow"], [])
+            dma("y", "st0", T.dn[:, :], row("lrow", 5), keys("lrow"), [])
         else:
-            gat("lrow", "q", sl(uwn, 1), [uwn, "sL", "bL"], scale=cl("sL"), bias=cl("bL"))
             cube(r + 1)
-        for h, (lo, hi) in enumerate(HALF):
+        for h, (lo, hi) in enumerate(RUNS):
             if h == 1 and not last:
                 e_list(r + 1)
                 e_first()

@@ -7,16 +7,17 @@ RUNS = [(0, 320), (320, C)]
 CH = [(0, 192), (192, 336)]
 CHZ = [(0, 192), (192, 352), (352, 448)]
 OWN = (320, 448)
+CUT = 16
 NZ = 1024.0
 BIG, E0, E1 = 2.0 ** 90, 2.0 ** 80, 2.0 ** 60
-SLOTS = ["iotaT", "iotaE", "mask", "inv", "glo", "A3", "A4", "A5", "B3", "B4", "B5", "d3", "e3", "np", "pbn", "t1", "t2", "t3", "t4", "xw"]
+SLOTS = ["iotaT", "iotaE", "iotaH", "A3", "A4", "A5", "B3", "B4", "B5", "d3", "e3", "np", "pbn", "t1", "t2", "t3", "t4", "xw"]
 ISLOTS = ["i1", "i2", "i3", "is", "odd", "ip", "ib", "dli", "nli", "bi"]
-COLS = ["pq", "bW", "sS", "bS", "sL", "bL", "b1", "s3", "sQ", "bQ", "s0", "b0", "c1", "c2", "c3", "c4"]
+COLS = ["pq", "bW", "sS", "bS", "sL", "bL", "b1", "c1", "c2", "c3", "c4", "u1"]
 
 SCRATCH = {
     "sm": ("sbuf", [128, K * len(SLOTS)], "float32"),
     "si": ("sbuf", [128, K * len(ISLOTS)], "int32"),
-    "cl": ("sbuf", [128, len(COLS)], "float32"), "ind": ("sbuf", [128, 16], "float32"), "c16": ("sbuf", [128, 16], "float32"),
+    "cl": ("sbuf", [128, len(COLS)], "float32"), "ind": ("sbuf", [128, 16], "float32"),
     "xp": ("sbuf", [128, 4 * C], "bfloat16"), "tmp": ("sbuf", [128, 4 * C], "bfloat16"),
     "z": ("sbuf", [128, 4 * C], "bfloat16"), "hh": ("sbuf", [128, 4 * F], "bfloat16"),
     "jp": ("sbuf", [128, 4 * C], "bfloat16"),
@@ -31,20 +32,20 @@ SCRATCH = {
     "qw": ("sbuf", [128, 512], "float8_e4m3fn_x4"), "sw": ("sbuf", [128, 512], "uint8"),
     "qe": ("sbuf", [128, 512], "float8_e4m3fn_x4"), "se_": ("sbuf", [128, 512], "uint8"),
     "fl": ("sbuf", [128, 8 * K], "float32"), "da": ("sbuf", [128, 8 * K], "float32"),
-    "ra": ("sbuf", [128, 8 * K], "float32"), "rb": ("sbuf", [128, 8 * K], "float32"),
+    "ra": ("sbuf", [128, 4 * K], "float32"), "rb": ("sbuf", [128, 4 * K], "float32"),
     "m56": ("sbuf", [128, 2 * K], "float32"), "i56": ("sbuf", [128, 2 * K], "float32"),
     "v56": ("sbuf", [128, 2 * K], "float32"), "u56": ("sbuf", [128, 2 * K], "float32"), "w56": ("sbuf", [128, 2 * K], "int32"),
     "lb": ("sbuf", [128, 3 * K], "float32"), "df": ("sbuf", [128, 3 * K], "float32"), "pr": ("sbuf", [128, 3 * K], "float32"),
-    "qi": ("sbuf", [128, C], "int32"),
     "ysb": ("sbuf", [128, C], "float32"),
     "ph": ("psum", [128, 2048], "float32"), "pd": ("psum", [128, 2048], "float32"),
 }
 for _n in ("mw", "mi", "ms", "o1", "o2", "to2", "g3o", "tg3o", "tbb", "sb", "g0", "g3", "tg0", "tg3", "tcb", "kn", "lrow", "l2", "d3p",
-           "q", "fi", "ep", "e1", "e2", "te", "e3p", "ei", "m1", "mn", "mp", "iotaS", "ide"):
+           "q", "fi", "ep", "e3p", "ei", "m1", "mn", "mp", "iotaS", "ride"):
     SCRATCH[_n] = ("sbuf", [128, C], "float32")
+for _n in ("e1", "e2", "te"): SCRATCH[_n] = ("sbuf", [128, C], "bfloat16")
 for _n in ("s480", "t480"): SCRATCH[_n] = ("sbuf", [128, C + 32], "float32")
 for _n in ("nW", "npW", "cpW", "d3W", "e3W", "aW", "bW"): SCRATCH[_n] = ("sbuf", [128, K], "uint16")
-SCRATCH["eW"] = ("sbuf", [128, 2 * K], "uint16")
+SCRATCH["eW"] = ("sbuf", [128, 2 * K * ROUNDS], "uint16")
 SCRATCH["uW"] = ("sbuf", [128, 8], "uint16")
 for _i in range(4):
     SCRATCH["x%d" % _i] = ("sbuf", [128, 4 * C], "bfloat16")
@@ -53,19 +54,18 @@ for _i in range(4):
 for _r in range(ROUNDS):
     SCRATCH["tsend%d" % _r] = ("sbuf", [128, 3 * K], "float32")
     SCRATCH["tland%d" % _r] = ("sbuf", [128, 3 * K], "float32")
-    SCRATCH["lland%d" % _r] = ("sbuf", [128, 2 * K], "float32")
+    SCRATCH["lland%d" % _r] = ("sbuf", [128, K], "float32")
+    SCRATCH["isend%d" % _r] = ("sbuf", [128, K], "float32")
+    SCRATCH["iland%d" % _r] = ("sbuf", [128, K], "float32")
     SCRATCH["qh%d" % _r] = ("sbuf", [128, F], "float8_e4m3fn_x4")
     SCRATCH["sh%d" % _r] = ("sbuf", [128, F], "uint8")
     SCRATCH["ql%d" % _r] = ("sbuf", [128, F], "float8_e4m3fn_x4")
     SCRATCH["sl%d" % _r] = ("sbuf", [128, F], "uint8")
-    if _r:
-        SCRATCH["isend%d" % _r] = ("sbuf", [128, K], "float32")
-        SCRATCH["iland%d" % _r] = ("sbuf", [128, K], "float32")
 
-SEMAPHORES = ["qv", "qs", "qt", "qg"] + ["ld%d" % i for i in range(10)] + ["st%d" % i for i in range(9)]
+SEMAPHORES = ["qv", "qs", "qt", "qg"] + ["ld%d" % i for i in range(9)] + ["st%d" % i for i in range(9)]
 SEMAPHORES += ["md3", "me2", "me3", "mei", "mmn", "mmp", "mkn", "mq9", "mq1", "mis", "mep", "mnp", "mx9"]
 for _r in range(ROUNDS):
-    for _n in ("t", "l", "c0", "s0", "c1", "s1") + (("i",) if _r else ()): SEMAPHORES += ["a%s%d" % (_n, _r), "o%s%d" % (_n, _r)]
+    for _n in ("t", "l", "u", "i", "c0", "s0", "c1", "s1"): SEMAPHORES += ["a%s%d" % (_n, _r), "o%s%d" % (_n, _r)]
 
 
 def rank_program(g, core, T, topo):
@@ -156,24 +156,21 @@ def rank_program(g, core, T, topo):
         elif scale == 1.0: op("s", lambda: g.scalar.activation(out, a, CP), r, w)
         else: op("s", lambda: g.scalar.activation(out, a, CP, scale=scale), r, w)
     def lin(n, src, skey, a, b): act(cl(n), src, [skey], [n], scale=a, bias=b)
-    ROWS = {"q": ["", "9"], "lrow": ["", "1"], "ep": ["", "9"], "ei": ["", "1", "9"], "e1": ["", "1"]}
+    ROWS = {"q": ["", "9"], "ride": ["", "5", "9"], "ep": ["", "9"], "ei": ["", "1", "9"], "e1": ["", "1"]}
     def keys(b): return [b + k for k in ROWS.get(b, [""])]
     def gat(out, win, off, r, **kw):
         act(whole(out), whole(win).indirect(off), keys(win) + r, keys(out), **kw)
     def quant(q, s, t, r, w): op("v", lambda: g.vector.quantize_mx(q, s, t), r, w)
     def mm(out, a, sa, b, sb, r, w): op("t", lambda: g.tensor.matmul_mx(out, a, sa, b, sb, True, True), r, w)
     def fill(ap, v, w): op("v", lambda: g.vector.memset(ap, v), [], w)
-    def iota(out, pat, base, cm, w, f=True):
-        if f: op("g", lambda: g.iota(out, pat, base, cm, allow_small_or_imprecise_dtypes=True), [], w)
-        else: op("g", lambda: g.iota(out, pat, base, cm), [], w)
-    def zero(ap, w): iota(ap, [[0, ap.shape[1]]], 0, 0, w)
+    def iota(out, pat, base, w): op("g", lambda: g.iota(out, pat, base, 0, allow_small_or_imprecise_dtypes=True), [], w)
+    def zero(ap, w): iota(ap, [[0, ap.shape[1]]], 0, w)
     PLACES = [[1, 16], [16, K]]
 
     peer = [T.cores[rank ^ m] for m in MASKS]
     for r in range(ROUNDS):
-        arrives(peer[r], "t%d" % r, ["tland%d" % r])
-        arrives(peer[r], "l%d" % r, ["lland%d" % r])
-        if r: arrives(peer[r], "i%d" % r, ["iland%d" % r])
+        for n in "tli": arrives(peer[r], "%s%d" % (n, r), ["%sland%d" % (n, r)])
+        arrives(peer[r], "u%d" % r, ["eW%d" % r])
         for k in range(2):
             arrives(peer[r], "c%d%d" % (k, r), ["ql%d.%d" % (r, k)])
             arrives(peer[r], "s%d%d" % (k, r), ["sl%d.%d" % (r, k)])
@@ -186,30 +183,35 @@ def rank_program(g, core, T, topo):
             k = 2 * h + b
             mm(T.pd[:, 512 * k:512 * k + hi - lo], whole(a), whole(sa), T.qx[:, lo:hi], T.sx[:, lo:hi], ka + ["qx%d" % h], ["Pd%d" % k])
 
-    def cube(r):
-        gat("lrow", "q", sl("uw%d" % r, 1), ["uw%d" % r, "sL", "bL"], scale=cl("sL"), bias=cl("bL"))
-        gat("l2", "lrow", sl("uw%d" % r, 0), ["uw%d" % r])
-        dma("y", "mq1", row("lrow", 1), row("ide", 1), ["ide"], ["lrow1"])
+    def powers(r):
+        gat("lrow", "q", sl("uw%d" % r, 1), ["uw%d" % r], scale=E1, bias=E0)
+        for q in (5, 9): dma("y", "mq1", row("ride", q), row("lrow", q), ["lrow", "ride"], ["ride%d" % q])
+
+    def cube_row(r): gat("l2", "lrow", sl("uw%d" % r, 0), ["uw%d" % r])
+    def cube_table():
         gat("d3p", "l2", whole("cpW"), ["cpW"], scale=1.0 / E1, bias=-E0 / E1)
         dma("y", "md3", sm("d3"), row("d3p", 9), ["d3p"], ["d3"])
 
-    def invert(off, okey):
-        op("v", lambda: g.vector.tensor_copy(whole("fi").indirect(off), whole("iotaS")), [okey, "iotaS"], ["fi"])
+    def invert(r, halves=(0, 1)):
+        lo, hi = K // 2 * halves[0], K // 2 * (halves[-1] + 1)
+        op("v", lambda: g.vector.tensor_copy(whole("fi").indirect(T["uw%d" % r][:, K + lo:K + hi]), T.iotaS[:, 16 * lo:16 * hi]), ["uw%d" % r, "iotaS"], ["fi"])
 
-    def e_row(r): dma("y", "mep", row("ep", 9), sl("lland%d" % r, 0), ["lland%d" % r], ["ep9"])
-    def e_list(r): cp(whole("eW"), whole("lland%d" % r), ["lland%d" % r], ["eW"])
-    def e_first(): gat("e1", "ep", sl("eW", 1), ["eW", "b1"], bias=cl("b1"))
-    def e_rest():
-        gat("e2", "e1", sl("eW", 0), ["eW"], bias=NZ)
-        gat("e3p", "e2", whole("npW"), ["npW"], bias=-3 * NZ)
+    def inverse_table(r): dma("y", "mis", whole("isend%d" % r), row("fi", 0), ["fi"], ["isend"])
+    def inverse_out(r): send(peer[r], "i%d" % r, whole("iland%d" % r), whole("isend%d" % r), ["isend"])
+
+    def e_row(r): dma("y", "mep", row("ep", 9), whole("lland%d" % r), ["lland%d" % r], ["ep9"])
+    def e_first(r): gat("e1", "ep", sl("eW", 2 * r + 1), ["eW%d" % r], bias=-C / 2)
+    def e_rest(r):
+        gat("e2", "e1", sl("eW", 2 * r), ["eW%d" % r])
         dma("y", "me2", row("e1", 1), row("e2", 9), ["e2"], ["e11"])
+        gat("e3p", "e2", whole("npW"), ["npW"], bias=C / 2)
         dma("y", "me3", sm("e3"), row("e3p", 9), ["e3p"], ["e3"])
 
     def planes(r, ts):
         for t in ts: act(T.xp[:, C * t:C * t + C], T["x%d" % r][:, t:4 * C:4], ["x%d.0" % r, "x%d.1" % r], ["xp%d" % t], 0.5)
 
+    def along_d(r): gat("m1", "ei", sl("uw%d" % r, 1), ["uw%d" % r])
     def mates(r):
-        gat("m1", "ei", sl("uw%d" % r, 1), ["uw%d" % r])
         gat("mn", "m1", whole("npW"), ["npW"])
         for i, q in enumerate((5, 9, 1)): dma("y", "mmn", sl("lb", i), row("mn", q), ["mn"], ["lb%d" % i])
         gat("mp", "m1", whole("cpW"), ["cpW"])
@@ -217,125 +219,118 @@ def rank_program(g, core, T, topo):
 
     def load_x(h): dma("y", "ld%d" % (2 + h), T.x0[:, 4 * RUNS[h][0]:4 * RUNS[h][1]], T.x[:, 4 * RUNS[h][0]:4 * RUNS[h][1]], [], ["x0.%d" % h])
     dma("s", "ld0", si("dli"), T.dl[:, :], [], ["dli"])
+    dma("y", "ld1", si("nli"), T.nl[:, :], [], ["nli"])
     dma("y", "ld4", T.ub[:, :], T.u[:, :], [], ["ub"])
-    dma("s", "ld1", si("nli"), T.nl[:, :], [], ["nli"])
     load_x(1)
-    iota(si("ip"), [[0, K]], 0, 1, ["ip"], False)
-    iota(whole("c16"), [[1, 16]], 0, 0, ["c16"])
-    iota(si("ib"), [[16, K]], 0, 0, ["ib"], False)
-    iota(sm("glo"), [[0, K // 2], [1, 2]], 0, 0, ["glo"])
-    iota(whole("qi"), PLACES, 0, 0, ["qi3", "qi9"], False)
-    dma("y", "ld8", row("qi", 9), T.dl[:, :], [], ["qi9"])
-    dma("y", "ld9", row("qi", 3), T.nl[:, :], [], ["qi3"])
-    load_x(0)
+    iota(whole("q"), PLACES, 0, keys("q"))
     fill(whole("mw"), 1.0, ["mw0", "mw1"])
     scan(whole("iotaS"), whole("mw"), whole("mw"), ["mw0", "mw1"], ["iotaS"], -1.0)
+    tr(T.mi[:, 0:32], T.iotaS[:, 0:32], ["iotaS"], ["mi0"])
+    act(whole("kn"), whole("iotaS"), ["iotaS"], ["kn"])
+    cp(si("ip"), T.mi[:, 0:K], ["mi0"], ["ip"])
+    ts1(cl("u1"), T.mi[:, 0:1], 16.0, A.is_ge, ["mi0"], ["u1"])
     ts1(si("i1"), si("ip"), 15, A.bitwise_and, ["ip"], ["i1"])
+    cp(si("ib"), T.iotaS[:, 0:K], ["iotaS"], ["ib"])
     cp(cl("pq"), si("i1", 1), ["i1"], ["pq"])
-    ts1(whole("ind"), whole("c16"), cl("pq"), A.is_equal, ["c16", "pq"], ["ind"])
-    tt(sm("xw"), si("i1"), si("ib"), A.add, ["i1", "ib"], ["xw"])
-    cp(whole("uW"), si("ib", 8), ["ib"], ["uW"])
-    tt(cl("c1"), ind(5), ind(9), A.add, ["ind"], ["c1"])
-    tt(cl("c2"), ind(4), ind(8), A.add, ["ind"], ["c2"])
-    ts2(si("i3"), sm("xw"), -0.5 * (K - 1), A.add, 1.0 / K, A.mult, ["xw"], ["i3"])
-    ts1(sm("t4"), sm("xw"), 16.0, A.mult, ["xw"], ["t4"])
-    ts1(sm("t3"), si("i3"), float(1 - C), A.mult, ["i3"], ["t3"])
-    tt(sm("t3"), sm("t3"), sm("t4"), A.add, ["t3", "t4"], ["t3"])
-    cp(whole("cpW"), sm("t3"), ["t3"], ["cpW"])
+    for h in range(2): act(T.sm[:, h:K:2], T.iotaS[:, 0:C:32], ["iotaS", "mi0"], ["iotaT" + "x" * h], bias=T.mi[:, 0:1])
+    lastw["iotaT"] = [("qs", count["qs"])]
+    act(sm("iotaH"), sm("iotaT"), ["iotaT"], ["iotaH"], bias=-C / 2)
+    act(sm("iotaE"), sm("iotaT"), ["iotaT"], ["iotaE"], scale=E1, bias=E0)
+    cp(sl("ln0", 0), si("dli"), ["dli"], ["ln0"])
+    ts1(whole("ind"), T.iotaS[:, 0:16], cl("pq"), A.is_equal, ["iotaS", "pq"], ["ind"])
+    send(peer[0], "l0", whole("lland0"), sl("ln0", 0), ["ln0"])
+    dma("y", "mq9", row("q", 9), sl("ln0", 0), ["ln0"], ["q9"])
+    cp(sm("t4"), si("nli"), ["nli"], ["t4"])
+    dma("y", "ld8", row("kn", 3), sm("t4"), ["t4"], ["kn"])
+    load_x(0)
     ts1(si("i2"), si("dli"), 4, A.arith_shift_right, ["dli"], ["i2"])
     ts1(sm("t2"), si("dli"), float(K), A.mult, ["dli"], ["t2"])
-    cp(sl("ln0", 0), si("dli"), ["dli"], ["ln0"])
+    tt(cl("c1"), ind(5), ind(9), A.add, ["ind"], ["c1"])
+    tt(cl("c2"), ind(4), ind(8), A.add, ["ind"], ["c2"])
     ts1(sm("t1"), si("i2"), float(1 - C), A.mult, ["i2"], ["t1"])
-    tt(sl("ln0", 1), sm("t1"), sm("t2"), A.add, ["t1", "t2", "ln0"], ["ln0"])
-    send(peer[0], "l0", whole("lland0"), sl("ln0", 0, 2), ["ln0"])
-    cp(sl("uw0", 0, 2), sl("ln0", 0, 2), ["ln0"], ["uw0"])
-    act(cl("sL"), ind(3), ["ind", "c1"], ["sL"], scale=1.0, bias=cl("c1"))
-    lin("sQ", cl("sL"), "sL", E1, 0.0)
-    lin("bQ", cl("sL"), "sL", E0 - BIG, BIG)
-    lin("s0", ind(1), "ind", E1, 0.0)
+    ts1(si("bi"), si("ib"), 1, A.bitwise_and, ["ib"], ["bi"])
+    tt(sl("ln0", 1), sm("t1"), sm("t2"), A.add, ["t1", "t2"], ["ln0p"])
+    tt(sm("xw"), si("i1"), col("iotaS", 0), A.add, ["i1", "iotaS"], ["xw"])
+    cp(sl("uw0", 0, 2), sl("ln0", 0, 2), ["ln0", "ln0p"], ["uw0"])
+    lastw["ln0"] = [("qv", count["qv"])]
+    send(peer[0], "u0", sl("eW", 0, 2), sl("uw0", 0, 2), ["uw0"])
+    lin("sL", ind(1), "ind", E1, 0.0)
     lin("c3", cl("c2"), "c2", -2 * BIG, BIG)
-    lin("c4", ind(1), "ind", E0 - BIG, 0.0)
+    act(cl("bL"), ind(1), ["ind", "c3"], ["bL"], scale=E0 - BIG, bias=cl("c3"))
+    act(whole("ride"), whole("iotaS"), ["iotaS", "sL", "bL"], ["ride"], scale=cl("sL"), bias=cl("bL"))
     lin("bW", ind(8), "ind", -BIG, BIG)
-    tt(cl("sS"), cl("c2"), ind(0), A.add, ["c2", "ind"], ["sS"])
-    tt(cl("b0"), cl("c3"), cl("c4"), A.add, ["c3", "c4"], ["b0"])
+    act(cl("sS"), ind(0), ["ind", "c2"], ["sS"], scale=1.0, bias=cl("c2"))
     lin("bS", cl("sS"), "sS", -BIG, BIG)
-    act(whole("ide"), whole("iotaS"), ["iotaS", "s0", "b0"], ["ide"], scale=cl("s0"), bias=cl("b0"))
-    ts2(si("i1"), si("ip"), 4, A.arith_shift_right, 1, A.bitwise_and, ["ip"], ["i1"])
-    ts1(si("i2"), si("ip"), 31, A.bitwise_and, ["ip"], ["i2"])
-    ts1(sm("t1"), sm("glo"), -16.0, A.mult, ["glo"], ["t1"])
-    tt(sm("mask"), si("i1"), sm("glo"), A.is_equal, ["i1", "glo"], ["mask"])
-    tt(sm("t2"), si("i2"), si("ib"), A.add, ["i2", "ib"], ["t2"])
-    tt(sm("inv"), si("i1"), sm("glo"), A.not_equal, ["i1", "glo"], ["inv"])
-    tt(sm("iotaT"), sm("t1"), sm("t2"), A.add, ["t1", "t2"], ["iotaT"])
-    for b, s in (("m56", "mask"), ("i56", "inv")):
-        act(T[b][:, 0:2 * K:2], sm(s), [s], [b + "a"], scale=1.0 / E1)
-        act(T[b][:, 1:2 * K:2], sm(s), [s], [b])
-    act(sm("iotaE"), sm("iotaT"), ["iotaT"], ["iotaE"], scale=E1, bias=E0)
-    lin("s3", ind(13), "ind", -1.0, 1.0)
-    tt(cl("sL"), cl("sQ"), cl("s0"), A.add, ["sQ", "s0"], ["sL"])
-    tt(cl("bL"), cl("b0"), cl("bQ"), A.min, ["b0", "bQ"], ["bL"])
+    act(cl("c4"), ind(1), ["ind", "c1"], ["c4"], scale=1.0, bias=cl("c1"))
+    lin("b1", cl("c4"), "c4", NZ, 0.0)
+    ts2(si("i3"), sm("xw"), -0.5 * (K - 1), A.add, 1.0 / K, A.mult, ["xw"], ["i3"])
+    ts1(sm("t2"), sm("xw"), 16.0, A.mult, ["xw"], ["t2"])
+    cp(whole("uW"), T.iotaS[:, 0:128:16], ["iotaS"], ["uW"])
+    ts1(sm("t3"), si("i3"), float(1 - C), A.mult, ["i3"], ["t3"])
     quant(T.qu[:, :], T.su[:, :], T.ub[:, :], ["ub"], ["qu"])
+    tt(sm("t3"), sm("t3"), sm("t2"), A.add, ["t3", "t2"], ["t3"])
     cp(whole("qu2").bitcast(dt.uint32), whole("qu").bitcast(dt.uint32).indirect(whole("uW")), ["qu", "uW"], ["qu2"])
     act(whole("su2"), whole("su").indirect(whole("uW")), ["qu", "uW"], ["su2"])
+    cp(whole("cpW"), sm("t3"), ["t3"], ["cpW"])
+    cp(whole("nW"), si("nli"), ["nli"], ["nW"])
     scores(0, 1)
-    act(cl("c3"), ind(9), ["ind", "c1"], ["c3"], scale=1.0, bias=cl("c1"))
-    lin("b1", cl("c3"), "c3", NZ, 0.0)
-    ts2(whole("m1"), whole("qi"), cl("sQ"), A.mult, cl("bQ"), A.add, ["qi3", "qi9", "sQ", "bQ"], ["m1"])
+    invert(0, [0])
     scores(0, 0)
-    tt(whole("lrow"), whole("m1").indirect(sl("uw0", 1)), whole("ide"), A.min, ["m1", "uw0", "ide"], keys("lrow"))
-    iota(whole("ep"), PLACES, 0, 0, keys("ep"))
-    gat("mn", "m1", whole("cpW"), ["cpW"], scale=1.0 / E1, bias=-E0 / E1)
+    invert(0, [1])
+    iota(whole("ep"), PLACES, 0, keys("ep"))
+    powers(0)
+    gat("mn", "kn", whole("cpW"), ["cpW"])
     dma("y", "mnp", sm("np"), row("mn", 3), ["mn"], ["np"])
     e_row(0)
+    cube_row(0)
+    iota(whole("ei"), PLACES, 0, keys("ei"))
+    inverse_table(0)
     dma("y", "ld5", T.qw[:, :].bitcast(dt.uint8), T.wc[:, :], [], ["qw"])
     dma("y", "ld6", T.sw[:, :], T.ws[:, :], [], ["sw"])
     dma("y", "ld7", T.vb[:, :], T.v[:, :], [], ["vb"])
-    planes(0, range(2))
-    iota(whole("ei"), PLACES, 0, 0, keys("ei"))
     dma("y", "mx9", row("ei", 9), row("iotaS", 9), ["iotaS"], ["ei9"])
-    for b in ("tbb", "tcb"): zero(whole(b), [b + k for k in ("", "s", "d")])
+    zero(whole("da"), ["da"])
+    zero(whole("tbb"), ["tbb", "tbbs", "tbbd"])
+    inverse_out(0)
 
     for r in range(ROUNDS):
         p = peer[r]
-        last = r == ROUNDS - 1
+        first, last = r == 0, r == ROUNDS - 1
         X, XN = "x%d" % r, "x%d" % (r + 1)
         uw, uwn, ln, lnn = "uw%d" % r, "uw%d" % (r + 1), "ln%d" % r, "ln%d" % (r + 1)
         dW = sl(uw, 0)
         for h, (lo, hi) in enumerate(RUNS):
-            tt(T.mi[:, lo:hi], T.pd[:, 1024 * h:1024 * h + hi - lo], T.lrow[:, lo:hi], A.max, ["Pd%d" % (2 * h)] + keys("lrow"), ["mi%d" % h])
+            tt(T.mi[:, lo:hi], T.pd[:, 1024 * h:1024 * h + hi - lo], T.ride[:, lo:hi], A.max, ["Pd%d" % (2 * h)] + keys("ride"), ["mi%d" % h])
         for b, s, sk, o in (("mw", ind(8), "ind", "bW"), ("ms", cl("sS"), "sS", "bS")):
             for h, (lo, hi) in enumerate(RUNS):
                 act(T[b][:, lo:hi], T.pd[:, 1024 * h + 512:1024 * h + 512 + hi - lo], ["Pd%d" % (2 * h + 1), sk, o], [b + str(h)], scale=s, bias=cl(o))
         tt(whole("o1"), whole("mw").indirect(dW), whole("mi"), A.min, ["mw0", "mw1", uw, "mi0", "mi1"], ["o1"])
-        if r == 0:
-            planes(0, range(2, 4))
-            e_list(0)
-            e_first()
+        if first:
+            cube_table()
+            e_first(0)
             cp(whole("npW"), sm("np"), ["np"], ["npW"])
         else:
             cp(whole("d3W"), sm("d3"), ["d3"], ["d3W"])
         tt(whole("o2"), whole("o1").indirect(dW), whole("ms"), A.min, ["o1", uw, "ms0", "ms1"], ["o2"])
         tr(whole("to2"), whole("o2"), ["o2"], ["to2"])
-        for i in range(3): cp(sl("tsend%d" % r, i), col("to2", 4 * i), ["to2"], ["tsend%d.%d" % (r, i)])
-        send(p, "t%d" % r, whole("tland%d" % r), whole("tsend%d" % r), ["tsend%d.%d" % (r, i) for i in range(3)])
-        e_rest()
-        if r == 0:
-            cp(whole("nW"), si("nli"), ["nli"], ["nW"])
-            for a, b in (("l2", "o2"), ("d3p", "l2"), ("g3o", "d3p")): gat(a, b, dW, [uw])
-            invert(sl("eW", 1), "eW")
-            dma("y", "mei", row("ei", 1), row("fi", 1), ["fi"], ["ei1"])
+        cp(sl("tsend%d" % r, 0, 2), T.to2[:, 0:C:8], ["to2"], ["tsend%d.0" % r])
+        cp(sl("tsend%d" % r, 2), col("to2", 4), ["to2"], ["tsend%d.1" % r])
+        send(p, "t%d" % r, whole("tland%d" % r), whole("tsend%d" % r), ["tsend%d.%d" % (r, i) for i in range(2)])
+        if first:
             cp(col("tbb", 13), sm("iotaT"), ["iotaT"], ["tbb"])
+            for b, o in (("m56", A.is_equal), ("i56", A.not_equal)):
+                ts2(sl(b, 0), si("bi"), cl("u1"), o, 1.0 / E1, A.mult, ["bi", "u1"], [b + "a"])
+                ts1(sl(b, 1), si("bi"), cl("u1"), o, ["bi", "u1"], [b])
             zero(whole("fl"), ["fl0", "fl1"])
-            zero(whole("da"), ["da"])
+            zero(whole("tcb"), ["tcb", "tcbs", "tcbd"])
             zero(T.s480[:, 0:16], ["s480"])
             zero(T.s480[:, 16 + C:32 + C], ["s480"])
-            iota(T.one[:, :], [[0, 512]], 1, 0, ["one"])
-            iota(whole("q"), PLACES, 0, 0, keys("q"))
+            iota(T.one[:, :], [[0, 512]], 1, ["one"])
             for b in range(4):
                 op("g", lambda: g.affine_select(T.et[:, 512 * b:512 * b + 512], T.one[:, :], [[-1, 512]], A.is_equal, 0.0, b, 4), ["one"], ["et%d" % b])
-        else:
-            gat("g3o", "o2", whole("d3W"), ["d3W"])
-            planes(r, range(4))
+        e_rest(r)
+        if not first: gat("g3o", "o2", whole("d3W"), ["d3W"])
+        planes(r, range(1 if first else 3))
         pw = [(sm("iotaE"), "iotaE")] + [(col(b, q), b) for b in ("to2", "tg3o") for q in (1, 5, 9)]
 
         def steps_a(js):
@@ -347,40 +342,54 @@ def rank_program(g, core, T, topo):
             steps_a(range(3, 6))
             act(slot("da", 1, 3), pw[6][0], ["tg3o", "da"], ["da6"], bias=-E0)
         steps_a(range(3))
+        if first:
+            for t in range(1, 4): ts1(T.xp[:, C * t:C * t + C], T.x0[:, t:4 * C:4], 0.5, A.mult, ["x0.0", "x0.1"], ["xp%d" % t])
+            cp(whole("d3W"), sm("d3"), ["d3"], ["d3W"])
+            gat("g3o", "o2", whole("d3W"), ["d3W"])
         tr(whole("te"), whole("e1"), keys("e1"), ["te"])
         tt(col("tbb", 1), col("te", 1), col("te", 9), A.subtract, ["te", "tbbd"], ["tbbd0"])
         tt(col("tbb", 5), col("te", 9), col("te", 5), A.subtract, ["te", "tbbd"], ["tbbd1"])
-        tt(col("tbb", 9), col("te", 5), sm("iotaT"), A.subtract, ["te", "iotaT", "tbbd"], ["tbbd2"])
-        if r: own_rest()
-        cp(whole("e3W"), sm("e3"), ["e3"], ["e3W"])
-        if r: dma("y", "mei", row("ei", 1), whole("iland%d" % r), ["iland%d" % r], ["ei1"])
-        for i in range(3): cp(col("tbb", 4 * i), sl("tland%d" % r, i), ["tland%d" % r, "tbbs"], ["tbbs%d" % i])
-        tr(whole("sb"), whole("tbb"), ["tbb"] + ["tbb%s%d" % (k, i) for k in "sd" for i in range(3)], ["sb"])
-        cp(T.g0[:, 0:C // 2], whole("sb").indirect(T.nW[:, 0:K // 2]), ["sb", "nW"], ["g0"])
-        act(T.g0[:, C // 2:C], whole("sb").indirect(T.nW[:, K // 2:K]), ["sb", "nW"], ["g0b"])
-        gat("g3", "sb", whole("e3W"), ["e3W", "s3"], scale=cl("s3"), bias=0.0)
-        if r == 0: own_rest()
+        tt(col("tbb", 9), col("te", 5), sm("iotaH"), A.subtract, ["te", "iotaH", "tbbd"], ["tbbd2"])
+        dma("y", "mei", row("ei", 1), whole("iland%d" % r), ["iland%d" % r], ["ei1"])
+        if not first:
+            along_d(r)
+            own_rest()
+            cp(whole("e3W"), sm("e3"), ["e3"], ["e3W"])
+        cp(T.tbb[:, 0:C:8], sl("tland%d" % r, 0, 2), ["tland%d" % r, "tbbs"], ["tbbs0"])
+        cp(col("tbb", 4), sl("tland%d" % r, 2), ["tland%d" % r, "tbbs"], ["tbbs1"])
+        tr(whole("sb"), whole("tbb"), ["tbb", "tbbs0", "tbbs1", "tbbd0", "tbbd1", "tbbd2"], ["sb"])
+        if first: cp(whole("e3W"), sm("e3"), ["e3"], ["e3W"])
+        ts1(T.g0[:, 0:16 * CUT], whole("sb").indirect(T.nW[:, 0:CUT]), cl("b1"), A.add, ["sb", "nW", "b1"], ["g0"])
+        act(T.g0[:, 16 * CUT:C], whole("sb").indirect(T.nW[:, CUT:K]), ["sb", "nW", "b1"], ["g0b"], bias=cl("b1"))
+        gat("g3", "sb", whole("e3W"), ["e3W", "b1"], bias=cl("b1"))
+        if first:
+            own_rest()
+            along_d(r)
+        else:
+            planes(r, [3])
         mates(r)
         tr(whole("tg0"), whole("g0"), ["g0", "g0b"], ["tg0"])
         for j in range(3): tt(slot("fl", 1, 3 - j), sm("A%d" % (5 - j)), col("tg0", 4 * j), A.is_le, ["A%d" % (5 - j), "tg0", "fl1"], ["h%d" % j])
-        scan(sl("rb", 4, 4), sl("fl", 4, 4), T.tg0[:, 1:C:4], ["h0", "h1", "h2", "tg0"], ["rb1"])
-        scan(sl("ra", 4, 4), sl("fl", 4, 4), sl("da", 4, 4), ["h0", "h1", "h2", "da3", "da4", "da5", "da6"], ["ra1"])
         tr(whole("tg3"), whole("g3"), ["g3"], ["tg3"])
+        scan(whole("ra"), sl("fl", 4, 4), sl("da", 4, 4), ["h0", "h1", "h2", "da3", "da4", "da5", "da6"], ["ra"])
+        scan(whole("rb"), sl("fl", 4, 4), T.tg0[:, 1:C:4], ["h0", "h1", "h2", "tg0"], ["rb"])
         for j in range(3): tt(sm("B%d" % (3 + j)), col("tg0", 8), col("tg3", 4 * j), A.min, ["tg0", "tg3"], ["B%d" % (3 + j)])
         for j in range(3): tt(slot("fl", 0, 3 - j), col("to2", 8 - 4 * j), sm("B%d" % (3 + j)), A.is_le, ["to2", "B%d" % (3 + j), "fl0"], ["h%d" % (3 + j)])
-        scan(sl("rb", 0, 4), sl("fl", 0, 4), T.tg3[:, 1:C:4], ["h3", "h4", "h5", "tg3"], ["rb0"])
-        scan(sl("ra", 0, 4), sl("fl", 0, 4), sl("da", 0, 4), ["h3", "h4", "h5", "da0", "da1", "da2"], ["ra0"])
-        tt(col("tcb", 8), slot("rb", 0, 3), slot("rb", 1, 3), A.add, ["rb0", "rb1", "tcb"], ["tcbs"])
-        tt(col("tcb", 0), slot("ra", 0, 3), slot("ra", 1, 3), A.add, ["ra0", "ra1", "tcb"], ["tcbd"])
+        cp(slot("da", 0, 3), slot("ra", 0, 3), ["ra", "da"], ["da7"])
+        cp(col("tg3", 13), slot("rb", 0, 3), ["rb", "tg3"], ["tg3b"])
+        scan(T.tcb[:, 0:C:4], sl("fl", 0, 4), sl("da", 0, 4), ["h3", "h4", "h5", "da0", "da1", "da2", "da7", "tcb"], ["tcbd"])
+        scan(T.tcb[:, 1:C:4], sl("fl", 0, 4), T.tg3[:, 1:C:4], ["h3", "h4", "h5", "tg3", "tg3b", "tcb"], ["tcbs"])
+        def in_place(i): tt(sl("v56", i), col("tcb", 12 + i), sl("m56", i), A.mult, ["tcbs", "tcbd", "m56", "m56a"], ["v56%d" % i])
         tr(T.s480[:, 16:16 + C], whole("tcb"), ["tcbs", "tcbd"], ["s480"])
         act(whole("kn"), T.s480[:, 16:16 + C].indirect(whole("npW")), ["s480", "npW"], ["kn"])
-        dma("y", "mkn", sm("pbn"), row("kn", 8), ["kn"], ["pbn"])
+        dma("y", "mkn", sm("pbn"), row("kn", 13), ["kn"], ["pbn"])
+        in_place(0)
         tr(whole("t480"), whole("s480"), ["s480"], ["t480"])
-        tt(whole("v56"), T.tcb[:, 0:C:8], whole("m56"), A.mult, ["tcbs", "tcbd", "m56", "m56a"], ["v56"])
-        tt(whole("u56"), T.t480[:, 16:16 + C:8], whole("i56"), A.mult, ["t480", "i56", "i56a"], ["u56"])
-        tt(whole("w56"), whole("v56"), whole("u56"), A.add, ["v56", "u56"], ["w56"])
-        cp(whole("aW"), T.w56[:, 0:2 * K:2], ["w56"], ["aW"])
-        ts1(si("bi"), T.w56[:, 1:2 * K:2], int(NZ) - 1, A.bitwise_and, ["w56"], ["bi"])
+        in_place(1)
+        for i in range(2): tt(sl("u56", i), T.t480[:, 28 + i:C + 16:16], sl("i56", i), A.mult, ["t480", "i56", "i56a"], ["u56%d" % i])
+        for i in range(2): tt(sl("w56", i), sl("v56", i), sl("u56", i), A.add, ["v56%d" % i, "u56%d" % i], ["w56%d" % i])
+        cp(whole("aW"), sl("w56", 0), ["w560"], ["aW"])
+        ts1(si("bi"), sl("w56", 1), int(NZ) - 1, A.bitwise_and, ["w561"], ["bi"])
         cp(whole("bW"), si("bi"), ["bi"], ["bW"])
 
         def gather_a(k, t):
@@ -409,7 +418,7 @@ def rank_program(g, core, T, topo):
             send(p, "s%d%d" % (k, r), T["sl%d" % r][:, lo:hi], T["sh%d" % r][:, lo:hi], ["qh%d%d" % (r, k)])
 
         def edit():
-            tt(si("is"), T.w56[:, 1:2 * K:2], sm("pbn"), A.add, ["w56", "pbn"], ["is"])
+            tt(si("is"), sl("w56", 1), sm("pbn"), A.add, ["w561", "pbn"], ["is"])
             tt(whole("df"), whole("lb"), whole(ln), A.subtract, ["lb0", "lb1", "lb2", ln, ln + "m"], ["df"])
             ts2(si("odd"), si("is"), 10, A.arith_shift_right, 1, A.bitwise_and, ["is"], ["odd"])
             for i in range(3): tt(sl("pr", i), sl("df", i), si("odd"), A.mult, ["df", "odd"], ["pr%d" % i])
@@ -426,37 +435,39 @@ def rank_program(g, core, T, topo):
         evac(0)
         pack(0)
         edit()
+        for t in range(2): gather_a(2, t)
         evac(1)
-        for t in range(4): gather_a(2, t)
+        for t in range(2, 4): gather_a(2, t)
         pack(1)
         for t in range(4): add_b(2, t)
         layer(OWN[0], OWN[1], "ph", "qo", "so", OWN[0], [1, 2], "qo")
-        if not last: send(peer[r + 1], "l%d" % (r + 1), whole("lland%d" % (r + 1)), sl(lnn, 0, 2), [lnn])
+        if not last:
+            send(peer[r + 1], "l%d" % (r + 1), whole("lland%d" % (r + 1)), sl(lnn, 0), [lnn])
+            send(peer[r + 1], "u%d" % (r + 1), sl("eW", 2 * r + 2, 2), sl(uwn, 0, 2), [uwn])
         for i in range(4): act(T.jp[:, C * i + F:C * i + C], T.ph[:, 512 * i + F - OWN[0]:512 * i + C - OWN[0]], ["Ph%d" % i], ["jp%dh" % i], 0.03125)
-        if r == 0: quant(whole("qe"), whole("se_"), whole("et"), ["et%d" % b for b in range(4)], ["qe"])
+        if first: quant(whole("qe"), whole("se_"), whole("et"), ["et%d" % b for b in range(4)], ["qe"])
         if last:
             quant(T.qv[:, :], T.sv_[:, :], T.vb[:, :], ["vb"], ["qv"])
         else:
-            invert(sl(uwn, 1), uwn)
-            dma("y", "mis", whole("isend%d" % (r + 1)), row("fi", 0), ["fi"], ["isend"])
-            send(peer[r + 1], "i%d" % (r + 1), whole("iland%d" % (r + 1)), whole("isend%d" % (r + 1)), ["isend"])
+            invert(r + 1)
+            inverse_table(r + 1)
+            inverse_out(r + 1)
             e_row(r + 1)
         for k, (lo, hi) in enumerate(CH):
             bank = ("pd", "ph")[k]
             for b in range(4):
                 mm(T[bank][:, 512 * b:512 * b + hi - lo], T.qe[:, 128 * b:128 * b + 128], T.se_[:, 128 * b:128 * b + 128], T["ql%d" % r][:, lo:hi], T["sl%d" % r][:, lo:hi],
                    ["qe", "ql%d.%d" % (r, k), "sl%d.%d" % (r, k)], ["P" + bank[1] + str(b)])
-            for b in range(4):
                 act(T.jp[:, C * b + lo:C * b + hi], T[bank][:, 512 * b:512 * b + hi - lo], ["P" + bank[1] + str(b)], ["jp%d%d" % (b, k)])
         if last:
             gat("lrow", "q", sl(uwn, 1), [uwn])
-            dma("y", "st0", T.dn[:, :], row("lrow", 5), keys("lrow"), [])
+            dma("y", "st0", T.dn[:, :], row("lrow", 5), ["lrow"], [])
         else:
-            cube(r + 1)
+            powers(r + 1)
+            cube_row(r + 1)
+            cube_table()
+            e_first(r + 1)
         for h, (lo, hi) in enumerate(RUNS):
-            if h == 1 and not last:
-                e_list(r + 1)
-                e_first()
             for t in range(4):
                 tt(T[XN][:, 4 * lo + t:4 * hi:4], T.jp[:, C * t:C * t + C].indirect(T[uwn][:, 2 * K + lo // 16:2 * K + hi // 16]), T[X][:, 4 * lo + t:4 * hi:4], A.add,
                    ["jp%d0" % t, "jp%d1" % t, "jp%dh" % t, uwn, X + ".%d" % h], [XN + "t%d%d" % (h, t)])

from concourse.mybir import dt, AluOpType, ActivationFunctionType

C, F, ROUNDS = 448, 336, 3
K = C // 16
MASKS = [1, 2, 3]
RUNS = [(0, 320), (320, C)]
CH = [(0, 192), (192, 336)]
CHZ = [(0, 192), (192, 352), (352, 448)]
OWN = (320, 448)
CUT = 16
NZ = 1024.0
BIG, E0, E1 = 2.0 ** 90, 2.0 ** 80, 2.0 ** 60
SLOTS = ["iotaT", "iotaE", "iotaH", "A3", "A4", "A5", "B3", "B4", "B5", "d3", "e3", "np", "pbn", "t1", "t2", "t3", "t4", "xw"]
ISLOTS = ["i1", "i2", "i3", "is", "odd", "ip", "ib", "dli", "nli", "bi"]
COLS = ["pq", "bW", "sS", "bS", "sL", "bL", "b1", "c1", "c2", "c3", "c4", "u1"]

SCRATCH = {
    "sm": ("sbuf", [128, K * len(SLOTS)], "float32"),
    "si": ("sbuf", [128, K * len(ISLOTS)], "int32"),
    "cl": ("sbuf", [128, len(COLS)], "float32"), "ind": ("sbuf", [128, 16], "float32"),
    "xp": ("sbuf", [128, 4 * C], "bfloat16"), "tmp": ("sbuf", [128, 4 * C], "bfloat16"),
    "z": ("sbuf", [128, 4 * C], "bfloat16"), "hh": ("sbuf", [128, 4 * F], "bfloat16"),
    "jp": ("sbuf", [128, 4 * C], "bfloat16"),
    "ub": ("sbuf", [128, 512], "bfloat16"), "vb": ("sbuf", [128, 512], "bfloat16"),
    "one": ("sbuf", [128, 512], "bfloat16"), "et": ("sbuf", [128, 2048], "bfloat16"),
    "qu": ("sbuf", [128, 128], "float8_e4m3fn_x4"), "su": ("sbuf", [128, 128], "uint8"),
    "qu2": ("sbuf", [128, 128], "float8_e4m3fn_x4"), "su2": ("sbuf", [128, 128], "uint8"),
    "qv": ("sbuf", [128, 128], "float8_e4m3fn_x4"), "sv_": ("sbuf", [128, 128], "uint8"),
    "qx": ("sbuf", [128, C], "float8_e4m3fn_x4"), "sx": ("sbuf", [128, C], "uint8"),
    "qz": ("sbuf", [128, C], "float8_e4m3fn_x4"), "sz": ("sbuf", [128, C], "uint8"),
    "qo": ("sbuf", [128, 128], "float8_e4m3fn_x4"), "so": ("sbuf", [128, 128], "uint8"),
    "qw": ("sbuf", [128, 512], "float8_e4m3fn_x4"), "sw": ("sbuf", [128, 512], "uint8"),
    "qe": ("sbuf", [128, 512], "float8_e4m3fn_x4"), "se_": ("sbuf", [128, 512], "uint8"),
    "fl": ("sbuf", [128, 8 * K], "float32"), "da": ("sbuf", [128, 8 * K], "float32"),
    "ra": ("sbuf", [128, 4 * K], "float32"), "rb": ("sbuf", [128, 4 * K], "float32"),
    "m56": ("sbuf", [128, 2 * K], "float32"), "i56": ("sbuf", [128, 2 * K], "float32"),
    "v56": ("sbuf", [128, 2 * K], "float32"), "u56": ("sbuf", [128, 2 * K], "float32"), "w56": ("sbuf", [128, 2 * K], "int32"),
    "lb": ("sbuf", [128, 3 * K], "float32"), "df": ("sbuf", [128, 3 * K], "float32"), "pr": ("sbuf", [128, 3 * K], "float32"),
    "ysb": ("sbuf", [128, C], "float32"),
    "ph": ("psum", [128, 2048], "float32"), "pd": ("psum", [128, 2048], "float32"),
}
for _n in ("mw", "mi", "ms", "o1", "o2", "to2", "g3o", "tg3o", "tbb", "sb", "g0", "g3", "tg0", "tg3", "tcb", "kn", "lrow", "l2", "d3p",
           "q", "fi", "ep", "e3p", "ei", "m1", "mn", "mp", "iotaS", "ride"):
    SCRATCH[_n] = ("sbuf", [128, C], "float32")
for _n in ("e1", "e2", "te"): SCRATCH[_n] = ("sbuf", [128, C], "bfloat16")
for _n in ("s480", "t480"): SCRATCH[_n] = ("sbuf", [128, C + 32], "float32")
for _n in ("nW", "npW", "cpW", "d3W", "e3W", "aW", "bW"): SCRATCH[_n] = ("sbuf", [128, K], "uint16")
SCRATCH["eW"] = ("sbuf", [128, 2 * K * ROUNDS], "uint16")
SCRATCH["uW"] = ("sbuf", [128, 8], "uint16")
for _i in range(4):
    SCRATCH["x%d" % _i] = ("sbuf", [128, 4 * C], "bfloat16")
    SCRATCH["ln%d" % _i] = ("sbuf", [128, 3 * K], "float32")
    SCRATCH["uw%d" % _i] = ("sbuf", [128, 3 * K], "uint16")
for _r in range(ROUNDS):
    SCRATCH["tsend%d" % _r] = ("sbuf", [128, 3 * K], "float32")
    SCRATCH["tland%d" % _r] = ("sbuf", [128, 3 * K], "float32")
    SCRATCH["lland%d" % _r] = ("sbuf", [128, K], "float32")
    SCRATCH["isend%d" % _r] = ("sbuf", [128, K], "float32")
    SCRATCH["iland%d" % _r] = ("sbuf", [128, K], "float32")
    SCRATCH["qh%d" % _r] = ("sbuf", [128, F], "float8_e4m3fn_x4")
    SCRATCH["sh%d" % _r] = ("sbuf", [128, F], "uint8")
    SCRATCH["ql%d" % _r] = ("sbuf", [128, F], "float8_e4m3fn_x4")
    SCRATCH["sl%d" % _r] = ("sbuf", [128, F], "uint8")

SEMAPHORES = ["qv", "qs", "qt", "qg"] + ["ld%d" % i for i in range(9)] + ["st%d" % i for i in range(9)]
SEMAPHORES += ["md3", "me2", "me3", "mei", "mmn", "mmp", "mkn", "mq9", "mq1", "mis", "mep", "mnp", "mx9"]
for _r in range(ROUNDS):
    for _n in ("t", "l", "u", "i", "c0", "s0", "c1", "s1"): SEMAPHORES += ["a%s%d" % (_n, _r), "o%s%d" % (_n, _r)]


def rank_program(g, core, T, topo):
    rank = T.rank_of(core)
    if rank is None:
        return
    A = AluOpType
    CP, ID = ActivationFunctionType.Copy, ActivationFunctionType.Identity
    eng = {"v": g.vector, "s": g.scalar, "t": g.tensor, "g": g, "y": g.sync}
    own = {"v": "qv", "s": "qs", "t": "qt", "g": "qg"}
    count, known, lastw, readers, snap = {}, {q: {} for q in eng}, {}, {}, {}

    def wait(q, ev):
        s, n = ev
        if known[q].get(s, 0) >= n: return
        eng[q].wait_ge(T.sem[s], n)
        known[q][s] = n
        for a, b in snap.get(ev, {}).items():
            if known[q].get(a, 0) < b: known[q][a] = b

    def need(q, r, w):
        deps = []
        for k in r: deps += lastw.get(k, [])
        for k in w: deps += lastw.get(k, []) + readers.get(k, [])
        best = {}
        for s, n in deps: best[s] = max(n, best.get(s, 0))
        for s in sorted(best): wait(q, (s, best[s]))

    def done(q, ev, r, w):
        snap[ev] = dict(known[q])
        for k in r: readers.setdefault(k, []).append(ev)
        for k in w: lastw[k], readers[k] = [ev], []

    def op(q, call, r, w):
        w = w + [k for k in r if k[0] == "P"]
        r = [k for k in r if k[0] != "P"]
        need(q, r, w)
        s = own[q]
        count[s] = count.get(s, 0) + 1
        call().then_inc(T.sem[s], 1)
        done(q, (s, count[s]), r, w)

    def dma(q, sem, out, in_, r, w):
        need(q, r, w)
        eng[q].dma_start(out, in_).then_inc(T.sem[sem], 16)
        count[sem] = count.get(sem, 0) + 16
        done(q, (sem, count[sem]), r, w)

    def send(dst, name, out, in_, r):
        need("g", r, [])
        m = topo.mask(core, dst)
        rid, pid = topo.addr(dst)[:2]
        g.remote_dma(out, in_, T.sem["a" + name], T.sem["o" + name], pid, rid, m)
        count["o" + name] = len(topo.engines(core, dst))
        done("g", ("o" + name, count["o" + name]), r, [])

    def arrives(src, name, w):
        count["a" + name] = len(topo.engines(src, core))
        for k in w: lastw[k] = [("a" + name, count["a" + name])]

    def sm(n):
        i = SLOTS.index(n)
        return T.sm[:, K * i:K * i + K]

    def si(n, w=K):
        i = ISLOTS.index(n)
        return T.si[:, K * i:K * i + w]

    def cl(n):
        i = COLS.index(n)
        return T.cl[:, i:i + 1]

    def sl(b, i, n=1): return T[b][:, K * i:K * i + K * n]
    def col(b, q): return T[b][:, q:C:16]
    def row(b, q): return T[b][q:128:16, :]
    def slot(b, h, s): return T[b][:, 4 * K * h + s:4 * K * (h + 1):4]
    def whole(b): return T[b][:, :]
    def ind(q): return T.ind[:, q:q + 1]

    def tt(out, a, b, o, r, w): op("v", lambda: g.vector.tensor_tensor(out, a, b, o), r, w)
    def ts1(out, a, s, o, r, w): op("v", lambda: g.vector.tensor_scalar(out, a, s, None, o), r, w)
    def ts2(out, a, s, o, s2, o2, r, w): op("v", lambda: g.vector.tensor_scalar(out, a, s, s2, o, o2), r, w)
    def cp(out, a, r, w): op("v", lambda: g.vector.tensor_copy(out, a), r, w)
    def tr(out, a, r, w): op("v", lambda: g.vector.transpose(out, a), r, w)
    def scan(out, a, b, r, w, first=0.0): op("v", lambda: g.vector.tensor_tensor_scan(out, a, b, first, A.mult, A.add), r, w)
    def act(out, a, r, w, scale=1.0, bias=None):
        if bias is not None: op("s", lambda: g.scalar.activation(out, a, ID, bias=bias, scale=scale), r, w)
        elif scale == 1.0: op("s", lambda: g.scalar.activation(out, a, CP), r, w)
        else: op("s", lambda: g.scalar.activation(out, a, CP, scale=scale), r, w)
    def lin(n, src, skey, a, b): act(cl(n), src, [skey], [n], scale=a, bias=b)
    ROWS = {"q": ["", "9"], "ride": ["", "5", "9"], "ep": ["", "9"], "ei": ["", "1", "9"], "e1": ["", "1"]}
    def keys(b): return [b + k for k in ROWS.get(b, [""])]
    def gat(out, win, off, r, **kw):
        act(whole(out), whole(win).indirect(off), keys(win) + r, keys(out), **kw)
    def quant(q, s, t, r, w): op("v", lambda: g.vector.quantize_mx(q, s, t), r, w)
    def mm(out, a, sa, b, sb, r, w): op("t", lambda: g.tensor.matmul_mx(out, a, sa, b, sb, True, True), r, w)
    def fill(ap, v, w): op("v", lambda: g.vector.memset(ap, v), [], w)
    def iota(out, pat, base, w): op("g", lambda: g.iota(out, pat, base, 0, allow_small_or_imprecise_dtypes=True), [], w)
    def zero(ap, w): iota(ap, [[0, ap.shape[1]]], 0, w)
    PLACES = [[1, 16], [16, K]]

    peer = [T.cores[rank ^ m] for m in MASKS]
    for r in range(ROUNDS):
        for n in "tli": arrives(peer[r], "%s%d" % (n, r), ["%sland%d" % (n, r)])
        arrives(peer[r], "u%d" % r, ["eW%d" % r])
        for k in range(2):
            arrives(peer[r], "c%d%d" % (k, r), ["ql%d.%d" % (r, k)])
            arrives(peer[r], "s%d%d" % (k, r), ["sl%d.%d" % (r, k)])

    def scores(r, h):
        lo, hi = RUNS[h]
        quant(T.qx[:, lo:hi], T.sx[:, lo:hi], T["x%d" % r][:, 4 * lo:4 * hi], ["x%d.%d" % (r, h)], ["qx%d" % h])
        a, sa, ka = ("qu2", "su2", ["qu2", "su2"]) if r < ROUNDS else ("qv", "sv_", ["qv"])
        for b in range(2 if r < ROUNDS else 1):
            k = 2 * h + b
            mm(T.pd[:, 512 * k:512 * k + hi - lo], whole(a), whole(sa), T.qx[:, lo:hi], T.sx[:, lo:hi], ka + ["qx%d" % h], ["Pd%d" % k])

    def powers(r):
        gat("lrow", "q", sl("uw%d" % r, 1), ["uw%d" % r], scale=E1, bias=E0)
        for q in (5, 9): dma("y", "mq1", row("ride", q), row("lrow", q), ["lrow", "ride"], ["ride%d" % q])

    def cube_row(r): gat("l2", "lrow", sl("uw%d" % r, 0), ["uw%d" % r])
    def cube_table():
        gat("d3p", "l2", whole("cpW"), ["cpW"], scale=1.0 / E1, bias=-E0 / E1)
        dma("y", "md3", sm("d3"), row("d3p", 9), ["d3p"], ["d3"])

    def invert(r, halves=(0, 1)):
        lo, hi = K // 2 * halves[0], K // 2 * (halves[-1] + 1)
        op("v", lambda: g.vector.tensor_copy(whole("fi").indirect(T["uw%d" % r][:, K + lo:K + hi]), T.iotaS[:, 16 * lo:16 * hi]), ["uw%d" % r, "iotaS"], ["fi"])

    def inverse_table(r): dma("y", "mis", whole("isend%d" % r), row("fi", 0), ["fi"], ["isend"])
    def inverse_out(r): send(peer[r], "i%d" % r, whole("iland%d" % r), whole("isend%d" % r), ["isend"])

    def e_row(r): dma("y", "mep", row("ep", 9), whole("lland%d" % r), ["lland%d" % r], ["ep9"])
    def e_first(r): gat("e1", "ep", sl("eW", 2 * r + 1), ["eW%d" % r], bias=-C / 2)
    def e_rest(r):
        gat("e2", "e1", sl("eW", 2 * r), ["eW%d" % r])
        dma("y", "me2", row("e1", 1), row("e2", 9), ["e2"], ["e11"])
        gat("e3p", "e2", whole("npW"), ["npW"], bias=C / 2)
        dma("y", "me3", sm("e3"), row("e3p", 9), ["e3p"], ["e3"])

    def planes(r, ts):
        for t in ts: act(T.xp[:, C * t:C * t + C], T["x%d" % r][:, t:4 * C:4], ["x%d.0" % r, "x%d.1" % r], ["xp%d" % t], 0.5)

    def along_d(r): gat("m1", "ei", sl("uw%d" % r, 1), ["uw%d" % r])
    def mates(r):
        gat("mn", "m1", whole("npW"), ["npW"])
        for i, q in enumerate((5, 9, 1)): dma("y", "mmn", sl("lb", i), row("mn", q), ["mn"], ["lb%d" % i])
        gat("mp", "m1", whole("cpW"), ["cpW"])
        dma("y", "mmp", sl("ln%d" % r, 2), row("mp", 1), ["mp"], ["ln%dm" % r])

    def load_x(h): dma("y", "ld%d" % (2 + h), T.x0[:, 4 * RUNS[h][0]:4 * RUNS[h][1]], T.x[:, 4 * RUNS[h][0]:4 * RUNS[h][1]], [], ["x0.%d" % h])
    dma("s", "ld0", si("dli"), T.dl[:, :], [], ["dli"])
    dma("y", "ld1", si("nli"), T.nl[:, :], [], ["nli"])
    dma("y", "ld4", T.ub[:, :], T.u[:, :], [], ["ub"])
    load_x(1)
    iota(whole("q"), PLACES, 0, keys("q"))
    fill(whole("mw"), 1.0, ["mw0", "mw1"])
    scan(whole("iotaS"), whole("mw"), whole("mw"), ["mw0", "mw1"], ["iotaS"], -1.0)
    tr(T.mi[:, 0:32], T.iotaS[:, 0:32], ["iotaS"], ["mi0"])
    act(whole("kn"), whole("iotaS"), ["iotaS"], ["kn"])
    cp(si("ip"), T.mi[:, 0:K], ["mi0"], ["ip"])
    ts1(cl("u1"), T.mi[:, 0:1], 16.0, A.is_ge, ["mi0"], ["u1"])
    ts1(si("i1"), si("ip"), 15, A.bitwise_and, ["ip"], ["i1"])
    cp(si("ib"), T.iotaS[:, 0:K], ["iotaS"], ["ib"])
    cp(cl("pq"), si("i1", 1), ["i1"], ["pq"])
    for h in range(2): act(T.sm[:, h:K:2], T.iotaS[:, 0:C:32], ["iotaS", "mi0"], ["iotaT" + "x" * h], bias=T.mi[:, 0:1])
    lastw["iotaT"] = [("qs", count["qs"])]
    act(sm("iotaH"), sm("iotaT"), ["iotaT"], ["iotaH"], bias=-C / 2)
    act(sm("iotaE"), sm("iotaT"), ["iotaT"], ["iotaE"], scale=E1, bias=E0)
    cp(sl("ln0", 0), si("dli"), ["dli"], ["ln0"])
    ts1(whole("ind"), T.iotaS[:, 0:16], cl("pq"), A.is_equal, ["iotaS", "pq"], ["ind"])
    send(peer[0], "l0", whole("lland0"), sl("ln0", 0), ["ln0"])
    dma("y", "mq9", row("q", 9), sl("ln0", 0), ["ln0"], ["q9"])
    cp(sm("t4"), si("nli"), ["nli"], ["t4"])
    dma("y", "ld8", row("kn", 3), sm("t4"), ["t4"], ["kn"])
    load_x(0)
    ts1(si("i2"), si("dli"), 4, A.arith_shift_right, ["dli"], ["i2"])
    ts1(sm("t2"), si("dli"), float(K), A.mult, ["dli"], ["t2"])
    tt(cl("c1"), ind(5), ind(9), A.add, ["ind"], ["c1"])
    tt(cl("c2"), ind(4), ind(8), A.add, ["ind"], ["c2"])
    ts1(sm("t1"), si("i2"), float(1 - C), A.mult, ["i2"], ["t1"])
    ts1(si("bi"), si("ib"), 1, A.bitwise_and, ["ib"], ["bi"])
    tt(sl("ln0", 1), sm("t1"), sm("t2"), A.add, ["t1", "t2"], ["ln0p"])
    tt(sm("xw"), si("i1"), col("iotaS", 0), A.add, ["i1", "iotaS"], ["xw"])
    cp(sl("uw0", 0, 2), sl("ln0", 0, 2), ["ln0", "ln0p"], ["uw0"])
    lastw["ln0"] = [("qv", count["qv"])]
    send(peer[0], "u0", sl("eW", 0, 2), sl("uw0", 0, 2), ["uw0"])
    lin("sL", ind(1), "ind", E1, 0.0)
    lin("c3", cl("c2"), "c2", -2 * BIG, BIG)
    act(cl("bL"), ind(1), ["ind", "c3"], ["bL"], scale=E0 - BIG, bias=cl("c3"))
    act(whole("ride"), whole("iotaS"), ["iotaS", "sL", "bL"], ["ride"], scale=cl("sL"), bias=cl("bL"))
    lin("bW", ind(8), "ind", -BIG, BIG)
    act(cl("sS"), ind(0), ["ind", "c2"], ["sS"], scale=1.0, bias=cl("c2"))
    lin("bS", cl("sS"), "sS", -BIG, BIG)
    act(cl("c4"), ind(1), ["ind", "c1"], ["c4"], scale=1.0, bias=cl("c1"))
    lin("b1", cl("c4"), "c4", NZ, 0.0)
    ts2(si("i3"), sm("xw"), -0.5 * (K - 1), A.add, 1.0 / K, A.mult, ["xw"], ["i3"])
    ts1(sm("t2"), sm("xw"), 16.0, A.mult, ["xw"], ["t2"])
    cp(whole("uW"), T.iotaS[:, 0:128:16], ["iotaS"], ["uW"])
    ts1(sm("t3"), si("i3"), float(1 - C), A.mult, ["i3"], ["t3"])
    quant(T.qu[:, :], T.su[:, :], T.ub[:, :], ["ub"], ["qu"])
    tt(sm("t3"), sm("t3"), sm("t2"), A.add, ["t3", "t2"], ["t3"])
    cp(whole("qu2").bitcast(dt.uint32), whole("qu").bitcast(dt.uint32).indirect(whole("uW")), ["qu", "uW"], ["qu2"])
    act(whole("su2"), whole("su").indirect(whole("uW")), ["qu", "uW"], ["su2"])
    cp(whole("cpW"), sm("t3"), ["t3"], ["cpW"])
    cp(whole("nW"), si("nli"), ["nli"], ["nW"])
    scores(0, 1)
    invert(0, [0])
    scores(0, 0)
    invert(0, [1])
    iota(whole("ep"), PLACES, 0, keys("ep"))
    powers(0)
    gat("mn", "kn", whole("cpW"), ["cpW"])
    dma("y", "mnp", sm("np"), row("mn", 3), ["mn"], ["np"])
    e_row(0)
    cube_row(0)
    iota(whole("ei"), PLACES, 0, keys("ei"))
    inverse_table(0)
    dma("y", "ld5", T.qw[:, :].bitcast(dt.uint8), T.wc[:, :], [], ["qw"])
    dma("y", "ld6", T.sw[:, :], T.ws[:, :], [], ["sw"])
    dma("y", "ld7", T.vb[:, :], T.v[:, :], [], ["vb"])
    dma("y", "mx9", row("ei", 9), row("iotaS", 9), ["iotaS"], ["ei9"])
    zero(whole("da"), ["da"])
    zero(whole("tbb"), ["tbb", "tbbs", "tbbd"])
    inverse_out(0)

    for r in range(ROUNDS):
        p = peer[r]
        first, last = r == 0, r == ROUNDS - 1
        X, XN = "x%d" % r, "x%d" % (r + 1)
        uw, uwn, ln, lnn = "uw%d" % r, "uw%d" % (r + 1), "ln%d" % r, "ln%d" % (r + 1)
        dW = sl(uw, 0)
        for h, (lo, hi) in enumerate(RUNS):
            tt(T.mi[:, lo:hi], T.pd[:, 1024 * h:1024 * h + hi - lo], T.ride[:, lo:hi], A.max, ["Pd%d" % (2 * h)] + keys("ride"), ["mi%d" % h])
        for b, s, sk, o in (("mw", ind(8), "ind", "bW"), ("ms", cl("sS"), "sS", "bS")):
            for h, (lo, hi) in enumerate(RUNS):
                act(T[b][:, lo:hi], T.pd[:, 1024 * h + 512:1024 * h + 512 + hi - lo], ["Pd%d" % (2 * h + 1), sk, o], [b + str(h)], scale=s, bias=cl(o))
        tt(whole("o1"), whole("mw").indirect(dW), whole("mi"), A.min, ["mw0", "mw1", uw, "mi0", "mi1"], ["o1"])
        if first:
            cube_table()
            e_first(0)
            cp(whole("npW"), sm("np"), ["np"], ["npW"])
        else:
            cp(whole("d3W"), sm("d3"), ["d3"], ["d3W"])
        tt(whole("o2"), whole("o1").indirect(dW), whole("ms"), A.min, ["o1", uw, "ms0", "ms1"], ["o2"])
        tr(whole("to2"), whole("o2"), ["o2"], ["to2"])
        cp(sl("tsend%d" % r, 0, 2), T.to2[:, 0:C:8], ["to2"], ["tsend%d.0" % r])
        cp(sl("tsend%d" % r, 2), col("to2", 4), ["to2"], ["tsend%d.1" % r])
        send(p, "t%d" % r, whole("tland%d" % r), whole("tsend%d" % r), ["tsend%d.%d" % (r, i) for i in range(2)])
        if first:
            cp(col("tbb", 13), sm("iotaT"), ["iotaT"], ["tbb"])
            for b, o in (("m56", A.is_equal), ("i56", A.not_equal)):
                ts2(sl(b, 0), si("bi"), cl("u1"), o, 1.0 / E1, A.mult, ["bi", "u1"], [b + "a"])
                ts1(sl(b, 1), si("bi"), cl("u1"), o, ["bi", "u1"], [b])
            zero(whole("fl"), ["fl0", "fl1"])
            zero(whole("tcb"), ["tcb", "tcbs", "tcbd"])
            zero(T.s480[:, 0:16], ["s480"])
            zero(T.s480[:, 16 + C:32 + C], ["s480"])
            iota(T.one[:, :], [[0, 512]], 1, ["one"])
            for b in range(4):
                op("g", lambda: g.affine_select(T.et[:, 512 * b:512 * b + 512], T.one[:, :], [[-1, 512]], A.is_equal, 0.0, b, 4), ["one"], ["et%d" % b])
        e_rest(r)
        if not first: gat("g3o", "o2", whole("d3W"), ["d3W"])
        planes(r, range(1 if first else 3))
        pw = [(sm("iotaE"), "iotaE")] + [(col(b, q), b) for b in ("to2", "tg3o") for q in (1, 5, 9)]

        def steps_a(js):
            for i in js: tt(slot("da", i // 3, i % 3), pw[i][0], pw[i + 1][0], A.subtract, [pw[i][1], pw[i + 1][1], "da"], ["da%d" % i])

        def own_rest():
            tr(whole("tg3o"), whole("g3o"), ["g3o"], ["tg3o"])
            for i in range(3): tt(sm("A%d" % (3 + i)), col("to2", 8), col("tg3o", 4 * i), A.min, ["to2", "tg3o"], ["A%d" % (3 + i)])
            steps_a(range(3, 6))
            act(slot("da", 1, 3), pw[6][0], ["tg3o", "da"], ["da6"], bias=-E0)
        steps_a(range(3))
        if first:
            for t in range(1, 4): ts1(T.xp[:, C * t:C * t + C], T.x0[:, t:4 * C:4], 0.5, A.mult, ["x0.0", "x0.1"], ["xp%d" % t])
            cp(whole("d3W"), sm("d3"), ["d3"], ["d3W"])
            gat("g3o", "o2", whole("d3W"), ["d3W"])
        tr(whole("te"), whole("e1"), keys("e1"), ["te"])
        tt(col("tbb", 1), col("te", 1), col("te", 9), A.subtract, ["te", "tbbd"], ["tbbd0"])
        tt(col("tbb", 5), col("te", 9), col("te", 5), A.subtract, ["te", "tbbd"], ["tbbd1"])
        tt(col("tbb", 9), col("te", 5), sm("iotaH"), A.subtract, ["te", "iotaH", "tbbd"], ["tbbd2"])
        dma("y", "mei", row("ei", 1), whole("iland%d" % r), ["iland%d" % r], ["ei1"])
        if not first:
            along_d(r)
            own_rest()
            cp(whole("e3W"), sm("e3"), ["e3"], ["e3W"])
        cp(T.tbb[:, 0:C:8], sl("tland%d" % r, 0, 2), ["tland%d" % r, "tbbs"], ["tbbs0"])
        cp(col("tbb", 4), sl("tland%d" % r, 2), ["tland%d" % r, "tbbs"], ["tbbs1"])
        tr(whole("sb"), whole("tbb"), ["tbb", "tbbs0", "tbbs1", "tbbd0", "tbbd1", "tbbd2"], ["sb"])
        if first: cp(whole("e3W"), sm("e3"), ["e3"], ["e3W"])
        ts1(T.g0[:, 0:16 * CUT], whole("sb").indirect(T.nW[:, 0:CUT]), cl("b1"), A.add, ["sb", "nW", "b1"], ["g0"])
        act(T.g0[:, 16 * CUT:C], whole("sb").indirect(T.nW[:, CUT:K]), ["sb", "nW", "b1"], ["g0b"], bias=cl("b1"))
        gat("g3", "sb", whole("e3W"), ["e3W", "b1"], bias=cl("b1"))
        if first:
            own_rest()
            along_d(r)
        else:
            planes(r, [3])
        mates(r)
        tr(whole("tg0"), whole("g0"), ["g0", "g0b"], ["tg0"])
        for j in range(3): tt(slot("fl", 1, 3 - j), sm("A%d" % (5 - j)), col("tg0", 4 * j), A.is_le, ["A%d" % (5 - j), "tg0", "fl1"], ["h%d" % j])
        tr(whole("tg3"), whole("g3"), ["g3"], ["tg3"])
        scan(whole("ra"), sl("fl", 4, 4), sl("da", 4, 4), ["h0", "h1", "h2", "da3", "da4", "da5", "da6"], ["ra"])
        scan(whole("rb"), sl("fl", 4, 4), T.tg0[:, 1:C:4], ["h0", "h1", "h2", "tg0"], ["rb"])
        for j in range(3): tt(sm("B%d" % (3 + j)), col("tg0", 8), col("tg3", 4 * j), A.min, ["tg0", "tg3"], ["B%d" % (3 + j)])
        for j in range(3): tt(slot("fl", 0, 3 - j), col("to2", 8 - 4 * j), sm("B%d" % (3 + j)), A.is_le, ["to2", "B%d" % (3 + j), "fl0"], ["h%d" % (3 + j)])
        cp(slot("da", 0, 3), slot("ra", 0, 3), ["ra", "da"], ["da7"])
        cp(col("tg3", 13), slot("rb", 0, 3), ["rb", "tg3"], ["tg3b"])
        scan(T.tcb[:, 0:C:4], sl("fl", 0, 4), sl("da", 0, 4), ["h3", "h4", "h5", "da0", "da1", "da2", "da7", "tcb"], ["tcbd"])
        scan(T.tcb[:, 1:C:4], sl("fl", 0, 4), T.tg3[:, 1:C:4], ["h3", "h4", "h5", "tg3", "tg3b", "tcb"], ["tcbs"])
        def in_place(i): tt(sl("v56", i), col("tcb", 12 + i), sl("m56", i), A.mult, ["tcbs", "tcbd", "m56", "m56a"], ["v56%d" % i])
        tr(T.s480[:, 16:16 + C], whole("tcb"), ["tcbs", "tcbd"], ["s480"])
        act(whole("kn"), T.s480[:, 16:16 + C].indirect(whole("npW")), ["s480", "npW"], ["kn"])
        dma("y", "mkn", sm("pbn"), row("kn", 13), ["kn"], ["pbn"])
        in_place(0)
        tr(whole("t480"), whole("s480"), ["s480"], ["t480"])
        in_place(1)
        for i in range(2): tt(sl("u56", i), T.t480[:, 28 + i:C + 16:16], sl("i56", i), A.mult, ["t480", "i56", "i56a"], ["u56%d" % i])
        for i in range(2): tt(sl("w56", i), sl("v56", i), sl("u56", i), A.add, ["v56%d" % i, "u56%d" % i], ["w56%d" % i])
        cp(whole("aW"), sl("w56", 0), ["w560"], ["aW"])
        ts1(si("bi"), sl("w56", 1), int(NZ) - 1, A.bitwise_and, ["w561"], ["bi"])
        cp(whole("bW"), si("bi"), ["bi"], ["bW"])

        def gather_a(k, t):
            lo, hi = CHZ[k]
            act(T.tmp[:, C * t + lo:C * t + hi], T.xp[:, C * t:C * t + C].indirect(T.aW[:, lo // 16:hi // 16]), ["xp%d" % t, "aW"], ["tmp%d%d" % (k, t)])

        def add_b(k, t):
            lo, hi = CHZ[k]
            tt(T.z[:, 4 * lo + t:4 * hi:4], T.xp[:, C * t:C * t + C].indirect(T.bW[:, lo // 16:hi // 16]), T.tmp[:, C * t + lo:C * t + hi], A.add,
               ["xp%d" % t, "bW", "tmp%d%d" % (k, t)], ["z%d%d" % (k, t)])

        def layer(lo, hi, bank, q, s, c0, zk, qk):
            quant(T[q][:, lo - c0:hi - c0], T[s][:, lo - c0:hi - c0], T.z[:, 4 * lo:4 * hi], ["z%d%d" % (k, t) for k in zk for t in range(4)], [qk])
            for i in range(4):
                mm(T[bank][:, 512 * i:512 * i + hi - lo], T.qw[:, 128 * i:128 * i + 128], T.sw[:, 128 * i:128 * i + 128], T[q][:, lo - c0:hi - c0], T[s][:, lo - c0:hi - c0],
                   ["qw", "sw", qk], ["P" + bank[1] + str(i)])

        def evac(k):
            lo, hi = CH[k]
            for i in range(4): act(T.hh[:, 4 * lo + i:4 * hi:4], T[("ph", "pd")[k]][:, 512 * i:512 * i + hi - lo], ["P" + "hd"[k] + str(i)], ["hh%d%d" % (k, i)], 0.03125)

        def pack(k):
            lo, hi = CH[k]
            quant(T["qh%d" % r][:, lo:hi], T["sh%d" % r][:, lo:hi], T.hh[:, 4 * lo:4 * hi], ["hh%d%d" % (k, i) for i in range(4)], ["qh%d%d" % (r, k)])
            send(p, "c%d%d" % (k, r), T["ql%d" % r][:, lo:hi].bitcast(dt.uint8), T["qh%d" % r][:, lo:hi].bitcast(dt.uint8), ["qh%d%d" % (r, k)])
            send(p, "s%d%d" % (k, r), T["sl%d" % r][:, lo:hi], T["sh%d" % r][:, lo:hi], ["qh%d%d" % (r, k)])

        def edit():
            tt(si("is"), sl("w56", 1), sm("pbn"), A.add, ["w561", "pbn"], ["is"])
            tt(whole("df"), whole("lb"), whole(ln), A.subtract, ["lb0", "lb1", "lb2", ln, ln + "m"], ["df"])
            ts2(si("odd"), si("is"), 10, A.arith_shift_right, 1, A.bitwise_and, ["is"], ["odd"])
            for i in range(3): tt(sl("pr", i), sl("df", i), si("odd"), A.mult, ["df", "odd"], ["pr%d" % i])
            tt(whole(lnn), whole(ln), whole("pr"), A.add, [ln, ln + "m", "pr0", "pr1", "pr2"], [lnn, lnn + "m"])
            cp(whole(uwn), whole(lnn), [lnn, lnn + "m"], [uwn])
            if not last: dma("y", "mq9", row("q", 9), sl(lnn, 0), [lnn], ["q9"])

        for k in range(2):
            for t in range(4): gather_a(k, t)
        for t in range(4): add_b(0, t)
        layer(*CH[0], "ph", "qz", "sz", 0, [0], "qz0")
        for t in range(4): add_b(1, t)
        layer(*CH[1], "pd", "qz", "sz", 0, [1], "qz1")
        evac(0)
        pack(0)
        edit()
        for t in range(2): gather_a(2, t)
        evac(1)
        for t in range(2, 4): gather_a(2, t)
        pack(1)
        for t in range(4): add_b(2, t)
        layer(OWN[0], OWN[1], "ph", "qo", "so", OWN[0], [1, 2], "qo")
        if not last:
            send(peer[r + 1], "l%d" % (r + 1), whole("lland%d" % (r + 1)), sl(lnn, 0), [lnn])
            send(peer[r + 1], "u%d" % (r + 1), sl("eW", 2 * r + 2, 2), sl(uwn, 0, 2), [uwn])
        for i in range(4): act(T.jp[:, C * i + F:C * i + C], T.ph[:, 512 * i + F - OWN[0]:512 * i + C - OWN[0]], ["Ph%d" % i], ["jp%dh" % i], 0.03125)
        if first: quant(whole("qe"), whole("se_"), whole("et"), ["et%d" % b for b in range(4)], ["qe"])
        if last:
            quant(T.qv[:, :], T.sv_[:, :], T.vb[:, :], ["vb"], ["qv"])
        else:
            invert(r + 1)
            inverse_table(r + 1)
            inverse_out(r + 1)
            e_row(r + 1)
        for k, (lo, hi) in enumerate(CH):
            bank = ("pd", "ph")[k]
            for b in range(4):
                mm(T[bank][:, 512 * b:512 * b + hi - lo], T.qe[:, 128 * b:128 * b + 128], T.se_[:, 128 * b:128 * b + 128], T["ql%d" % r][:, lo:hi], T["sl%d" % r][:, lo:hi],
                   ["qe", "ql%d.%d" % (r, k), "sl%d.%d" % (r, k)], ["P" + bank[1] + str(b)])
                act(T.jp[:, C * b + lo:C * b + hi], T[bank][:, 512 * b:512 * b + hi - lo], ["P" + bank[1] + str(b)], ["jp%d%d" % (b, k)])
        if last:
            gat("lrow", "q", sl(uwn, 1), [uwn])
            dma("y", "st0", T.dn[:, :], row("lrow", 5), ["lrow"], [])
        else:
            powers(r + 1)
            cube_row(r + 1)
            cube_table()
            e_first(r + 1)
        for h, (lo, hi) in enumerate(RUNS):
            for t in range(4):
                tt(T[XN][:, 4 * lo + t:4 * hi:4], T.jp[:, C * t:C * t + C].indirect(T[uwn][:, 2 * K + lo // 16:2 * K + hi // 16]), T[X][:, 4 * lo + t:4 * hi:4], A.add,
                   ["jp%d0" % t, "jp%d1" % t, "jp%dh" % t, uwn, X + ".%d" % h], [XN + "t%d%d" % (h, t)])
            lastw[XN + ".%d" % h] = [("qv", count["qv"])]
            scores(r + 1, h)
            if last:
                dma("y", "st%d" % (1 + h), T.oc[:, 4 * lo:4 * hi], T.qx[:, lo:hi].bitcast(dt.uint8), ["qx%d" % h], [])
                act(T.ysb[:, lo:hi], T.pd[:, 1024 * h:1024 * h + hi - lo], ["Pd%d" % (2 * h)], ["ysb%d" % h])
                dma("s", "st%d" % (3 + h), T.y[:, lo:hi], T.ysb[:, lo:hi], ["ysb%d" % h], [])

    for k in range(4): dma("y", "st%d" % (5 + k), T.osc[4 * k:4 * k + 4, :], T.sx[32 * k:32 * k + 4, :], ["qx0", "qx1"], [])
    for s in sorted(count): wait("g", (s, count[s]))
